import numpy as np
import ml_dtypes


def mxq(x, axis, fmt="e4m3"):
    dtype, down = {"e4m3": (ml_dtypes.float8_e4m3fn, 7), "e5m2": (ml_dtypes.float8_e5m2, 14)}[fmt]
    v = np.moveaxis(np.asarray(x, np.float32).astype(ml_dtypes.bfloat16).astype(np.float64), axis, -1)
    blocks = v.reshape(v.shape[:-1] + (-1, 32))
    amax = np.abs(blocks).max(-1, keepdims=True)
    byte = np.maximum(np.where(amax > 0, np.frexp(amax)[1] - 1 + 127, 0) - down, 1)
    scale = np.exp2(byte - 127.0)
    codes = (blocks / scale).astype(np.float32).astype(dtype).astype(np.float64)
    return np.moveaxis((codes * scale).reshape(v.shape), -1, axis)


WIDE = False


def mx_kscale(k, group=512):
    if not WIDE:
        return np.ones(k)
    levels = np.array([10, -10, 5, -5, 0])
    if group != 512:
        return np.exp2(np.random.permutation(np.resize(levels, k // group))).repeat(group)
    if k % 512:
        return np.exp2(np.random.permutation(np.resize(levels, k // 32))).repeat(32)
    a = np.empty((k // 512, 16))
    for p in range(k // 512):
        a[p, :8] = np.random.permutation(np.resize(levels, 8))
        for g in range(8):
            far = levels[np.abs(levels - a[p, g]) >= 10]
            a[p, g + 8] = far[np.random.randint(len(far))]
    return np.exp2(a.ravel()).repeat(32)


def f64(x):
    return np.asarray(x).astype(np.float64)


def striped(idx):
    return np.tile(np.asarray(idx).reshape(-1, 16).T, (8, 1)).astype(np.uint16)


def unstriped(offs):
    return offs[:16].T.reshape(-1).astype(np.int64)


H, KV, D, NQ, N = 4, 1, 256, 512, 512


def setup_inputs():
    n = np.random.standard_normal
    s = mx_kscale(D, 0)[:, None]
    u = mx_kscale(N)
    t = np.random.uniform(0.5, 2.0, N) * u
    v = n((KV, N, 128))
    return {
        "qT": (n((H, D, NQ)) * s * (0.70 / np.sqrt(D))).astype(np.float32),
        "kT": (n((KV, D, N)) / s).astype(np.float32),
        "t": t.reshape(N, 1).astype(np.float32),
        "v": (v / t[:, None]).astype(np.float32),
        "kb": (0.5 * n((N, 1))).astype(np.float32),
        "mask": np.exp2(-np.abs(np.arange(NQ)[None, :] * N / NQ - np.arange(N)[:, None]) / 256.0).astype(np.float32),
    }


def reference(qT, kT, t, v, kb, mask):
    a = np.repeat(mxq(f64(kT), 1, "e4m3"), H // KV, 0).transpose(0, 2, 1) @ mxq(f64(qT), 1, "e4m3")
    a = a + f64(kb)
    p = a
    p = p * f64(mask)
    w = p * f64(t)
    y = mxq(w, 1, "e4m3").transpose(0, 2, 1) @ np.repeat(mxq(f64(v), 1, "e4m3"), H // KV, 0)
    y = y / 16.0
    return y

@@ -1,0 +1,239 @@
+from contextlib import ExitStack
+
+import concourse.mybir as mybir
+
+H, D, NQ, N, E = 4, 256, 512, 512, 128
+FLOPS = 2 * H * N * NQ * (D + E)
+
+F32 = mybir.dt.float32
+BF16 = mybir.dt.bfloat16
+U32 = mybir.dt.uint32
+U8 = mybir.dt.uint8
+FP8X4 = mybir.dt.float8_e4m3fn_x4
+IDENT = mybir.ActivationFunctionType.Identity
+MULT = mybir.AluOpType.mult
+
+P = 128
+PACK = 4
+ROWS = D // PACK
+HALF = NQ // 2
+K_VECTOR = 88
+Q_VECTOR = 176
+
+
+def tile_rows_a_lin_kb_mask_kernel(tc, qT, kT, t, v, kb, mask, out):
+    nc = tc.nc
+    with ExitStack() as ctx:
+        sb = ctx.enter_context(tc.tile_pool(name="sb", bufs=1))
+        ps = ctx.enter_context(tc.psum_pool(name="ps", bufs=1))
+        ctx.enter_context(tc.manual_schedule())
+
+        def tile(name, shape, dtype):
+            return sb.tile(shape, dtype, name=name, align_bytes=64)
+
+        score_banks = [[ps.tile([P, 2, HALF], F32, name="score%d_%d" % (g, i)) for i in range(3)] for g in range(2)]
+        y_banks = [ps.tile([P, 2 * HALF], F32, name="y%d" % i) for i in range(2)]
+
+        k_raw = tile("k_raw", [P, PACK, N], F32)
+        q_raw = [tile("q_raw%d" % i, [P, PACK, HALF], F32) for i in range(4)]
+        mask_sb = [tile("mask%d" % i, [P, PACK, HALF], F32) for i in range(2)]
+        v_raw = tile("v_raw", [P, PACK, E], F32)
+        t_sb = tile("t_sb", [P, PACK], F32)
+        kb_sb = tile("kb_sb", [P, PACK], F32)
+        kbt = tile("kbt", [P, PACK], F32)
+
+        k_rows = kT[0].rearrange("(p j) n -> p j n", j=PACK)
+        q_rows = qT.rearrange("(a g) (p j) n -> a (g p) j n", g=2, j=PACK)
+        mask_rows = mask.rearrange("(p j) n -> p j n", j=PACK)
+
+        def load_q(i):
+            pair, half = divmod(i, 2)
+            nc.sync.dma_start(out=q_raw[i][:], in_=q_rows[pair][:, :, half * HALF : (half + 1) * HALF])
+
+        def load_mask(half):
+            nc.sync.dma_start(out=mask_sb[half][:], in_=mask_rows[:, :, half * HALF : (half + 1) * HALF])
+
+        nc.sync.dma_start(out=k_raw[0:ROWS], in_=k_rows)
+        nc.scalar.dma_start(out=k_raw[ROWS:P], in_=k_rows)
+        nc.scalar.dma_start(out=t_sb[:], in_=t.rearrange("(p j) o -> p (j o)", j=PACK))
+        nc.scalar.dma_start(out=kb_sb[:], in_=kb.rearrange("(p j) o -> p (j o)", j=PACK))
+        load_q(0)
+        load_q(1)
+        load_mask(0)
+        load_q(2)
+        load_mask(1)
+        nc.sync.dma_start(out=v_raw[:], in_=v[0].rearrange("(p j) e -> p j e", j=PACK))
+        load_q(3)
+
+        def mx_tiles(name, columns):
+            return (
+                tile(name + "_bf16", [P, columns, PACK], BF16),
+                tile(name + "_codes", [P, columns], U32),
+                tile(name + "_scales", [P, columns], U8),
+            )
+
+        def quantize(mx):
+            nc.vector.quantize_mx(
+                out=mx[1][:].bitcast(FP8X4), scales=mx[2][:], in_=mx[0][:].rearrange("p c j -> p (c j)")
+            )
+
+        def interleave(engine, mx, raw, c0, c1):
+            dst = mx[0][:, c0:c1, :].rearrange("p (c i) j -> p c j i", i=4)
+            src = raw[:, :, c0:c1].rearrange("p j (c i) -> p c j i", i=4)
+            if engine == "vector":
+                nc.vector.tensor_copy(out=dst, in_=src)
+            else:
+                nc.scalar.activation(out=dst, in_=src, func=IDENT)
+
+        k_mx = mx_tiles("k", N)
+        q_mx = [mx_tiles("q%d" % i, HALF) for i in range(4)]
+        v_mx = mx_tiles("v", E)
+
+        k_dst = k_mx[0][:].rearrange("p (a b s) j -> p a s j b", a=2, b=2)
+        k_src = k_raw[:].rearrange("p j (s a b) -> p a s j b", a=2, b=2)
+        nc.vector.tensor_copy(out=k_dst[:, :, 0:K_VECTOR], in_=k_src[:, :, 0:K_VECTOR])
+        for a in range(2):
+            nc.scalar.activation(out=k_dst[:, a, K_VECTOR:P], in_=k_src[:, a, K_VECTOR:P], func=IDENT)
+        nc.vector.tensor_tensor(out=kbt[:], in0=kb_sb[:], in1=t_sb[:], op=MULT)
+        quantize(k_mx)
+        interleave("vector", q_mx[0], q_raw[0], 0, Q_VECTOR)
+        interleave("scalar", q_mx[0], q_raw[0], Q_VECTOR, HALF)
+        quantize(q_mx[0])
+
+        scaled = [tile("scaled%d" % u, [P, PACK, HALF], F32) for u in range(8)]
+        pieces = [(u, 0, HALF) for u in range(7)] + [(7, 0, P), (7, P, P)]
+        w_mx = [mx_tiles("w%d" % n, width) for n, (u, c0, width) in enumerate(pieces)]
+        y_sb = [tile("y_sb%d" % n, [P, width // P, E], F32) for n, (u, c0, width) in enumerate(pieces)]
+
+        def scores(step):
+            i, a = divmod(step, 2)
+            for b in range(2):
+                k_cols = slice((2 * a + b) * P, (2 * a + b + 1) * P)
+                for c0 in range(0, HALF, P):
+                    for g in range(2):
+                        rows = slice(g * ROWS, (g + 1) * ROWS)
+                        nc.tensor.matmul_mx(
+                            out=score_banks[g][step % 3][:, b, c0 : c0 + P],
+                            lhsT=k_mx[1][rows, k_cols].bitcast(FP8X4),
+                            lhsT_scale=k_mx[2][rows, k_cols],
+                            rhs=q_mx[i][1][rows, c0 : c0 + P].bitcast(FP8X4),
+                            rhs_scale=q_mx[i][2][rows, c0 : c0 + P],
+                            start=True,
+                            stop=True,
+                        )
+
+        def bias_scale(u, a):
+            i, g = divmod(u, 2)
+            for b in range(2):
+                r = 2 * a + b
+                nc.scalar.activation(
+                    out=scaled[u][:, r, :],
+                    in_=score_banks[g][(2 * i + a) % 3][:, b, :],
+                    func=IDENT,
+                    scale=t_sb[:, r : r + 1],
+                    bias=kbt[:, r : r + 1],
+                )
+
+        def weigh(n):
+            u, c0, width = pieces[n]
+            cols = slice(c0, c0 + width)
+            nc.vector.tensor_tensor(
+                out=w_mx[n][0][:].rearrange("p (c i) r -> p c r i", i=2),
+                in0=scaled[u][:, :, cols].rearrange("p r (c i) -> p c r i", i=2),
+                in1=mask_sb[u // 2 % 2][:, :, cols].rearrange("p r (c i) -> p c r i", i=2),
+                op=MULT,
+            )
+
+        def values(n):
+            width = pieces[n][2]
+            for c0 in range(0, width, P):
+                nc.tensor.matmul_mx(
+                    out=y_banks[n % 2][:, c0 : c0 + P],
+                    lhsT=w_mx[n][1][:, c0 : c0 + P].bitcast(FP8X4),
+                    lhsT_scale=w_mx[n][2][:, c0 : c0 + P],
+                    rhs=v_mx[1][:].bitcast(FP8X4),
+                    rhs_scale=v_mx[2][:],
+                    start=True,
+                    stop=True,
+                )
+
+        def finish(n):
+            u, c0, width = pieces[n]
+            i, g = divmod(u, 2)
+            pair, half = divmod(i, 2)
+            nc.scalar.activation(
+                out=y_sb[n][:].rearrange("p b e -> p (b e)"), in_=y_banks[n % 2][:, 0:width], func=IDENT, scale=1.0 / 16.0
+            )
+            q0 = half * HALF + c0
+            nc.sync.dma_start(
+                out=out[2 * pair + g, q0 : q0 + width, :].rearrange("(b m) e -> m b e", m=P), in_=y_sb[n][:]
+            )
+
+        scores(0)
+        scores(1)
+        interleave("vector", q_mx[1], q_raw[1], 0, HALF)
+        quantize(q_mx[1])
+        scores(2)
+        bias_scale(0, 0)
+        bias_scale(0, 1)
+        weigh(0)
+        interleave("vector", q_mx[2], q_raw[2], 0, HALF)
+        bias_scale(1, 0)
+        scores(3)
+        bias_scale(1, 1)
+        weigh(1)
+        quantize(q_mx[2])
+        scores(4)
+        quantize(w_mx[0])
+        bias_scale(2, 0)
+        bias_scale(2, 1)
+        weigh(2)
+        bias_scale(3, 0)
+        scores(5)
+        bias_scale(3, 1)
+        interleave("scalar", v_mx, v_raw, 0, E)
+        interleave("vector", q_mx[3], q_raw[3], 0, HALF)
+        quantize(w_mx[1])
+        weigh(3)
+        quantize(q_mx[3])
+        scores(6)
+        quantize(v_mx)
+        quantize(w_mx[2])
+        values(0)
+        values(1)
+        bias_scale(4, 0)
+        bias_scale(4, 1)
+        weigh(4)
+        quantize(w_mx[3])
+        bias_scale(5, 0)
+        scores(7)
+        bias_scale(5, 1)
+        finish(0)
+        finish(1)
+        values(2)
+        values(3)
+        weigh(5)
+        quantize(w_mx[4])
+        bias_scale(6, 0)
+        bias_scale(6, 1)
+        finish(2)
+        values(4)
+        weigh(6)
+        quantize(w_mx[5])
+        bias_scale(7, 0)
+        bias_scale(7, 1)
+        finish(3)
+        values(5)
+        finish(4)
+        weigh(7)
+        quantize(w_mx[6])
+        values(6)
+        finish(5)
+        weigh(8)
+        quantize(w_mx[7])
+        values(7)
+        finish(6)
+        quantize(w_mx[8])
+        finish(7)
+        values(8)
+        finish(8)

@@ -18,7 +18,6 @@ PACK = 4
 ROWS = D // PACK
 HALF = NQ // 2
 K_VECTOR = 88
-Q_VECTOR = 176
 
 
 def tile_rows_a_lin_kb_mask_kernel(tc, qT, kT, t, v, kb, mask, out):
@@ -31,7 +30,7 @@ def tile_rows_a_lin_kb_mask_kernel(tc, qT, kT, t, v, kb, mask, out):
         def tile(name, shape, dtype):
             return sb.tile(shape, dtype, name=name, align_bytes=64)
 
-        score_banks = [[ps.tile([P, 2, HALF], F32, name="score%d_%d" % (g, i)) for i in range(3)] for g in range(2)]
+        score_banks = [[ps.tile([P, NQ], F32, name="score%d_%d" % (g, i)) for i in range(3)] for g in range(2)]
         y_banks = [ps.tile([P, 2 * HALF], F32, name="y%d" % i) for i in range(2)]
 
         k_raw = tile("k_raw", [P, PACK, N], F32)
@@ -41,6 +40,7 @@ def tile_rows_a_lin_kb_mask_kernel(tc, qT, kT, t, v, kb, mask, out):
         t_sb = tile("t_sb", [P, PACK], F32)
         kb_sb = tile("kb_sb", [P, PACK], F32)
         kbt = tile("kbt", [P, PACK], F32)
+        warm = tile("warm", [P, 2], F32)
 
         k_rows = kT[0].rearrange("(p j) n -> p j n", j=PACK)
         q_rows = qT.rearrange("(a g) (p j) n -> a (g p) j n", g=2, j=PACK)
@@ -53,16 +53,21 @@ def tile_rows_a_lin_kb_mask_kernel(tc, qT, kT, t, v, kb, mask, out):
         def load_mask(half):
             nc.sync.dma_start(out=mask_sb[half][:], in_=mask_rows[:, :, half * HALF : (half + 1) * HALF])
 
-        nc.sync.dma_start(out=k_raw[0:ROWS], in_=k_rows)
-        nc.scalar.dma_start(out=k_raw[ROWS:P], in_=k_rows)
+        row_tiles = [slice(g * ROWS, (g + 1) * ROWS) for g in range(2)]
+        queues = (nc.sync, nc.scalar)
+        for queue, rows in zip(queues, row_tiles):
+            queue.dma_start(out=q_raw[0][rows], in_=q_rows[0][rows, :, 0:HALF])
+        for queue, rows in zip(queues, row_tiles):
+            queue.dma_start(out=k_raw[rows], in_=k_rows)
         nc.scalar.dma_start(out=t_sb[:], in_=t.rearrange("(p j) o -> p (j o)", j=PACK))
         nc.scalar.dma_start(out=kb_sb[:], in_=kb.rearrange("(p j) o -> p (j o)", j=PACK))
-        load_q(0)
+        nc.gpsimd.memset(warm[:, 0:1], 0.0)
+        nc.scalar.activation(out=warm[:, 1:2], in_=warm[:, 0:1], func=IDENT)
         load_q(1)
-        load_mask(0)
         load_q(2)
-        load_mask(1)
+        load_mask(0)
         nc.sync.dma_start(out=v_raw[:], in_=v[0].rearrange("(p j) e -> p j e", j=PACK))
+        load_mask(1)
         load_q(3)
 
         def mx_tiles(name, columns):
@@ -85,70 +90,67 @@ def tile_rows_a_lin_kb_mask_kernel(tc, qT, kT, t, v, kb, mask, out):
             else:
                 nc.scalar.activation(out=dst, in_=src, func=IDENT)
 
-        k_mx = mx_tiles("k", N)
+        k_mx = [mx_tiles("k%d" % a, 2 * P) for a in range(2)]
         q_mx = [mx_tiles("q%d" % i, HALF) for i in range(4)]
         v_mx = mx_tiles("v", E)
 
-        k_dst = k_mx[0][:].rearrange("p (a b s) j -> p a s j b", a=2, b=2)
-        k_src = k_raw[:].rearrange("p j (s a b) -> p a s j b", a=2, b=2)
-        nc.vector.tensor_copy(out=k_dst[:, :, 0:K_VECTOR], in_=k_src[:, :, 0:K_VECTOR])
-        for a in range(2):
-            nc.scalar.activation(out=k_dst[:, a, K_VECTOR:P], in_=k_src[:, a, K_VECTOR:P], func=IDENT)
-        nc.vector.tensor_tensor(out=kbt[:], in0=kb_sb[:], in1=t_sb[:], op=MULT)
-        quantize(k_mx)
-        interleave("vector", q_mx[0], q_raw[0], 0, Q_VECTOR)
-        interleave("scalar", q_mx[0], q_raw[0], Q_VECTOR, HALF)
-        quantize(q_mx[0])
+        def deal_keys(a):
+            dst = k_mx[a][0][:].rearrange("p (b s) j -> p s j b", b=2)
+            src = k_raw[:].rearrange("p j (s a b) -> p a s j b", a=2, b=2)[:, a]
+            nc.vector.tensor_copy(out=dst[:, 0:K_VECTOR], in_=src[:, 0:K_VECTOR])
+            nc.scalar.activation(out=dst[:, K_VECTOR:P], in_=src[:, K_VECTOR:P], func=IDENT)
 
-        scaled = [tile("scaled%d" % u, [P, PACK, HALF], F32) for u in range(8)]
-        pieces = [(u, 0, HALF) for u in range(7)] + [(7, 0, P), (7, P, P)]
-        w_mx = [mx_tiles("w%d" % n, width) for n, (u, c0, width) in enumerate(pieces)]
-        y_sb = [tile("y_sb%d" % n, [P, width // P, E], F32) for n, (u, c0, width) in enumerate(pieces)]
+        steps = [(0, range(PACK), c0, P) for c0 in (0, P)]
+        steps = steps + [(i, range(2 * a, 2 * a + 2), 0, HALF) for i in range(1, 4) for a in range(2)]
+        pieces = [(0, g, c0, P) for c0 in (0, P) for g in range(2)]
+        pieces = pieces + [(i, g, 0, HALF) for i in range(1, 4) for g in range(2)][:-1] + [(3, 1, 0, P), (3, 1, P, P)]
+        scaled = [[tile("scaled%d_%d" % (i, g), [P, PACK, HALF], F32) for g in range(2)] for i in range(4)]
+        w_mx = [mx_tiles("w%d" % n, piece[3]) for n, piece in enumerate(pieces)]
 
         def scores(step):
-            i, a = divmod(step, 2)
-            for b in range(2):
-                k_cols = slice((2 * a + b) * P, (2 * a + b + 1) * P)
-                for c0 in range(0, HALF, P):
-                    for g in range(2):
-                        rows = slice(g * ROWS, (g + 1) * ROWS)
+            i, places, q0, width = steps[step]
+            for slot, r in enumerate(places):
+                keys = k_mx[r // 2]
+                k_cols = slice(r % 2 * P, (r % 2 + 1) * P)
+                for c0 in range(0, width, P):
+                    q_cols = slice(q0 + c0, q0 + c0 + P)
+                    for g, rows in enumerate(row_tiles):
                         nc.tensor.matmul_mx(
-                            out=score_banks[g][step % 3][:, b, c0 : c0 + P],
-                            lhsT=k_mx[1][rows, k_cols].bitcast(FP8X4),
-                            lhsT_scale=k_mx[2][rows, k_cols],
-                            rhs=q_mx[i][1][rows, c0 : c0 + P].bitcast(FP8X4),
-                            rhs_scale=q_mx[i][2][rows, c0 : c0 + P],
+                            out=score_banks[g][step % 3][:, slot * width + c0 : slot * width + c0 + P],
+                            lhsT=keys[1][rows, k_cols].bitcast(FP8X4),
+                            lhsT_scale=keys[2][rows, k_cols],
+                            rhs=q_mx[i][1][rows, q_cols].bitcast(FP8X4),
+                            rhs_scale=q_mx[i][2][rows, q_cols],
                             start=True,
                             stop=True,
                         )
 
-        def bias_scale(u, a):
-            i, g = divmod(u, 2)
-            for b in range(2):
-                r = 2 * a + b
+        def bias_scale(step, g):
+            i, places, q0, width = steps[step]
+            for slot, r in enumerate(places):
                 nc.scalar.activation(
-                    out=scaled[u][:, r, :],
-                    in_=score_banks[g][(2 * i + a) % 3][:, b, :],
+                    out=scaled[i][g][:, r, q0 : q0 + width],
+                    in_=score_banks[g][step % 3][:, slot * width : (slot + 1) * width],
                     func=IDENT,
                     scale=t_sb[:, r : r + 1],
                     bias=kbt[:, r : r + 1],
                 )
 
         def weigh(n):
-            u, c0, width = pieces[n]
+            i, g, c0, width = pieces[n]
             cols = slice(c0, c0 + width)
             nc.vector.tensor_tensor(
                 out=w_mx[n][0][:].rearrange("p (c i) r -> p c r i", i=2),
-                in0=scaled[u][:, :, cols].rearrange("p r (c i) -> p c r i", i=2),
-                in1=mask_sb[u // 2 % 2][:, :, cols].rearrange("p r (c i) -> p c r i", i=2),
+                in0=scaled[i][g][:, :, cols].rearrange("p r (c i) -> p c r i", i=2),
+                in1=mask_sb[i % 2][:, :, cols].rearrange("p r (c i) -> p c r i", i=2),
                 op=MULT,
             )
 
         def values(n):
-            width = pieces[n][2]
+            i, g, q0, width = pieces[n]
             for c0 in range(0, width, P):
                 nc.tensor.matmul_mx(
-                    out=y_banks[n % 2][:, c0 : c0 + P],
+                    out=y_banks[n % 2][:, q0 + c0 : q0 + c0 + P],
                     lhsT=w_mx[n][1][:, c0 : c0 + P].bitcast(FP8X4),
                     lhsT_scale=w_mx[n][2][:, c0 : c0 + P],
                     rhs=v_mx[1][:].bitcast(FP8X4),
@@ -157,83 +159,99 @@ def tile_rows_a_lin_kb_mask_kernel(tc, qT, kT, t, v, kb, mask, out):
                     stop=True,
                 )
 
-        def finish(n):
-            u, c0, width = pieces[n]
-            i, g = divmod(u, 2)
+        def finish(n, c0, width):
+            i, g = pieces[n][0:2]
             pair, half = divmod(i, 2)
+            y_sb = tile("y_sb%d" % n, [P, width // P, E], F32)
             nc.scalar.activation(
-                out=y_sb[n][:].rearrange("p b e -> p (b e)"), in_=y_banks[n % 2][:, 0:width], func=IDENT, scale=1.0 / 16.0
+                out=y_sb[:].rearrange("p b e -> p (b e)"),
+                in_=y_banks[n % 2][:, c0 : c0 + width],
+                func=IDENT,
+                scale=1.0 / 16.0,
             )
             q0 = half * HALF + c0
             nc.sync.dma_start(
-                out=out[2 * pair + g, q0 : q0 + width, :].rearrange("(b m) e -> m b e", m=P), in_=y_sb[n][:]
+                out=out[2 * pair + g, q0 : q0 + width, :].rearrange("(b m) e -> m b e", m=P), in_=y_sb[:]
             )
 
+        interleave("vector", q_mx[0], q_raw[0], 0, HALF)
+        quantize(q_mx[0])
+        deal_keys(0)
+        deal_keys(1)
+        quantize(k_mx[0])
+        quantize(k_mx[1])
         scores(0)
         scores(1)
+        nc.vector.tensor_tensor(out=kbt[:], in0=kb_sb[:], in1=t_sb[:], op=MULT)
         interleave("vector", q_mx[1], q_raw[1], 0, HALF)
+        interleave("vector", q_mx[2], q_raw[2], 0, HALF)
         quantize(q_mx[1])
         scores(2)
-        bias_scale(0, 0)
-        bias_scale(0, 1)
-        weigh(0)
-        interleave("vector", q_mx[2], q_raw[2], 0, HALF)
-        bias_scale(1, 0)
-        scores(3)
-        bias_scale(1, 1)
-        weigh(1)
         quantize(q_mx[2])
-        scores(4)
+        bias_scale(0, 0)
+        weigh(0)
+        bias_scale(0, 1)
+        scores(3)
+        weigh(1)
+        bias_scale(1, 0)
         quantize(w_mx[0])
-        bias_scale(2, 0)
-        bias_scale(2, 1)
         weigh(2)
-        bias_scale(3, 0)
-        scores(5)
-        bias_scale(3, 1)
-        interleave("scalar", v_mx, v_raw, 0, E)
-        interleave("vector", q_mx[3], q_raw[3], 0, HALF)
+        bias_scale(1, 1)
+        scores(4)
         quantize(w_mx[1])
+        interleave("vector", v_mx, v_raw, 0, E)
         weigh(3)
-        quantize(q_mx[3])
-        scores(6)
         quantize(v_mx)
         quantize(w_mx[2])
+        bias_scale(2, 0)
+        bias_scale(3, 0)
+        weigh(4)
+        interleave("vector", q_mx[3], q_raw[3], 0, HALF)
+        quantize(w_mx[3])
+        quantize(q_mx[3])
+        bias_scale(2, 1)
+        scores(5)
         values(0)
         values(1)
-        bias_scale(4, 0)
-        bias_scale(4, 1)
-        weigh(4)
-        quantize(w_mx[3])
-        bias_scale(5, 0)
-        scores(7)
-        bias_scale(5, 1)
-        finish(0)
-        finish(1)
         values(2)
+        bias_scale(3, 1)
+        scores(6)
         values(3)
         weigh(5)
         quantize(w_mx[4])
-        bias_scale(6, 0)
-        bias_scale(6, 1)
-        finish(2)
-        values(4)
+        bias_scale(4, 0)
+        bias_scale(5, 0)
         weigh(6)
         quantize(w_mx[5])
-        bias_scale(7, 0)
-        bias_scale(7, 1)
-        finish(3)
+        bias_scale(4, 1)
+        scores(7)
+        bias_scale(5, 1)
+        finish(0, 0, HALF)
+        finish(1, 0, HALF)
+        values(4)
         values(5)
-        finish(4)
         weigh(7)
         quantize(w_mx[6])
+        bias_scale(6, 0)
+        bias_scale(7, 0)
+        finish(4, 0, HALF)
         values(6)
-        finish(5)
         weigh(8)
         quantize(w_mx[7])
+        bias_scale(6, 1)
+        bias_scale(7, 1)
+        finish(5, 0, HALF)
         values(7)
-        finish(6)
+        finish(6, 0, HALF)
+        weigh(9)
         quantize(w_mx[8])
-        finish(7)
         values(8)
-        finish(8)
+        finish(7, 0, HALF)
+        weigh(10)
+        quantize(w_mx[9])
+        values(9)
+        finish(8, 0, HALF)
+        quantize(w_mx[10])
+        values(10)
+        finish(9, 0, P)
+        finish(10, P, P)

@@ -9,6 +9,7 @@ F32 = mybir.dt.float32
 BF16 = mybir.dt.bfloat16
 U32 = mybir.dt.uint32
 U8 = mybir.dt.uint8
+I32 = mybir.dt.int32
 FP8X4 = mybir.dt.float8_e4m3fn_x4
 IDENT = mybir.ActivationFunctionType.Identity
 MULT = mybir.AluOpType.mult
@@ -18,6 +19,7 @@ PACK = 4
 ROWS = D // PACK
 HALF = NQ // 2
 K_VECTOR = 88
+Q_VECTOR = 176
 
 
 def tile_rows_a_lin_kb_mask_kernel(tc, qT, kT, t, v, kb, mask, out):
@@ -33,9 +35,10 @@ def tile_rows_a_lin_kb_mask_kernel(tc, qT, kT, t, v, kb, mask, out):
         score_banks = [[ps.tile([P, NQ], F32, name="score%d_%d" % (g, i)) for i in range(3)] for g in range(2)]
         y_banks = [ps.tile([P, 2 * HALF], F32, name="y%d" % i) for i in range(2)]
 
-        k_raw = tile("k_raw", [P, PACK, N], F32)
-        q_raw = [tile("q_raw%d" % i, [P, PACK, HALF], F32) for i in range(4)]
-        mask_sb = [tile("mask%d" % i, [P, PACK, HALF], F32) for i in range(2)]
+        k_raw = tile("k_raw", [ROWS, PACK, N], F32)
+        q_pair = [tile("q_raw%d" % pair, [P, PACK, NQ], F32) for pair in range(2)]
+        q_raw = [q_pair[i // 2][:, :, i % 2 * HALF : (i % 2 + 1) * HALF] for i in range(4)]
+        mask_sb = tile("mask_sb", [P, PACK, NQ], F32)
         v_raw = tile("v_raw", [P, PACK, E], F32)
         t_sb = tile("t_sb", [P, PACK], F32)
         kb_sb = tile("kb_sb", [P, PACK], F32)
@@ -46,29 +49,22 @@ def tile_rows_a_lin_kb_mask_kernel(tc, qT, kT, t, v, kb, mask, out):
         q_rows = qT.rearrange("(a g) (p j) n -> a (g p) j n", g=2, j=PACK)
         mask_rows = mask.rearrange("(p j) n -> p j n", j=PACK)
 
-        def load_q(i):
-            pair, half = divmod(i, 2)
-            nc.sync.dma_start(out=q_raw[i][:], in_=q_rows[pair][:, :, half * HALF : (half + 1) * HALF])
-
-        def load_mask(half):
-            nc.sync.dma_start(out=mask_sb[half][:], in_=mask_rows[:, :, half * HALF : (half + 1) * HALF])
-
         row_tiles = [slice(g * ROWS, (g + 1) * ROWS) for g in range(2)]
-        queues = (nc.sync, nc.scalar)
-        for queue, rows in zip(queues, row_tiles):
-            queue.dma_start(out=q_raw[0][rows], in_=q_rows[0][rows, :, 0:HALF])
-        for queue, rows in zip(queues, row_tiles):
-            queue.dma_start(out=k_raw[rows], in_=k_rows)
+        k_words = tile("k_words", [P, N + N // PACK], I32)
+        k_codes = k_words[:, 0:N]
+        k_scales = k_words[:, N : N + N // PACK].bitcast(U8)
+        k_bf16 = tile("k_bf16", [ROWS, N, PACK], BF16)
+
+        nc.sync.dma_start(out=k_raw[:], in_=k_rows)
         nc.scalar.dma_start(out=t_sb[:], in_=t.rearrange("(p j) o -> p (j o)", j=PACK))
         nc.scalar.dma_start(out=kb_sb[:], in_=kb.rearrange("(p j) o -> p (j o)", j=PACK))
+        nc.sync.dma_start(out=q_pair[0][:], in_=q_rows[0])
+        nc.sync.dma_start(out=v_raw[:], in_=v[0].rearrange("(p j) e -> p j e", j=PACK))
+        nc.sync.dma_start(out=mask_sb[:], in_=mask_rows)
+        nc.sync.dma_start(out=q_pair[1][:], in_=q_rows[1])
+        nc.vector.memset(k_words[0:ROWS, N : N + N // PACK], 0)
         nc.gpsimd.memset(warm[:, 0:1], 0.0)
         nc.scalar.activation(out=warm[:, 1:2], in_=warm[:, 0:1], func=IDENT)
-        load_q(1)
-        load_q(2)
-        load_mask(0)
-        nc.sync.dma_start(out=v_raw[:], in_=v[0].rearrange("(p j) e -> p j e", j=PACK))
-        load_mask(1)
-        load_q(3)
 
         def mx_tiles(name, columns):
             return (
@@ -90,35 +86,39 @@ def tile_rows_a_lin_kb_mask_kernel(tc, qT, kT, t, v, kb, mask, out):
             else:
                 nc.scalar.activation(out=dst, in_=src, func=IDENT)
 
-        k_mx = [mx_tiles("k%d" % a, 2 * P) for a in range(2)]
         q_mx = [mx_tiles("q%d" % i, HALF) for i in range(4)]
         v_mx = mx_tiles("v", E)
 
-        def deal_keys(a):
-            dst = k_mx[a][0][:].rearrange("p (b s) j -> p s j b", b=2)
-            src = k_raw[:].rearrange("p j (s a b) -> p a s j b", a=2, b=2)[:, a]
-            nc.vector.tensor_copy(out=dst[:, 0:K_VECTOR], in_=src[:, 0:K_VECTOR])
-            nc.scalar.activation(out=dst[:, K_VECTOR:P], in_=src[:, K_VECTOR:P], func=IDENT)
+        def keys():
+            dst = k_bf16[:].rearrange("p (a b s) j -> p a s j b", a=2, b=2)
+            src = k_raw[:].rearrange("p j (s a b) -> p a s j b", a=2, b=2)
+            nc.vector.tensor_copy(out=dst[:, :, 0:K_VECTOR], in_=src[:, :, 0:K_VECTOR])
+            for a in range(2):
+                nc.scalar.activation(out=dst[:, a, K_VECTOR:P], in_=src[:, a, K_VECTOR:P], func=IDENT)
+            nc.vector.quantize_mx(
+                out=k_codes[0:ROWS].bitcast(FP8X4), scales=k_scales[0:ROWS], in_=k_bf16[:].rearrange("p c j -> p (c j)")
+            )
+            nc.scalar.dma_start(out=k_words[ROWS:P], in_=k_words[0:ROWS])
 
         steps = [(0, range(PACK), c0, P) for c0 in (0, P)]
         steps = steps + [(i, range(2 * a, 2 * a + 2), 0, HALF) for i in range(1, 4) for a in range(2)]
-        pieces = [(0, g, c0, P) for c0 in (0, P) for g in range(2)]
+        pieces = [(0, g, c0, P) for g in range(2) for c0 in (0, P)]
         pieces = pieces + [(i, g, 0, HALF) for i in range(1, 4) for g in range(2)][:-1] + [(3, 1, 0, P), (3, 1, P, P)]
         scaled = [[tile("scaled%d_%d" % (i, g), [P, PACK, HALF], F32) for g in range(2)] for i in range(4)]
         w_mx = [mx_tiles("w%d" % n, piece[3]) for n, piece in enumerate(pieces)]
 
-        def scores(step):
+        def scores(step, tiles=(0, 1)):
             i, places, q0, width = steps[step]
             for slot, r in enumerate(places):
-                keys = k_mx[r // 2]
-                k_cols = slice(r % 2 * P, (r % 2 + 1) * P)
+                k_cols = slice(r * P, (r + 1) * P)
                 for c0 in range(0, width, P):
                     q_cols = slice(q0 + c0, q0 + c0 + P)
-                    for g, rows in enumerate(row_tiles):
+                    for g in tiles:
+                        rows = row_tiles[g]
                         nc.tensor.matmul_mx(
                             out=score_banks[g][step % 3][:, slot * width + c0 : slot * width + c0 + P],
-                            lhsT=keys[1][rows, k_cols].bitcast(FP8X4),
-                            lhsT_scale=keys[2][rows, k_cols],
+                            lhsT=k_codes[rows, k_cols].bitcast(FP8X4),
+                            lhsT_scale=k_scales[rows, k_cols],
                             rhs=q_mx[i][1][rows, q_cols].bitcast(FP8X4),
                             rhs_scale=q_mx[i][2][rows, q_cols],
                             start=True,
@@ -142,15 +142,18 @@ def tile_rows_a_lin_kb_mask_kernel(tc, qT, kT, t, v, kb, mask, out):
             nc.vector.tensor_tensor(
                 out=w_mx[n][0][:].rearrange("p (c i) r -> p c r i", i=2),
                 in0=scaled[i][g][:, :, cols].rearrange("p r (c i) -> p c r i", i=2),
-                in1=mask_sb[i % 2][:, :, cols].rearrange("p r (c i) -> p c r i", i=2),
+                in1=mask_sb[:, :, i % 2 * HALF + c0 : i % 2 * HALF + c0 + width].rearrange("p r (c i) -> p c r i", i=2),
                 op=MULT,
             )
+
+        def y_bank(n):
+            return y_banks[pieces[n][1] if n + 1 < len(pieces) else 0]
 
         def values(n):
             i, g, q0, width = pieces[n]
             for c0 in range(0, width, P):
                 nc.tensor.matmul_mx(
-                    out=y_banks[n % 2][:, q0 + c0 : q0 + c0 + P],
+                    out=y_bank(n)[:, q0 + c0 : q0 + c0 + P],
                     lhsT=w_mx[n][1][:, c0 : c0 + P].bitcast(FP8X4),
                     lhsT_scale=w_mx[n][2][:, c0 : c0 + P],
                     rhs=v_mx[1][:].bitcast(FP8X4),
@@ -165,7 +168,7 @@ def tile_rows_a_lin_kb_mask_kernel(tc, qT, kT, t, v, kb, mask, out):
             y_sb = tile("y_sb%d" % n, [P, width // P, E], F32)
             nc.scalar.activation(
                 out=y_sb[:].rearrange("p b e -> p (b e)"),
-                in_=y_banks[n % 2][:, c0 : c0 + width],
+                in_=y_bank(n)[:, c0 : c0 + width],
                 func=IDENT,
                 scale=1.0 / 16.0,
             )
@@ -174,34 +177,34 @@ def tile_rows_a_lin_kb_mask_kernel(tc, qT, kT, t, v, kb, mask, out):
                 out=out[2 * pair + g, q0 : q0 + width, :].rearrange("(b m) e -> m b e", m=P), in_=y_sb[:]
             )
 
-        interleave("vector", q_mx[0], q_raw[0], 0, HALF)
-        quantize(q_mx[0])
-        deal_keys(0)
-        deal_keys(1)
-        quantize(k_mx[0])
-        quantize(k_mx[1])
-        scores(0)
-        scores(1)
+        keys()
+        interleave("vector", q_mx[0], q_raw[0], 0, Q_VECTOR)
+        interleave("scalar", q_mx[0], q_raw[0], Q_VECTOR, HALF)
         nc.vector.tensor_tensor(out=kbt[:], in0=kb_sb[:], in1=t_sb[:], op=MULT)
+        quantize(q_mx[0])
+        scores(0, (0,))
+        scores(1, (0,))
+        scores(0, (1,))
+        scores(1, (1,))
+        interleave("scalar", v_mx, v_raw, 0, E)
         interleave("vector", q_mx[1], q_raw[1], 0, HALF)
-        interleave("vector", q_mx[2], q_raw[2], 0, HALF)
         quantize(q_mx[1])
+        quantize(v_mx)
         scores(2)
-        quantize(q_mx[2])
         bias_scale(0, 0)
         weigh(0)
+        bias_scale(1, 0)
+        weigh(1)
         bias_scale(0, 1)
         scores(3)
-        weigh(1)
-        bias_scale(1, 0)
         quantize(w_mx[0])
         weigh(2)
         bias_scale(1, 1)
-        scores(4)
+        interleave("vector", q_mx[2], q_raw[2], 0, HALF)
         quantize(w_mx[1])
-        interleave("vector", v_mx, v_raw, 0, E)
+        quantize(q_mx[2])
+        scores(4)
         weigh(3)
-        quantize(v_mx)
         quantize(w_mx[2])
         bias_scale(2, 0)
         bias_scale(3, 0)
@@ -227,7 +230,7 @@ def tile_rows_a_lin_kb_mask_kernel(tc, qT, kT, t, v, kb, mask, out):
         scores(7)
         bias_scale(5, 1)
         finish(0, 0, HALF)
-        finish(1, 0, HALF)
+        finish(2, 0, HALF)
         values(4)
         values(5)
         weigh(7)

@@ -19,7 +19,6 @@ PACK = 4
 ROWS = D // PACK
 HALF = NQ // 2
 K_VECTOR = 88
-Q_VECTOR = 176
 
 
 def tile_rows_a_lin_kb_mask_kernel(tc, qT, kT, t, v, kb, mask, out):
@@ -61,7 +60,6 @@ def tile_rows_a_lin_kb_mask_kernel(tc, qT, kT, t, v, kb, mask, out):
         nc.sync.dma_start(out=q_pair[0][:], in_=q_rows[0])
         nc.sync.dma_start(out=v_raw[:], in_=v[0].rearrange("(p j) e -> p j e", j=PACK))
         nc.sync.dma_start(out=mask_sb[:], in_=mask_rows)
-        nc.sync.dma_start(out=q_pair[1][:], in_=q_rows[1])
         nc.vector.memset(k_words[0:ROWS, N : N + N // PACK], 0)
         nc.gpsimd.memset(warm[:, 0:1], 0.0)
         nc.scalar.activation(out=warm[:, 1:2], in_=warm[:, 0:1], func=IDENT)
@@ -73,9 +71,11 @@ def tile_rows_a_lin_kb_mask_kernel(tc, qT, kT, t, v, kb, mask, out):
                 tile(name + "_scales", [P, columns], U8),
             )
 
-        def quantize(mx):
+        def quantize(mx, cols=slice(None)):
             nc.vector.quantize_mx(
-                out=mx[1][:].bitcast(FP8X4), scales=mx[2][:], in_=mx[0][:].rearrange("p c j -> p (c j)")
+                out=mx[1][:, cols].bitcast(FP8X4),
+                scales=mx[2][:, cols],
+                in_=mx[0][:, cols, :].rearrange("p c j -> p (c j)"),
             )
 
         def interleave(engine, mx, raw, c0, c1):
@@ -98,35 +98,36 @@ def tile_rows_a_lin_kb_mask_kernel(tc, qT, kT, t, v, kb, mask, out):
             nc.vector.quantize_mx(
                 out=k_codes[0:ROWS].bitcast(FP8X4), scales=k_scales[0:ROWS], in_=k_bf16[:].rearrange("p c j -> p (c j)")
             )
-            nc.scalar.dma_start(out=k_words[ROWS:P], in_=k_words[0:ROWS])
+            nc.sync.dma_start(out=k_words[ROWS:P], in_=k_words[0:ROWS])
+            nc.sync.dma_start(out=q_pair[1][:], in_=q_rows[1])
 
-        steps = [(0, range(PACK), c0, P) for c0 in (0, P)]
-        steps = steps + [(i, range(2 * a, 2 * a + 2), 0, HALF) for i in range(1, 4) for a in range(2)]
-        pieces = [(0, g, c0, P) for g in range(2) for c0 in (0, P)]
-        pieces = pieces + [(i, g, 0, HALF) for i in range(1, 4) for g in range(2)][:-1] + [(3, 1, 0, P), (3, 1, P, P)]
+        wide_steps = [(i, range(2 * a, 2 * a + 2), 0, HALF) for i in range(4) for a in range(2)]
+        steps = [[(0, range(PACK), c0, P) for c0 in (0, P)] + wide_steps[2:], wide_steps]
+        pieces = [(0, 0, 0, P), (0, 0, P, P), (1, 0, 0, HALF), (0, 1, 0, HALF), (1, 1, 0, HALF)]
+        pieces = pieces + [(2, 0, 0, HALF), (2, 1, 0, HALF), (3, 0, 0, HALF), (3, 1, 0, P), (3, 1, P, P)]
         scaled = [[tile("scaled%d_%d" % (i, g), [P, PACK, HALF], F32) for g in range(2)] for i in range(4)]
         w_mx = [mx_tiles("w%d" % n, piece[3]) for n, piece in enumerate(pieces)]
 
-        def scores(step, tiles=(0, 1)):
-            i, places, q0, width = steps[step]
-            for slot, r in enumerate(places):
-                k_cols = slice(r * P, (r + 1) * P)
-                for c0 in range(0, width, P):
+        def scores(step, tiles):
+            for block in range(PACK):
+                for g in tiles:
+                    i, places, q0, width = steps[g][step]
+                    slot, c0 = divmod(block * P, width)
+                    rows = row_tiles[g]
+                    k_cols = slice(places[slot] * P, (places[slot] + 1) * P)
                     q_cols = slice(q0 + c0, q0 + c0 + P)
-                    for g in tiles:
-                        rows = row_tiles[g]
-                        nc.tensor.matmul_mx(
-                            out=score_banks[g][step % 3][:, slot * width + c0 : slot * width + c0 + P],
-                            lhsT=k_codes[rows, k_cols].bitcast(FP8X4),
-                            lhsT_scale=k_scales[rows, k_cols],
-                            rhs=q_mx[i][1][rows, q_cols].bitcast(FP8X4),
-                            rhs_scale=q_mx[i][2][rows, q_cols],
-                            start=True,
-                            stop=True,
-                        )
+                    nc.tensor.matmul_mx(
+                        out=score_banks[g][step % 3][:, block * P : (block + 1) * P],
+                        lhsT=k_codes[rows, k_cols].bitcast(FP8X4),
+                        lhsT_scale=k_scales[rows, k_cols],
+                        rhs=q_mx[i][1][rows, q_cols].bitcast(FP8X4),
+                        rhs_scale=q_mx[i][2][rows, q_cols],
+                        start=True,
+                        stop=True,
+                    )
 
         def bias_scale(step, g):
-            i, places, q0, width = steps[step]
+            i, places, q0, width = steps[g][step]
             for slot, r in enumerate(places):
                 nc.scalar.activation(
                     out=scaled[i][g][:, r, q0 : q0 + width],
@@ -147,7 +148,7 @@ def tile_rows_a_lin_kb_mask_kernel(tc, qT, kT, t, v, kb, mask, out):
             )
 
         def y_bank(n):
-            return y_banks[pieces[n][1] if n + 1 < len(pieces) else 0]
+            return y_banks[max(n - 1, 0) % 2]
 
         def values(n):
             i, g, q0, width = pieces[n]
@@ -178,83 +179,85 @@ def tile_rows_a_lin_kb_mask_kernel(tc, qT, kT, t, v, kb, mask, out):
             )
 
         keys()
-        interleave("vector", q_mx[0], q_raw[0], 0, Q_VECTOR)
-        interleave("scalar", q_mx[0], q_raw[0], Q_VECTOR, HALF)
+        interleave("vector", q_mx[0], q_raw[0], 0, P)
+        interleave("scalar", q_mx[0], q_raw[0], P, HALF)
         nc.vector.tensor_tensor(out=kbt[:], in0=kb_sb[:], in1=t_sb[:], op=MULT)
-        quantize(q_mx[0])
+        quantize(q_mx[0], slice(0, P))
         scores(0, (0,))
-        scores(1, (0,))
-        scores(0, (1,))
-        scores(1, (1,))
         interleave("scalar", v_mx, v_raw, 0, E)
         interleave("vector", q_mx[1], q_raw[1], 0, HALF)
+        quantize(q_mx[0], slice(P, HALF))
+        scores(1, (0,))
         quantize(q_mx[1])
         quantize(v_mx)
-        scores(2)
+        scores(2, (0,))
         bias_scale(0, 0)
+        scores(3, (0,))
+        scores(0, (1,))
+        scores(1, (1,))
+        scores(2, (1,))
         weigh(0)
         bias_scale(1, 0)
         weigh(1)
-        bias_scale(0, 1)
-        scores(3)
         quantize(w_mx[0])
-        weigh(2)
-        bias_scale(1, 1)
-        interleave("vector", q_mx[2], q_raw[2], 0, HALF)
-        quantize(w_mx[1])
-        quantize(q_mx[2])
-        scores(4)
-        weigh(3)
-        quantize(w_mx[2])
         bias_scale(2, 0)
         bias_scale(3, 0)
-        weigh(4)
-        interleave("vector", q_mx[3], q_raw[3], 0, HALF)
-        quantize(w_mx[3])
-        quantize(q_mx[3])
-        bias_scale(2, 1)
-        scores(5)
+        weigh(2)
+        quantize(w_mx[1])
+        bias_scale(0, 1)
+        scores(3, (1,))
         values(0)
         values(1)
+        bias_scale(1, 1)
+        interleave("scalar", q_mx[2], q_raw[2], P, HALF)
+        interleave("vector", q_mx[2], q_raw[2], 0, P)
+        quantize(w_mx[2])
+        quantize(q_mx[2])
+        scores(4, (0, 1))
         values(2)
+        weigh(3)
+        bias_scale(2, 1)
+        scores(5, (0, 1))
         bias_scale(3, 1)
-        scores(6)
+        interleave("scalar", q_mx[3], q_raw[3], P, HALF)
+        interleave("vector", q_mx[3], q_raw[3], 0, P)
+        weigh(4)
+        quantize(q_mx[3])
+        scores(6, (0, 1))
+        quantize(w_mx[3])
+        bias_scale(4, 0)
+        bias_scale(5, 0)
+        finish(0, 0, HALF)
         values(3)
         weigh(5)
         quantize(w_mx[4])
-        bias_scale(4, 0)
-        bias_scale(5, 0)
-        weigh(6)
-        quantize(w_mx[5])
         bias_scale(4, 1)
-        scores(7)
+        scores(7, (0, 1))
         bias_scale(5, 1)
-        finish(0, 0, HALF)
         finish(2, 0, HALF)
         values(4)
+        finish(3, 0, HALF)
+        weigh(6)
+        quantize(w_mx[5])
         values(5)
-        weigh(7)
-        quantize(w_mx[6])
         bias_scale(6, 0)
         bias_scale(7, 0)
         finish(4, 0, HALF)
+        weigh(7)
+        quantize(w_mx[6])
         values(6)
-        weigh(8)
-        quantize(w_mx[7])
         bias_scale(6, 1)
         bias_scale(7, 1)
         finish(5, 0, HALF)
-        values(7)
         finish(6, 0, HALF)
+        weigh(8)
+        quantize(w_mx[7])
+        values(7)
         weigh(9)
+        finish(7, 0, HALF)
         quantize(w_mx[8])
         values(8)
-        finish(7, 0, HALF)
-        weigh(10)
         quantize(w_mx[9])
         values(9)
-        finish(8, 0, HALF)
-        quantize(w_mx[10])
-        values(10)
-        finish(9, 0, P)
-        finish(10, P, P)
+        finish(8, 0, P)
+        finish(9, P, P)

@@ -13,12 +13,14 @@ I32 = mybir.dt.int32
 FP8X4 = mybir.dt.float8_e4m3fn_x4
 IDENT = mybir.ActivationFunctionType.Identity
 MULT = mybir.AluOpType.mult
+ADD = mybir.AluOpType.add
 
 P = 128
 PACK = 4
 ROWS = D // PACK
-HALF = NQ // 2
-K_VECTOR = 88
+BANK = 512
+WALK = 2
+PARTS = ((0, 256), (256, 256))
 
 
 def tile_rows_a_lin_kb_mask_kernel(tc, qT, kT, t, v, kb, mask, out):
@@ -31,38 +33,26 @@ def tile_rows_a_lin_kb_mask_kernel(tc, qT, kT, t, v, kb, mask, out):
         def tile(name, shape, dtype):
             return sb.tile(shape, dtype, name=name, align_bytes=64)
 
-        score_banks = [[ps.tile([P, NQ], F32, name="score%d_%d" % (g, i)) for i in range(3)] for g in range(2)]
-        y_banks = [ps.tile([P, 2 * HALF], F32, name="y%d" % i) for i in range(2)]
+        score_banks = [[ps.tile([P, BANK], F32, name="score%d_%d" % (g, i)) for i in range(3)] for g in range(2)]
+        y_banks = [ps.tile([P, BANK], F32, name="y%d" % i) for i in range(2)]
 
-        k_raw = tile("k_raw", [ROWS, PACK, N], F32)
-        q_pair = [tile("q_raw%d" % pair, [P, PACK, NQ], F32) for pair in range(2)]
-        q_raw = [q_pair[i // 2][:, :, i % 2 * HALF : (i % 2 + 1) * HALF] for i in range(4)]
-        mask_sb = tile("mask_sb", [P, PACK, NQ], F32)
+        k_rows = kT[0].rearrange("(p j) n -> p j n", j=PACK)
+        q_rows = qT.rearrange("(a g) (p j) n -> a (g p) j n", g=2, j=PACK)
+        mask_rows = mask.rearrange("(p j) n -> p j n", j=PACK)
+        row_tiles = [slice(g * ROWS, (g + 1) * ROWS) for g in range(2)]
+
+        k_raw = [tile("k_raw%d" % i, [ROWS, PACK, N // 2], F32) for i in range(2)]
+        q_raw = [[tile("q_raw%d_%d" % (a, i), [P, PACK, w], F32) for i, (c0, w) in enumerate(PARTS)] for a in range(2)]
+        mask_sb = [tile("mask%d" % i, [P, PACK, w], F32) for i, (c0, w) in enumerate(PARTS)]
         v_raw = tile("v_raw", [P, PACK, E], F32)
         t_sb = tile("t_sb", [P, PACK], F32)
         kb_sb = tile("kb_sb", [P, PACK], F32)
         kbt = tile("kbt", [P, PACK], F32)
         warm = tile("warm", [P, 2], F32)
-
-        k_rows = kT[0].rearrange("(p j) n -> p j n", j=PACK)
-        q_rows = qT.rearrange("(a g) (p j) n -> a (g p) j n", g=2, j=PACK)
-        mask_rows = mask.rearrange("(p j) n -> p j n", j=PACK)
-
-        row_tiles = [slice(g * ROWS, (g + 1) * ROWS) for g in range(2)]
         k_words = tile("k_words", [P, N + N // PACK], I32)
         k_codes = k_words[:, 0:N]
         k_scales = k_words[:, N : N + N // PACK].bitcast(U8)
         k_bf16 = tile("k_bf16", [ROWS, N, PACK], BF16)
-
-        nc.sync.dma_start(out=k_raw[:], in_=k_rows)
-        nc.scalar.dma_start(out=t_sb[:], in_=t.rearrange("(p j) o -> p (j o)", j=PACK))
-        nc.scalar.dma_start(out=kb_sb[:], in_=kb.rearrange("(p j) o -> p (j o)", j=PACK))
-        nc.sync.dma_start(out=q_pair[0][:], in_=q_rows[0])
-        nc.sync.dma_start(out=v_raw[:], in_=v[0].rearrange("(p j) e -> p j e", j=PACK))
-        nc.sync.dma_start(out=mask_sb[:], in_=mask_rows)
-        nc.vector.memset(k_words[0:ROWS, N : N + N // PACK], 0)
-        nc.gpsimd.memset(warm[:, 0:1], 0.0)
-        nc.scalar.activation(out=warm[:, 1:2], in_=warm[:, 0:1], func=IDENT)
 
         def mx_tiles(name, columns):
             return (
@@ -71,193 +61,242 @@ def tile_rows_a_lin_kb_mask_kernel(tc, qT, kT, t, v, kb, mask, out):
                 tile(name + "_scales", [P, columns], U8),
             )
 
-        def quantize(mx, cols=slice(None)):
+        q_mx = [[mx_tiles("q%d_%d" % (a, i), w) for i, (c0, w) in enumerate(PARTS)] for a in range(2)]
+        v_mx = mx_tiles("v", E)
+        scaled = [[tile("scaled%d_%d" % (h, i), [P, PACK, w], F32) for i, (c0, w) in enumerate(PARTS)] for h in range(H)]
+        w_mx = [[mx_tiles("w%d_%d" % (h, i), w) for i, (c0, w) in enumerate(PARTS)] for h in range(H)]
+
+        def load_k(i):
+            nc.sync.dma_start(out=k_raw[i][:], in_=k_rows[:, :, i * N // 2 : (i + 1) * N // 2])
+
+        def load_q(a, i):
+            c0, w = PARTS[i]
+            nc.sync.dma_start(out=q_raw[a][i][:], in_=q_rows[a][:, :, c0 : c0 + w])
+
+        def load_mask(i):
+            c0, w = PARTS[i]
+            nc.sync.dma_start(out=mask_sb[i][:], in_=mask_rows[:, :, c0 : c0 + w])
+
+        def load_v():
+            nc.sync.dma_start(out=v_raw[:], in_=v[0].rearrange("(p j) e -> p j e", j=PACK))
+
+        def copy_k():
+            nc.sync.dma_start(out=k_words[ROWS:P], in_=k_words[0:ROWS])
+
+        def cast(engine, dst, src):
+            if engine == "vector":
+                nc.vector.tensor_copy(out=dst, in_=src)
+            else:
+                nc.scalar.copy(out=dst, in_=src)
+
+        def cast_k(engine, i, s0, s1):
+            half = N // 2 // PACK
+            dst = k_bf16[:].rearrange("p (a b s) j -> p a s j b", a=2, b=2)[:, :, i * half + s0 : i * half + s1]
+            src = k_raw[i][:].rearrange("p j (s a b) -> p a s j b", a=2, b=2)[:, :, s0:s1]
+            cast(engine, dst, src)
+
+        def quantize_k(c0, c1):
             nc.vector.quantize_mx(
-                out=mx[1][:, cols].bitcast(FP8X4),
-                scales=mx[2][:, cols],
-                in_=mx[0][:, cols, :].rearrange("p c j -> p (c j)"),
+                out=k_codes[0:ROWS, c0:c1].bitcast(FP8X4),
+                scales=k_scales[0:ROWS, c0:c1],
+                in_=k_bf16[:, c0:c1, :].rearrange("p c j -> p (c j)"),
             )
 
         def interleave(engine, mx, raw, c0, c1):
             dst = mx[0][:, c0:c1, :].rearrange("p (c i) j -> p c j i", i=4)
             src = raw[:, :, c0:c1].rearrange("p j (c i) -> p c j i", i=4)
-            if engine == "vector":
-                nc.vector.tensor_copy(out=dst, in_=src)
-            else:
-                nc.scalar.activation(out=dst, in_=src, func=IDENT)
+            cast(engine, dst, src)
 
-        q_mx = [mx_tiles("q%d" % i, HALF) for i in range(4)]
-        v_mx = mx_tiles("v", E)
-
-        def keys():
-            dst = k_bf16[:].rearrange("p (a b s) j -> p a s j b", a=2, b=2)
-            src = k_raw[:].rearrange("p j (s a b) -> p a s j b", a=2, b=2)
-            nc.vector.tensor_copy(out=dst[:, :, 0:K_VECTOR], in_=src[:, :, 0:K_VECTOR])
-            for a in range(2):
-                nc.scalar.activation(out=dst[:, a, K_VECTOR:P], in_=src[:, a, K_VECTOR:P], func=IDENT)
+        def quantize(mx, c0, c1):
             nc.vector.quantize_mx(
-                out=k_codes[0:ROWS].bitcast(FP8X4), scales=k_scales[0:ROWS], in_=k_bf16[:].rearrange("p c j -> p (c j)")
+                out=mx[1][:, c0:c1].bitcast(FP8X4),
+                scales=mx[2][:, c0:c1],
+                in_=mx[0][:, c0:c1, :].rearrange("p c j -> p (c j)"),
             )
-            nc.sync.dma_start(out=k_words[ROWS:P], in_=k_words[0:ROWS])
-            nc.sync.dma_start(out=q_pair[1][:], in_=q_rows[1])
 
-        wide_steps = [(i, range(2 * a, 2 * a + 2), 0, HALF) for i in range(4) for a in range(2)]
-        steps = [[(0, range(PACK), c0, P) for c0 in (0, P)] + wide_steps[2:], wide_steps]
-        pieces = [(0, 0, 0, P), (0, 0, P, P), (1, 0, 0, HALF), (0, 1, 0, HALF), (1, 1, 0, HALF)]
-        pieces = pieces + [(2, 0, 0, HALF), (2, 1, 0, HALF), (3, 0, 0, HALF), (3, 1, 0, P), (3, 1, P, P)]
-        scaled = [[tile("scaled%d_%d" % (i, g), [P, PACK, HALF], F32) for g in range(2)] for i in range(4)]
-        w_mx = [mx_tiles("w%d" % n, piece[3]) for n, piece in enumerate(pieces)]
+        fills = [[], []]
 
-        def scores(step, tiles):
-            for block in range(PACK):
-                for g in tiles:
-                    i, places, q0, width = steps[g][step]
-                    slot, c0 = divmod(block * P, width)
-                    rows = row_tiles[g]
-                    k_cols = slice(places[slot] * P, (places[slot] + 1) * P)
-                    q_cols = slice(q0 + c0, q0 + c0 + P)
-                    nc.tensor.matmul_mx(
-                        out=score_banks[g][step % 3][:, block * P : (block + 1) * P],
-                        lhsT=k_codes[rows, k_cols].bitcast(FP8X4),
-                        lhsT_scale=k_scales[rows, k_cols],
-                        rhs=q_mx[i][1][rows, q_cols].bitcast(FP8X4),
-                        rhs_scale=q_mx[i][2][rows, q_cols],
-                        start=True,
-                        stop=True,
+        def scores(h, i, places, c0, c1):
+            a, g = divmod(h, 2)
+            bank = score_banks[g][len(fills[g]) % 3]
+            fills[g].append((h, i, places, c0, c1))
+            rows = row_tiles[g]
+            calls = []
+            for slot, r in enumerate(places):
+                for q0 in range(c0, c1, P):
+                    calls.append((bank, slot * (c1 - c0) + q0 - c0, rows, r, q_mx[a][i], q0))
+            return calls
+
+        def matmuls(*lists):
+            for n in range(max(len(x) for x in lists)):
+                for x in lists:
+                    if n < len(x):
+                        bank, b0, rows, r, mx, q0 = x[n]
+                        nc.tensor.matmul_mx(
+                            out=bank[:, b0 : b0 + P],
+                            lhsT=k_codes[rows, r * P : (r + 1) * P].bitcast(FP8X4),
+                            lhsT_scale=k_scales[rows, r * P : (r + 1) * P],
+                            rhs=mx[1][rows, q0 : q0 + P].bitcast(FP8X4),
+                            rhs_scale=mx[2][rows, q0 : q0 + P],
+                            start=True,
+                            stop=True,
+                        )
+
+        emptied = [0, 0]
+
+        def affine(g, engine="scalar"):
+            n = emptied[g]
+            emptied[g] = n + 1
+            h, i, places, c0, c1 = fills[g][n]
+            for slot, r in enumerate(places):
+                dst = scaled[h][i][:, r, c0:c1]
+                src = score_banks[g][n % 3][:, slot * (c1 - c0) : (slot + 1) * (c1 - c0)]
+                if engine == "scalar":
+                    nc.scalar.activation(out=dst, in_=src, func=IDENT, scale=t_sb[:, r : r + 1], bias=kbt[:, r : r + 1])
+                else:
+                    nc.vector.tensor_scalar(
+                        out=dst, in0=src, scalar1=t_sb[:, r : r + 1], scalar2=kbt[:, r : r + 1], op0=MULT, op1=ADD
                     )
 
-        def bias_scale(step, g):
-            i, places, q0, width = steps[g][step]
-            for slot, r in enumerate(places):
-                nc.scalar.activation(
-                    out=scaled[i][g][:, r, q0 : q0 + width],
-                    in_=score_banks[g][step % 3][:, slot * width : (slot + 1) * width],
-                    func=IDENT,
-                    scale=t_sb[:, r : r + 1],
-                    bias=kbt[:, r : r + 1],
-                )
-
-        def weigh(n):
-            i, g, c0, width = pieces[n]
-            cols = slice(c0, c0 + width)
+        def weigh(h, i, c0, c1):
             nc.vector.tensor_tensor(
-                out=w_mx[n][0][:].rearrange("p (c i) r -> p c r i", i=2),
-                in0=scaled[i][g][:, :, cols].rearrange("p r (c i) -> p c r i", i=2),
-                in1=mask_sb[:, :, i % 2 * HALF + c0 : i % 2 * HALF + c0 + width].rearrange("p r (c i) -> p c r i", i=2),
+                out=w_mx[h][i][0][:, c0:c1].rearrange("p (c i) r -> p c r i", i=WALK),
+                in0=scaled[h][i][:, :, c0:c1].rearrange("p r (c i) -> p c r i", i=WALK),
+                in1=mask_sb[i][:, :, c0:c1].rearrange("p r (c i) -> p c r i", i=WALK),
                 op=MULT,
             )
 
-        def y_bank(n):
-            return y_banks[max(n - 1, 0) % 2]
-
-        def values(n):
-            i, g, q0, width = pieces[n]
-            for c0 in range(0, width, P):
+        def values(bank, b0, h, i, c0, c1):
+            for q0 in range(c0, c1, P):
                 nc.tensor.matmul_mx(
-                    out=y_bank(n)[:, q0 + c0 : q0 + c0 + P],
-                    lhsT=w_mx[n][1][:, c0 : c0 + P].bitcast(FP8X4),
-                    lhsT_scale=w_mx[n][2][:, c0 : c0 + P],
+                    out=y_banks[bank][:, b0 + q0 - c0 : b0 + q0 - c0 + P],
+                    lhsT=w_mx[h][i][1][:, q0 : q0 + P].bitcast(FP8X4),
+                    lhsT_scale=w_mx[h][i][2][:, q0 : q0 + P],
                     rhs=v_mx[1][:].bitcast(FP8X4),
                     rhs_scale=v_mx[2][:],
                     start=True,
                     stop=True,
                 )
 
-        def finish(n, c0, width):
-            i, g = pieces[n][0:2]
-            pair, half = divmod(i, 2)
-            y_sb = tile("y_sb%d" % n, [P, width // P, E], F32)
-            nc.scalar.activation(
-                out=y_sb[:].rearrange("p b e -> p (b e)"),
-                in_=y_bank(n)[:, c0 : c0 + width],
-                func=IDENT,
-                scale=1.0 / 16.0,
-            )
-            q0 = half * HALF + c0
-            nc.sync.dma_start(
-                out=out[2 * pair + g, q0 : q0 + width, :].rearrange("(b m) e -> m b e", m=P), in_=y_sb[:]
-            )
+        def finish(bank, b0, pieces, engine="scalar"):
+            width = sum(c1 - c0 for h, i, c0, c1 in pieces)
+            y_sb = tile("y_sb%d_%d_%d" % pieces[0][0:3], [P, width // P, E], F32)
+            dst = y_sb[:].rearrange("p b e -> p (b e)")
+            src = y_banks[bank][:, b0 : b0 + width]
+            if engine == "scalar":
+                nc.scalar.activation(out=dst, in_=src, func=IDENT, scale=1.0 / 16.0)
+            else:
+                nc.vector.tensor_scalar(out=dst, in0=src, scalar1=1.0 / 16.0, scalar2=None, op0=MULT)
+            block = 0
+            for h, i, c0, c1 in pieces:
+                q0 = PARTS[i][0] + c0
+                blocks = (c1 - c0) // P
+                nc.sync.dma_start(
+                    out=out[h, q0 : q0 + c1 - c0, :].rearrange("(b m) e -> m b e", m=P), in_=y_sb[:, block : block + blocks]
+                )
+                block = block + blocks
 
-        keys()
-        interleave("vector", q_mx[0], q_raw[0], 0, P)
-        interleave("scalar", q_mx[0], q_raw[0], P, HALF)
+        def small_loads():
+            nc.scalar.dma_start(out=t_sb[:], in_=t.rearrange("(p j) o -> p (j o)", j=PACK))
+            nc.scalar.dma_start(out=kb_sb[:], in_=kb.rearrange("(p j) o -> p (j o)", j=PACK))
+            nc.vector.memset(k_words[0:ROWS, N : N + N // PACK], 0)
+            nc.gpsimd.memset(warm[:, 0:1], 0.0)
+            nc.scalar.activation(out=warm[:, 1:2], in_=warm[:, 0:1], func=IDENT)
+
+        load_k(0)
+        small_loads()
+        load_k(1)
+        load_q(0, 0)
+        load_q(1, 0)
+        load_mask(0)
+        cast_k("vector", 0, 0, 64)
         nc.vector.tensor_tensor(out=kbt[:], in0=kb_sb[:], in1=t_sb[:], op=MULT)
-        quantize(q_mx[0], slice(0, P))
-        scores(0, (0,))
-        interleave("scalar", v_mx, v_raw, 0, E)
-        interleave("vector", q_mx[1], q_raw[1], 0, HALF)
-        quantize(q_mx[0], slice(P, HALF))
-        scores(1, (0,))
-        quantize(q_mx[1])
-        quantize(v_mx)
-        scores(2, (0,))
-        bias_scale(0, 0)
-        scores(3, (0,))
-        scores(0, (1,))
-        scores(1, (1,))
-        scores(2, (1,))
-        weigh(0)
-        bias_scale(1, 0)
-        weigh(1)
-        quantize(w_mx[0])
-        bias_scale(2, 0)
-        bias_scale(3, 0)
-        weigh(2)
-        quantize(w_mx[1])
-        bias_scale(0, 1)
-        scores(3, (1,))
-        values(0)
-        values(1)
-        bias_scale(1, 1)
-        interleave("scalar", q_mx[2], q_raw[2], P, HALF)
-        interleave("vector", q_mx[2], q_raw[2], 0, P)
-        quantize(w_mx[2])
-        quantize(q_mx[2])
-        scores(4, (0, 1))
-        values(2)
-        weigh(3)
-        bias_scale(2, 1)
-        scores(5, (0, 1))
-        bias_scale(3, 1)
-        interleave("scalar", q_mx[3], q_raw[3], P, HALF)
-        interleave("vector", q_mx[3], q_raw[3], 0, P)
-        weigh(4)
-        quantize(q_mx[3])
-        scores(6, (0, 1))
-        quantize(w_mx[3])
-        bias_scale(4, 0)
-        bias_scale(5, 0)
-        finish(0, 0, HALF)
-        values(3)
-        weigh(5)
-        quantize(w_mx[4])
-        bias_scale(4, 1)
-        scores(7, (0, 1))
-        bias_scale(5, 1)
-        finish(2, 0, HALF)
-        values(4)
-        finish(3, 0, HALF)
-        weigh(6)
-        quantize(w_mx[5])
-        values(5)
-        bias_scale(6, 0)
-        bias_scale(7, 0)
-        finish(4, 0, HALF)
-        weigh(7)
-        quantize(w_mx[6])
-        values(6)
-        bias_scale(6, 1)
-        bias_scale(7, 1)
-        finish(5, 0, HALF)
-        finish(6, 0, HALF)
-        weigh(8)
-        quantize(w_mx[7])
-        values(7)
-        weigh(9)
-        finish(7, 0, HALF)
-        quantize(w_mx[8])
-        values(8)
-        quantize(w_mx[9])
-        values(9)
-        finish(8, 0, P)
-        finish(9, P, P)
+        cast_k("vector", 1, 0, 44)
+        cast_k("scalar", 1, 44, 64)
+        quantize_k(0, 512)
+        copy_k()
+        load_q(0, 1)
+        load_v()
+        load_q(1, 1)
+        load_mask(1)
+        interleave("vector", q_mx[0][0], q_raw[0][0], 0, 128)
+        interleave("scalar", q_mx[0][0], q_raw[0][0], 128, 256)
+        quantize(q_mx[0][0], 0, 128)
+        matmuls(scores(0, 0, (0, 1), 0, 128))
+        matmuls(scores(0, 0, (2, 3), 0, 128))
+        quantize(q_mx[0][0], 128, 256)
+        matmuls(scores(0, 0, (0, 1, 2, 3), 128, 256))
+        interleave("vector", q_mx[1][0], q_raw[1][0], 0, 160)
+        interleave("scalar", q_mx[1][0], q_raw[1][0], 160, 256)
+        affine(0)
+        affine(0)
+        affine(0)
+        quantize(q_mx[1][0], 0, 256)
+        matmuls(scores(2, 0, (0, 1), 0, 256))
+        matmuls(scores(2, 0, (2, 3), 0, 256))
+        matmuls(scores(1, 0, (0, 1), 0, 256))
+        matmuls(scores(1, 0, (2, 3), 0, 256))
+        matmuls(scores(3, 0, (0, 1), 0, 256))
+        weigh(0, 0, 0, 128)
+        weigh(0, 0, 128, 256)
+        affine(0)
+        affine(0)
+        quantize(w_mx[0][0], 0, 256)
+        interleave("vector", q_mx[0][1], q_raw[0][1], 0, 256)
+        weigh(2, 0, 0, 256)
+        quantize(q_mx[0][1], 0, 256)
+        affine(1)
+        matmuls(scores(3, 0, (2, 3), 0, 256))
+        affine(1)
+        matmuls(scores(0, 1, (0, 1), 0, 256), scores(1, 1, (0, 1), 0, 256))
+        matmuls(scores(0, 1, (2, 3), 0, 256))
+        quantize(w_mx[2][0], 0, 256)
+        weigh(1, 0, 0, 256)
+        interleave("scalar", v_mx, v_raw, 0, 128)
+        affine(1)
+        interleave("scalar", q_mx[1][1], q_raw[1][1], 160, 256)
+        matmuls(scores(1, 1, (2, 3), 0, 256))
+        affine(1)
+        interleave("vector", q_mx[1][1], q_raw[1][1], 0, 160)
+        quantize(w_mx[1][0], 0, 256)
+        quantize(v_mx, 0, 128)
+        quantize(q_mx[1][1], 0, 256)
+        values(0, 0, 0, 0, 0, 256)
+        values(0, 256, 2, 0, 0, 256)
+        values(1, 0, 1, 0, 0, 256)
+        weigh(3, 0, 0, 256)
+        affine(0)
+        affine(0)
+        matmuls(scores(2, 1, (0, 1), 0, 256))
+        matmuls(scores(2, 1, (2, 3), 0, 256))
+        weigh(0, 1, 0, 256)
+        quantize(w_mx[3][0], 0, 256)
+        affine(1)
+        matmuls(scores(3, 1, (0, 1, 2, 3), 0, 128))
+        values(1, 256, 3, 0, 0, 256)
+        affine(1)
+        matmuls(scores(3, 1, (0, 1, 2, 3), 128, 256))
+        finish(0, 0, [(0, 0, 0, 256), (2, 0, 0, 256)])
+        weigh(1, 1, 0, 256)
+        quantize(w_mx[0][1], 0, 256)
+        values(0, 0, 0, 1, 0, 256)
+        affine(0)
+        affine(0)
+        finish(1, 0, [(1, 0, 0, 256), (3, 0, 0, 256)])
+        weigh(2, 1, 0, 256)
+        quantize(w_mx[1][1], 0, 256)
+        values(0, 256, 1, 1, 0, 256)
+        affine(1)
+        affine(1)
+        weigh(3, 1, 0, 128)
+        quantize(w_mx[2][1], 0, 256)
+        values(1, 0, 2, 1, 0, 256)
+        finish(0, 0, [(0, 1, 0, 256), (1, 1, 0, 256)])
+        weigh(3, 1, 128, 256)
+        finish(1, 0, [(2, 1, 0, 256)])
+        quantize(w_mx[3][1], 0, 128)
+        values(0, 0, 3, 1, 0, 128)
+        quantize(w_mx[3][1], 128, 256)
+        values(1, 0, 3, 1, 128, 256)
+        finish(0, 0, [(3, 1, 0, 128)])
+        finish(1, 0, [(3, 1, 128, 256)])

@@ -19,7 +19,7 @@ P = 128
 PACK = 4
 ROWS = D // PACK
 BANK = 512
-WALK = 2
+WALK = 4
 PARTS = ((0, 256), (256, 256))
 
 

@@ -19,7 +19,10 @@ P = 128
 PACK = 4
 ROWS = D // PACK
 BANK = 512
+HALF = 256
 WALK = 4
+BANKS = (3, 2)
+DOUBLES = ()
 PARTS = ((0, 256), (256, 256))
 
 
@@ -33,17 +36,15 @@ def tile_rows_a_lin_kb_mask_kernel(tc, qT, kT, t, v, kb, mask, out):
         def tile(name, shape, dtype):
             return sb.tile(shape, dtype, name=name, align_bytes=64)
 
-        score_banks = [[ps.tile([P, BANK], F32, name="score%d_%d" % (g, i)) for i in range(3)] for g in range(2)]
-        y_banks = [ps.tile([P, BANK], F32, name="y%d" % i) for i in range(2)]
+        score_banks = [[ps.tile([P, BANK], F32, name="score%d_%d" % (g, i)) for i in range(BANKS[g])] for g in range(2)]
+        y_banks = [ps.tile([P, BANK], F32, name="y%d" % i) for i in range(8 - sum(BANKS))]
 
         k_rows = kT[0].rearrange("(p j) n -> p j n", j=PACK)
         q_rows = qT.rearrange("(a g) (p j) n -> a (g p) j n", g=2, j=PACK)
         mask_rows = mask.rearrange("(p j) n -> p j n", j=PACK)
         row_tiles = [slice(g * ROWS, (g + 1) * ROWS) for g in range(2)]
 
-        k_raw = [tile("k_raw%d" % i, [ROWS, PACK, N // 2], F32) for i in range(2)]
-        q_raw = [[tile("q_raw%d_%d" % (a, i), [P, PACK, w], F32) for i, (c0, w) in enumerate(PARTS)] for a in range(2)]
-        mask_sb = [tile("mask%d" % i, [P, PACK, w], F32) for i, (c0, w) in enumerate(PARTS)]
+        k_raw, q_raw, mask_sb = {}, {}, {}
         v_raw = tile("v_raw", [P, PACK, E], F32)
         t_sb = tile("t_sb", [P, PACK], F32)
         kb_sb = tile("kb_sb", [P, PACK], F32)
@@ -64,18 +65,26 @@ def tile_rows_a_lin_kb_mask_kernel(tc, qT, kT, t, v, kb, mask, out):
         q_mx = [[mx_tiles("q%d_%d" % (a, i), w) for i, (c0, w) in enumerate(PARTS)] for a in range(2)]
         v_mx = mx_tiles("v", E)
         scaled = [[tile("scaled%d_%d" % (h, i), [P, PACK, w], F32) for i, (c0, w) in enumerate(PARTS)] for h in range(H)]
+        scaled_pair = {}
+        for g, i in DOUBLES:
+            scaled_pair[g, i] = tile("scaled_pair%d_%d" % (g, i), [P, 2, PACK, HALF], F32)
+            for a in range(2):
+                scaled[2 * a + g][i] = scaled_pair[g, i][:, a]
         w_mx = [[mx_tiles("w%d_%d" % (h, i), w) for i, (c0, w) in enumerate(PARTS)] for h in range(H)]
 
-        def load_k(i):
-            nc.sync.dma_start(out=k_raw[i][:], in_=k_rows[:, :, i * N // 2 : (i + 1) * N // 2])
+        def load_k(n0, n1, queue=nc.sync):
+            k_raw[n0] = tile("k_raw%d" % n0, [ROWS, PACK, n1 - n0], F32)
+            queue.dma_start(out=k_raw[n0][:], in_=k_rows[:, :, n0:n1])
 
-        def load_q(a, i):
-            c0, w = PARTS[i]
-            nc.sync.dma_start(out=q_raw[a][i][:], in_=q_rows[a][:, :, c0 : c0 + w])
+        def load_q(a, c0, c1, queue=nc.sync):
+            raw = tile("q_raw%d_%d" % (a, c0), [P, PACK, c1 - c0], F32)
+            q_raw[a, c0] = (raw, c1)
+            queue.dma_start(out=raw[:], in_=q_rows[a][:, :, c0:c1])
 
-        def load_mask(i):
-            c0, w = PARTS[i]
-            nc.sync.dma_start(out=mask_sb[i][:], in_=mask_rows[:, :, c0 : c0 + w])
+        def load_mask(c0, c1, queue=nc.sync):
+            raw = tile("mask%d" % c0, [P, PACK, c1 - c0], F32)
+            mask_sb[c0] = (raw, c1)
+            queue.dma_start(out=raw[:], in_=mask_rows[:, :, c0:c1])
 
         def load_v():
             nc.sync.dma_start(out=v_raw[:], in_=v[0].rearrange("(p j) e -> p j e", j=PACK))
@@ -89,10 +98,17 @@ def tile_rows_a_lin_kb_mask_kernel(tc, qT, kT, t, v, kb, mask, out):
             else:
                 nc.scalar.copy(out=dst, in_=src)
 
-        def cast_k(engine, i, s0, s1):
-            half = N // 2 // PACK
-            dst = k_bf16[:].rearrange("p (a b s) j -> p a s j b", a=2, b=2)[:, :, i * half + s0 : i * half + s1]
-            src = k_raw[i][:].rearrange("p j (s a b) -> p a s j b", a=2, b=2)[:, :, s0:s1]
+        def cast_k(engine, n0, s0, s1):
+            base = n0 // PACK
+            dst = k_bf16[:].rearrange("p (a b s) j -> p a s j b", a=2, b=2)[:, :, base + s0 : base + s1]
+            src = k_raw[n0][:].rearrange("p j (s a b) -> p a s j b", a=2, b=2)[:, :, s0:s1]
+            cast(engine, dst, src)
+
+        def cast_q(engine, a, c0, c1):
+            start = max(x for b, x in q_raw if b == a and x <= c0)
+            i = c0 // HALF
+            dst = q_mx[a][i][0][:, c0 - i * HALF : c1 - i * HALF, :].rearrange("p (c i) j -> p c j i", i=4)
+            src = q_raw[a, start][0][:, :, c0 - start : c1 - start].rearrange("p j (c i) -> p c j i", i=4)
             cast(engine, dst, src)
 
         def quantize_k(c0, c1):
@@ -118,7 +134,7 @@ def tile_rows_a_lin_kb_mask_kernel(tc, qT, kT, t, v, kb, mask, out):
 
         def scores(h, i, places, c0, c1):
             a, g = divmod(h, 2)
-            bank = score_banks[g][len(fills[g]) % 3]
+            bank = score_banks[g][len(fills[g]) % BANKS[g]]
             fills[g].append((h, i, places, c0, c1))
             rows = row_tiles[g]
             calls = []
@@ -126,6 +142,11 @@ def tile_rows_a_lin_kb_mask_kernel(tc, qT, kT, t, v, kb, mask, out):
                 for q0 in range(c0, c1, P):
                     calls.append((bank, slot * (c1 - c0) + q0 - c0, rows, r, q_mx[a][i], q0))
             return calls
+
+        def scores_pair(g, i, r):
+            bank = score_banks[g][len(fills[g]) % BANKS[g]]
+            fills[g].append((None, i, r, 0, HALF))
+            return [(bank, a * HALF + q0, row_tiles[g], r, q_mx[a][i], q0) for a in range(2) for q0 in range(0, HALF, P)]
 
         def matmuls(*lists):
             for n in range(max(len(x) for x in lists)):
@@ -148,9 +169,18 @@ def tile_rows_a_lin_kb_mask_kernel(tc, qT, kT, t, v, kb, mask, out):
             n = emptied[g]
             emptied[g] = n + 1
             h, i, places, c0, c1 = fills[g][n]
+            if h is None:
+                nc.scalar.activation(
+                    out=scaled_pair[g, i][:, :, places, :],
+                    in_=score_banks[g][n % BANKS[g]][:].rearrange("p (a c) -> p a c", a=2),
+                    func=IDENT,
+                    scale=t_sb[:, places : places + 1],
+                    bias=kbt[:, places : places + 1],
+                )
+                return
             for slot, r in enumerate(places):
                 dst = scaled[h][i][:, r, c0:c1]
-                src = score_banks[g][n % 3][:, slot * (c1 - c0) : (slot + 1) * (c1 - c0)]
+                src = score_banks[g][n % BANKS[g]][:, slot * (c1 - c0) : (slot + 1) * (c1 - c0)]
                 if engine == "scalar":
                     nc.scalar.activation(out=dst, in_=src, func=IDENT, scale=t_sb[:, r : r + 1], bias=kbt[:, r : r + 1])
                 else:
@@ -159,10 +189,11 @@ def tile_rows_a_lin_kb_mask_kernel(tc, qT, kT, t, v, kb, mask, out):
                     )
 
         def weigh(h, i, c0, c1):
+            start = max(x for x in mask_sb if x <= i * HALF + c0) - i * HALF
             nc.vector.tensor_tensor(
                 out=w_mx[h][i][0][:, c0:c1].rearrange("p (c i) r -> p c r i", i=WALK),
                 in0=scaled[h][i][:, :, c0:c1].rearrange("p r (c i) -> p c r i", i=WALK),
-                in1=mask_sb[i][:, :, c0:c1].rearrange("p r (c i) -> p c r i", i=WALK),
+                in1=mask_sb[start + i * HALF][0][:, :, c0 - start : c1 - start].rearrange("p r (c i) -> p c r i", i=WALK),
                 op=MULT,
             )
 
@@ -196,68 +227,73 @@ def tile_rows_a_lin_kb_mask_kernel(tc, qT, kT, t, v, kb, mask, out):
                 )
                 block = block + blocks
 
-        def small_loads():
-            nc.scalar.dma_start(out=t_sb[:], in_=t.rearrange("(p j) o -> p (j o)", j=PACK))
-            nc.scalar.dma_start(out=kb_sb[:], in_=kb.rearrange("(p j) o -> p (j o)", j=PACK))
+        def small_loads(queue):
+            queue.dma_start(out=t_sb[:], in_=t.rearrange("(p j) o -> p (j o)", j=PACK))
+            queue.dma_start(out=kb_sb[:], in_=kb.rearrange("(p j) o -> p (j o)", j=PACK))
+
+        def setup():
             nc.vector.memset(k_words[0:ROWS, N : N + N // PACK], 0)
             nc.gpsimd.memset(warm[:, 0:1], 0.0)
             nc.scalar.activation(out=warm[:, 1:2], in_=warm[:, 0:1], func=IDENT)
 
-        load_k(0)
-        small_loads()
-        load_k(1)
-        load_q(0, 0)
-        load_q(1, 0)
-        load_mask(0)
+        load_k(0, 256)
+        setup()
+        load_k(256, 512)
+        load_q(0, 0, 256)
+        small_loads(nc.sync)
+        load_q(1, 0, 256)
+        load_mask(0, 256)
         cast_k("vector", 0, 0, 64)
-        nc.vector.tensor_tensor(out=kbt[:], in0=kb_sb[:], in1=t_sb[:], op=MULT)
-        cast_k("vector", 1, 0, 44)
-        cast_k("scalar", 1, 44, 64)
+        cast_k("vector", 256, 0, 44)
+        cast_k("scalar", 256, 44, 64)
         quantize_k(0, 512)
         copy_k()
-        load_q(0, 1)
+        load_q(0, 256, 512)
         load_v()
-        load_q(1, 1)
-        load_mask(1)
-        interleave("vector", q_mx[0][0], q_raw[0][0], 0, 128)
-        interleave("scalar", q_mx[0][0], q_raw[0][0], 128, 256)
+        load_q(1, 256, 512)
+        load_mask(256, 512)
+        cast_q("vector", 0, 0, 128)
+        cast_q("scalar", 0, 128, 256)
+        nc.vector.tensor_tensor(out=kbt[:], in0=kb_sb[:], in1=t_sb[:], op=MULT)
         quantize(q_mx[0][0], 0, 128)
         matmuls(scores(0, 0, (0, 1), 0, 128))
         matmuls(scores(0, 0, (2, 3), 0, 128))
         quantize(q_mx[0][0], 128, 256)
         matmuls(scores(0, 0, (0, 1, 2, 3), 128, 256))
-        interleave("vector", q_mx[1][0], q_raw[1][0], 0, 160)
-        interleave("scalar", q_mx[1][0], q_raw[1][0], 160, 256)
+        cast_q("vector", 1, 0, 160)
+        cast_q("scalar", 1, 160, 256)
         affine(0)
         affine(0)
         affine(0)
-        quantize(q_mx[1][0], 0, 256)
+        quantize(q_mx[1][0], 0, 128)
+        quantize(q_mx[1][0], 128, 256)
         matmuls(scores(2, 0, (0, 1), 0, 256))
         matmuls(scores(2, 0, (2, 3), 0, 256))
         matmuls(scores(1, 0, (0, 1), 0, 256))
         matmuls(scores(1, 0, (2, 3), 0, 256))
-        matmuls(scores(3, 0, (0, 1), 0, 256))
         weigh(0, 0, 0, 128)
         weigh(0, 0, 128, 256)
         affine(0)
         affine(0)
         quantize(w_mx[0][0], 0, 256)
-        interleave("vector", q_mx[0][1], q_raw[0][1], 0, 256)
+        cast_q("vector", 0, 256, 512)
         weigh(2, 0, 0, 256)
         quantize(q_mx[0][1], 0, 256)
         affine(1)
-        matmuls(scores(3, 0, (2, 3), 0, 256))
+        matmuls(scores(3, 0, (0, 1), 0, 256))
         affine(1)
-        matmuls(scores(0, 1, (0, 1), 0, 256), scores(1, 1, (0, 1), 0, 256))
+        matmuls(scores(3, 0, (2, 3), 0, 256))
+        matmuls(scores(0, 1, (0, 1), 0, 256))
         matmuls(scores(0, 1, (2, 3), 0, 256))
         quantize(w_mx[2][0], 0, 256)
         weigh(1, 0, 0, 256)
         interleave("scalar", v_mx, v_raw, 0, 128)
         affine(1)
-        interleave("scalar", q_mx[1][1], q_raw[1][1], 160, 256)
-        matmuls(scores(1, 1, (2, 3), 0, 256))
+        matmuls(scores(1, 1, (0, 1), 0, 256))
+        cast_q("scalar", 1, 384, 512)
         affine(1)
-        interleave("vector", q_mx[1][1], q_raw[1][1], 0, 160)
+        matmuls(scores(1, 1, (2, 3), 0, 256))
+        cast_q("vector", 1, 256, 384)
         quantize(w_mx[1][0], 0, 256)
         quantize(v_mx, 0, 128)
         quantize(q_mx[1][1], 0, 256)
@@ -279,24 +315,25 @@ def tile_rows_a_lin_kb_mask_kernel(tc, qT, kT, t, v, kb, mask, out):
         finish(0, 0, [(0, 0, 0, 256), (2, 0, 0, 256)])
         weigh(1, 1, 0, 256)
         quantize(w_mx[0][1], 0, 256)
-        values(0, 0, 0, 1, 0, 256)
+        values(2, 0, 0, 1, 0, 256)
         affine(0)
         affine(0)
         finish(1, 0, [(1, 0, 0, 256), (3, 0, 0, 256)])
         weigh(2, 1, 0, 256)
         quantize(w_mx[1][1], 0, 256)
-        values(0, 256, 1, 1, 0, 256)
+        values(0, 0, 1, 1, 0, 256)
         affine(1)
         affine(1)
+        finish(2, 0, [(0, 1, 0, 256)])
+        finish(0, 0, [(1, 1, 0, 256)])
         weigh(3, 1, 0, 128)
         quantize(w_mx[2][1], 0, 256)
         values(1, 0, 2, 1, 0, 256)
-        finish(0, 0, [(0, 1, 0, 256), (1, 1, 0, 256)])
         weigh(3, 1, 128, 256)
         finish(1, 0, [(2, 1, 0, 256)])
         quantize(w_mx[3][1], 0, 128)
-        values(0, 0, 3, 1, 0, 128)
+        values(2, 0, 3, 1, 0, 128)
         quantize(w_mx[3][1], 128, 256)
-        values(1, 0, 3, 1, 128, 256)
-        finish(0, 0, [(3, 1, 0, 128)])
-        finish(1, 0, [(3, 1, 128, 256)])
+        values(0, 0, 3, 1, 128, 256)
+        finish(2, 0, [(3, 1, 0, 128)])
+        finish(0, 0, [(3, 1, 128, 256)])

@@ -138,8 +138,8 @@ def tile_rows_a_lin_kb_mask_kernel(tc, qT, kT, t, v, kb, mask, out):
             fills[g].append((h, i, places, c0, c1))
             rows = row_tiles[g]
             calls = []
-            for slot, r in enumerate(places):
-                for q0 in range(c0, c1, P):
+            for q0 in range(c0, c1, P):
+                for slot, r in enumerate(places):
                     calls.append((bank, slot * (c1 - c0) + q0 - c0, rows, r, q_mx[a][i], q0))
             return calls
 
@@ -237,10 +237,10 @@ def tile_rows_a_lin_kb_mask_kernel(tc, qT, kT, t, v, kb, mask, out):
             nc.scalar.activation(out=warm[:, 1:2], in_=warm[:, 0:1], func=IDENT)
 
         load_k(0, 256)
+        small_loads(nc.scalar)
         setup()
         load_k(256, 512)
         load_q(0, 0, 256)
-        small_loads(nc.sync)
         load_q(1, 0, 256)
         load_mask(0, 256)
         cast_k("vector", 0, 0, 64)

@@ -13,17 +13,18 @@ I32 = mybir.dt.int32
 FP8X4 = mybir.dt.float8_e4m3fn_x4
 IDENT = mybir.ActivationFunctionType.Identity
 MULT = mybir.AluOpType.mult
-ADD = mybir.AluOpType.add
 
 P = 128
 PACK = 4
 ROWS = D // PACK
 BANK = 512
-HALF = 256
-WALK = 4
-BANKS = (3, 2)
-DOUBLES = ()
-PARTS = ((0, 256), (256, 256))
+HALF = NQ // 2
+RUN = 4
+SCORE_BANKS = (3, 2)
+Y_BANKS = 3
+K_VECTOR = 44
+Q_VECTOR = 160
+LOW, HIGH, ALL = (0, 1), (2, 3), (0, 1, 2, 3)
 
 
 def tile_rows_a_lin_kb_mask_kernel(tc, qT, kT, t, v, kb, mask, out):
@@ -36,15 +37,26 @@ def tile_rows_a_lin_kb_mask_kernel(tc, qT, kT, t, v, kb, mask, out):
         def tile(name, shape, dtype):
             return sb.tile(shape, dtype, name=name, align_bytes=64)
 
-        score_banks = [[ps.tile([P, BANK], F32, name="score%d_%d" % (g, i)) for i in range(BANKS[g])] for g in range(2)]
-        y_banks = [ps.tile([P, BANK], F32, name="y%d" % i) for i in range(8 - sum(BANKS))]
+        def mx_tiles(name, columns):
+            return (
+                tile(name + "_bf16", [P, columns, PACK], BF16),
+                tile(name + "_codes", [P, columns], U32),
+                tile(name + "_scales", [P, columns], U8),
+            )
+
+        score_banks = [
+            [ps.tile([P, BANK], F32, name="score%d_%d" % (g, i)) for i in range(SCORE_BANKS[g])] for g in range(2)
+        ]
+        y_banks = [ps.tile([P, BANK], F32, name="y%d" % i) for i in range(Y_BANKS)]
 
         k_rows = kT[0].rearrange("(p j) n -> p j n", j=PACK)
         q_rows = qT.rearrange("(a g) (p j) n -> a (g p) j n", g=2, j=PACK)
-        mask_rows = mask.rearrange("(p j) n -> p j n", j=PACK)
+        mask_rows = mask.rearrange("(p r) n -> p r n", r=PACK)
         row_tiles = [slice(g * ROWS, (g + 1) * ROWS) for g in range(2)]
 
-        k_raw, q_raw, mask_sb = {}, {}, {}
+        k_raw = [tile("k_raw%d" % i, [ROWS, PACK, N // 2], F32) for i in range(2)]
+        q_raw = [[tile("q_raw%d_%d" % (pair, half), [P, PACK, HALF], F32) for half in range(2)] for pair in range(2)]
+        mask_sb = [tile("mask%d" % half, [P, PACK, HALF], F32) for half in range(2)]
         v_raw = tile("v_raw", [P, PACK, E], F32)
         t_sb = tile("t_sb", [P, PACK], F32)
         kb_sb = tile("kb_sb", [P, PACK], F32)
@@ -54,76 +66,35 @@ def tile_rows_a_lin_kb_mask_kernel(tc, qT, kT, t, v, kb, mask, out):
         k_codes = k_words[:, 0:N]
         k_scales = k_words[:, N : N + N // PACK].bitcast(U8)
         k_bf16 = tile("k_bf16", [ROWS, N, PACK], BF16)
-
-        def mx_tiles(name, columns):
-            return (
-                tile(name + "_bf16", [P, columns, PACK], BF16),
-                tile(name + "_codes", [P, columns], U32),
-                tile(name + "_scales", [P, columns], U8),
-            )
-
-        q_mx = [[mx_tiles("q%d_%d" % (a, i), w) for i, (c0, w) in enumerate(PARTS)] for a in range(2)]
+        q_mx = [[mx_tiles("q%d_%d" % (pair, half), HALF) for half in range(2)] for pair in range(2)]
         v_mx = mx_tiles("v", E)
-        scaled = [[tile("scaled%d_%d" % (h, i), [P, PACK, w], F32) for i, (c0, w) in enumerate(PARTS)] for h in range(H)]
-        scaled_pair = {}
-        for g, i in DOUBLES:
-            scaled_pair[g, i] = tile("scaled_pair%d_%d" % (g, i), [P, 2, PACK, HALF], F32)
-            for a in range(2):
-                scaled[2 * a + g][i] = scaled_pair[g, i][:, a]
-        w_mx = [[mx_tiles("w%d_%d" % (h, i), w) for i, (c0, w) in enumerate(PARTS)] for h in range(H)]
+        scaled = [[tile("scaled%d_%d" % (h, half), [P, PACK, HALF], F32) for half in range(2)] for h in range(H)]
+        w_mx = [[mx_tiles("w%d_%d" % (h, half), HALF) for half in range(2)] for h in range(H)]
 
-        def load_k(n0, n1, queue=nc.sync):
-            k_raw[n0] = tile("k_raw%d" % n0, [ROWS, PACK, n1 - n0], F32)
-            queue.dma_start(out=k_raw[n0][:], in_=k_rows[:, :, n0:n1])
+        def load_half(dst, rows, half):
+            nc.sync.dma_start(out=dst[:], in_=rows[:, :, half * HALF : (half + 1) * HALF])
 
-        def load_q(a, c0, c1, queue=nc.sync):
-            raw = tile("q_raw%d_%d" % (a, c0), [P, PACK, c1 - c0], F32)
-            q_raw[a, c0] = (raw, c1)
-            queue.dma_start(out=raw[:], in_=q_rows[a][:, :, c0:c1])
-
-        def load_mask(c0, c1, queue=nc.sync):
-            raw = tile("mask%d" % c0, [P, PACK, c1 - c0], F32)
-            mask_sb[c0] = (raw, c1)
-            queue.dma_start(out=raw[:], in_=mask_rows[:, :, c0:c1])
-
-        def load_v():
-            nc.sync.dma_start(out=v_raw[:], in_=v[0].rearrange("(p j) e -> p j e", j=PACK))
-
-        def copy_k():
-            nc.sync.dma_start(out=k_words[ROWS:P], in_=k_words[0:ROWS])
-
-        def cast(engine, dst, src):
+        def round_copy(engine, dst, src):
             if engine == "vector":
                 nc.vector.tensor_copy(out=dst, in_=src)
             else:
                 nc.scalar.copy(out=dst, in_=src)
 
-        def cast_k(engine, n0, s0, s1):
-            base = n0 // PACK
+        def round_keys(engine, half, s0, s1):
+            base = half * N // 2 // PACK
             dst = k_bf16[:].rearrange("p (a b s) j -> p a s j b", a=2, b=2)[:, :, base + s0 : base + s1]
-            src = k_raw[n0][:].rearrange("p j (s a b) -> p a s j b", a=2, b=2)[:, :, s0:s1]
-            cast(engine, dst, src)
+            src = k_raw[half][:].rearrange("p j (s a b) -> p a s j b", a=2, b=2)[:, :, s0:s1]
+            round_copy(engine, dst, src)
 
-        def cast_q(engine, a, c0, c1):
-            start = max(x for b, x in q_raw if b == a and x <= c0)
-            i = c0 // HALF
-            dst = q_mx[a][i][0][:, c0 - i * HALF : c1 - i * HALF, :].rearrange("p (c i) j -> p c j i", i=4)
-            src = q_raw[a, start][0][:, :, c0 - start : c1 - start].rearrange("p j (c i) -> p c j i", i=4)
-            cast(engine, dst, src)
+        def round_rows(engine, mx, raw, c0, c1):
+            dst = mx[0][:, c0:c1, :].rearrange("p (c i) j -> p c j i", i=RUN)
+            src = raw[:, :, c0:c1].rearrange("p j (c i) -> p c j i", i=RUN)
+            round_copy(engine, dst, src)
 
-        def quantize_k(c0, c1):
-            nc.vector.quantize_mx(
-                out=k_codes[0:ROWS, c0:c1].bitcast(FP8X4),
-                scales=k_scales[0:ROWS, c0:c1],
-                in_=k_bf16[:, c0:c1, :].rearrange("p c j -> p (c j)"),
-            )
+        def round_queries(engine, pair, half, c0, c1):
+            round_rows(engine, q_mx[pair][half], q_raw[pair][half], c0, c1)
 
-        def interleave(engine, mx, raw, c0, c1):
-            dst = mx[0][:, c0:c1, :].rearrange("p (c i) j -> p c j i", i=4)
-            src = raw[:, :, c0:c1].rearrange("p j (c i) -> p c j i", i=4)
-            cast(engine, dst, src)
-
-        def quantize(mx, c0, c1):
+        def quantize(mx, c0=0, c1=HALF):
             nc.vector.quantize_mx(
                 out=mx[1][:, c0:c1].bitcast(FP8X4),
                 scales=mx[2][:, c0:c1],
@@ -131,209 +102,178 @@ def tile_rows_a_lin_kb_mask_kernel(tc, qT, kT, t, v, kb, mask, out):
             )
 
         fills = [[], []]
-
-        def scores(h, i, places, c0, c1):
-            a, g = divmod(h, 2)
-            bank = score_banks[g][len(fills[g]) % BANKS[g]]
-            fills[g].append((h, i, places, c0, c1))
-            rows = row_tiles[g]
-            calls = []
-            for q0 in range(c0, c1, P):
-                for slot, r in enumerate(places):
-                    calls.append((bank, slot * (c1 - c0) + q0 - c0, rows, r, q_mx[a][i], q0))
-            return calls
-
-        def scores_pair(g, i, r):
-            bank = score_banks[g][len(fills[g]) % BANKS[g]]
-            fills[g].append((None, i, r, 0, HALF))
-            return [(bank, a * HALF + q0, row_tiles[g], r, q_mx[a][i], q0) for a in range(2) for q0 in range(0, HALF, P)]
-
-        def matmuls(*lists):
-            for n in range(max(len(x) for x in lists)):
-                for x in lists:
-                    if n < len(x):
-                        bank, b0, rows, r, mx, q0 = x[n]
-                        nc.tensor.matmul_mx(
-                            out=bank[:, b0 : b0 + P],
-                            lhsT=k_codes[rows, r * P : (r + 1) * P].bitcast(FP8X4),
-                            lhsT_scale=k_scales[rows, r * P : (r + 1) * P],
-                            rhs=mx[1][rows, q0 : q0 + P].bitcast(FP8X4),
-                            rhs_scale=mx[2][rows, q0 : q0 + P],
-                            start=True,
-                            stop=True,
-                        )
-
         emptied = [0, 0]
 
-        def affine(g, engine="scalar"):
-            n = emptied[g]
-            emptied[g] = n + 1
-            h, i, places, c0, c1 = fills[g][n]
-            if h is None:
-                nc.scalar.activation(
-                    out=scaled_pair[g, i][:, :, places, :],
-                    in_=score_banks[g][n % BANKS[g]][:].rearrange("p (a c) -> p a c", a=2),
-                    func=IDENT,
-                    scale=t_sb[:, places : places + 1],
-                    bias=kbt[:, places : places + 1],
-                )
-                return
-            for slot, r in enumerate(places):
-                dst = scaled[h][i][:, r, c0:c1]
-                src = score_banks[g][n % BANKS[g]][:, slot * (c1 - c0) : (slot + 1) * (c1 - c0)]
-                if engine == "scalar":
-                    nc.scalar.activation(out=dst, in_=src, func=IDENT, scale=t_sb[:, r : r + 1], bias=kbt[:, r : r + 1])
-                else:
-                    nc.vector.tensor_scalar(
-                        out=dst, in0=src, scalar1=t_sb[:, r : r + 1], scalar2=kbt[:, r : r + 1], op0=MULT, op1=ADD
+        def scores(h, half, places, c0=0, c1=HALF):
+            pair, g = divmod(h, 2)
+            bank = score_banks[g][len(fills[g]) % SCORE_BANKS[g]]
+            fills[g].append((h, half, places, c0, c1))
+            rows = row_tiles[g]
+            for q0 in range(c0, c1, P):
+                for slot, r in enumerate(places):
+                    b0 = slot * (c1 - c0) + q0 - c0
+                    nc.tensor.matmul_mx(
+                        out=bank[:, b0 : b0 + P],
+                        lhsT=k_codes[rows, r * P : (r + 1) * P].bitcast(FP8X4),
+                        lhsT_scale=k_scales[rows, r * P : (r + 1) * P],
+                        rhs=q_mx[pair][half][1][rows, q0 : q0 + P].bitcast(FP8X4),
+                        rhs_scale=q_mx[pair][half][2][rows, q0 : q0 + P],
+                        start=True,
+                        stop=True,
                     )
 
-        def weigh(h, i, c0, c1):
-            start = max(x for x in mask_sb if x <= i * HALF + c0) - i * HALF
+        def affine(g):
+            n = emptied[g]
+            emptied[g] = n + 1
+            h, half, places, c0, c1 = fills[g][n]
+            for slot, r in enumerate(places):
+                nc.scalar.activation(
+                    out=scaled[h][half][:, r, c0:c1],
+                    in_=score_banks[g][n % SCORE_BANKS[g]][:, slot * (c1 - c0) : (slot + 1) * (c1 - c0)],
+                    func=IDENT,
+                    scale=t_sb[:, r : r + 1],
+                    bias=kbt[:, r : r + 1],
+                )
+
+        def weigh(h, half, c0=0, c1=HALF):
             nc.vector.tensor_tensor(
-                out=w_mx[h][i][0][:, c0:c1].rearrange("p (c i) r -> p c r i", i=WALK),
-                in0=scaled[h][i][:, :, c0:c1].rearrange("p r (c i) -> p c r i", i=WALK),
-                in1=mask_sb[start + i * HALF][0][:, :, c0 - start : c1 - start].rearrange("p r (c i) -> p c r i", i=WALK),
+                out=w_mx[h][half][0][:, c0:c1].rearrange("p (c i) r -> p c r i", i=RUN),
+                in0=scaled[h][half][:, :, c0:c1].rearrange("p r (c i) -> p c r i", i=RUN),
+                in1=mask_sb[half][:, :, c0:c1].rearrange("p r (c i) -> p c r i", i=RUN),
                 op=MULT,
             )
 
-        def values(bank, b0, h, i, c0, c1):
+        def values(bank, b0, h, half, c0=0, c1=HALF):
             for q0 in range(c0, c1, P):
                 nc.tensor.matmul_mx(
                     out=y_banks[bank][:, b0 + q0 - c0 : b0 + q0 - c0 + P],
-                    lhsT=w_mx[h][i][1][:, q0 : q0 + P].bitcast(FP8X4),
-                    lhsT_scale=w_mx[h][i][2][:, q0 : q0 + P],
+                    lhsT=w_mx[h][half][1][:, q0 : q0 + P].bitcast(FP8X4),
+                    lhsT_scale=w_mx[h][half][2][:, q0 : q0 + P],
                     rhs=v_mx[1][:].bitcast(FP8X4),
                     rhs_scale=v_mx[2][:],
                     start=True,
                     stop=True,
                 )
 
-        def finish(bank, b0, pieces, engine="scalar"):
-            width = sum(c1 - c0 for h, i, c0, c1 in pieces)
-            y_sb = tile("y_sb%d_%d_%d" % pieces[0][0:3], [P, width // P, E], F32)
-            dst = y_sb[:].rearrange("p b e -> p (b e)")
-            src = y_banks[bank][:, b0 : b0 + width]
-            if engine == "scalar":
-                nc.scalar.activation(out=dst, in_=src, func=IDENT, scale=1.0 / 16.0)
-            else:
-                nc.vector.tensor_scalar(out=dst, in0=src, scalar1=1.0 / 16.0, scalar2=None, op0=MULT)
-            block = 0
-            for h, i, c0, c1 in pieces:
-                q0 = PARTS[i][0] + c0
-                blocks = (c1 - c0) // P
+        def finish(bank, half, heads, c0=0, c1=HALF):
+            blocks = (c1 - c0) // P
+            y_sb = tile("y_sb%d_%d_%d" % (heads[0], half, c0), [P, len(heads) * blocks, E], F32)
+            nc.scalar.activation(
+                out=y_sb[:].rearrange("p b e -> p (b e)"),
+                in_=y_banks[bank][:, 0 : len(heads) * blocks * E],
+                func=IDENT,
+                scale=1.0 / 16.0,
+            )
+            q0 = half * HALF + c0
+            for n, h in enumerate(heads):
                 nc.sync.dma_start(
-                    out=out[h, q0 : q0 + c1 - c0, :].rearrange("(b m) e -> m b e", m=P), in_=y_sb[:, block : block + blocks]
+                    out=out[h, q0 : q0 + c1 - c0, :].rearrange("(b m) e -> m b e", m=P),
+                    in_=y_sb[:, n * blocks : (n + 1) * blocks],
                 )
-                block = block + blocks
 
-        def small_loads(queue):
-            queue.dma_start(out=t_sb[:], in_=t.rearrange("(p j) o -> p (j o)", j=PACK))
-            queue.dma_start(out=kb_sb[:], in_=kb.rearrange("(p j) o -> p (j o)", j=PACK))
+        load_half(k_raw[0], k_rows, 0)
+        nc.scalar.dma_start(out=t_sb[:], in_=t.rearrange("(p r) o -> p (r o)", r=PACK))
+        nc.scalar.dma_start(out=kb_sb[:], in_=kb.rearrange("(p r) o -> p (r o)", r=PACK))
+        nc.vector.memset(k_words[0:ROWS, N : N + N // PACK], 0)
+        nc.gpsimd.memset(warm[:, 0:1], 0.0)
+        nc.scalar.activation(out=warm[:, 1:2], in_=warm[:, 0:1], func=IDENT)
+        load_half(k_raw[1], k_rows, 1)
+        load_half(q_raw[0][0], q_rows[0], 0)
+        load_half(q_raw[1][0], q_rows[1], 0)
+        load_half(mask_sb[0], mask_rows, 0)
 
-        def setup():
-            nc.vector.memset(k_words[0:ROWS, N : N + N // PACK], 0)
-            nc.gpsimd.memset(warm[:, 0:1], 0.0)
-            nc.scalar.activation(out=warm[:, 1:2], in_=warm[:, 0:1], func=IDENT)
+        round_keys("vector", 0, 0, ROWS)
+        round_keys("vector", 1, 0, K_VECTOR)
+        round_keys("scalar", 1, K_VECTOR, ROWS)
+        nc.vector.quantize_mx(
+            out=k_codes[0:ROWS].bitcast(FP8X4), scales=k_scales[0:ROWS], in_=k_bf16[:].rearrange("p c j -> p (c j)")
+        )
+        nc.sync.dma_start(out=k_words[ROWS:P], in_=k_words[0:ROWS])
+        nc.sync.dma_start(out=v_raw[:], in_=v[0].rearrange("(p r) e -> p r e", r=PACK))
+        load_half(q_raw[0][1], q_rows[0], 1)
+        load_half(q_raw[1][1], q_rows[1], 1)
+        load_half(mask_sb[1], mask_rows, 1)
 
-        load_k(0, 256)
-        small_loads(nc.scalar)
-        setup()
-        load_k(256, 512)
-        load_q(0, 0, 256)
-        load_q(1, 0, 256)
-        load_mask(0, 256)
-        cast_k("vector", 0, 0, 64)
-        cast_k("vector", 256, 0, 44)
-        cast_k("scalar", 256, 44, 64)
-        quantize_k(0, 512)
-        copy_k()
-        load_q(0, 256, 512)
-        load_v()
-        load_q(1, 256, 512)
-        load_mask(256, 512)
-        cast_q("vector", 0, 0, 128)
-        cast_q("scalar", 0, 128, 256)
+        round_queries("vector", 0, 0, 0, P)
+        round_queries("scalar", 0, 0, P, HALF)
         nc.vector.tensor_tensor(out=kbt[:], in0=kb_sb[:], in1=t_sb[:], op=MULT)
-        quantize(q_mx[0][0], 0, 128)
-        matmuls(scores(0, 0, (0, 1), 0, 128))
-        matmuls(scores(0, 0, (2, 3), 0, 128))
-        quantize(q_mx[0][0], 128, 256)
-        matmuls(scores(0, 0, (0, 1, 2, 3), 128, 256))
-        cast_q("vector", 1, 0, 160)
-        cast_q("scalar", 1, 160, 256)
+        quantize(q_mx[0][0], 0, P)
+        scores(0, 0, LOW, 0, P)
+        scores(0, 0, HIGH, 0, P)
+        quantize(q_mx[0][0], P, HALF)
+        scores(0, 0, ALL, P, HALF)
+        round_queries("vector", 1, 0, 0, Q_VECTOR)
+        round_queries("scalar", 1, 0, Q_VECTOR, HALF)
+        for fill in range(SCORE_BANKS[0]):
+            affine(0)
+        quantize(q_mx[1][0], 0, P)
+        quantize(q_mx[1][0], P, HALF)
+        for h in (2, 1):
+            scores(h, 0, LOW)
+            scores(h, 0, HIGH)
+        weigh(0, 0, 0, P)
+        weigh(0, 0, P, HALF)
+        round_rows("vector", v_mx, v_raw, 0, E)
+        quantize(w_mx[0][0])
+        quantize(v_mx, 0, E)
+
         affine(0)
         affine(0)
-        affine(0)
-        quantize(q_mx[1][0], 0, 128)
-        quantize(q_mx[1][0], 128, 256)
-        matmuls(scores(2, 0, (0, 1), 0, 256))
-        matmuls(scores(2, 0, (2, 3), 0, 256))
-        matmuls(scores(1, 0, (0, 1), 0, 256))
-        matmuls(scores(1, 0, (2, 3), 0, 256))
-        weigh(0, 0, 0, 128)
-        weigh(0, 0, 128, 256)
-        affine(0)
-        affine(0)
-        quantize(w_mx[0][0], 0, 256)
-        cast_q("vector", 0, 256, 512)
-        weigh(2, 0, 0, 256)
-        quantize(q_mx[0][1], 0, 256)
+        weigh(2, 0)
+        for places in (LOW, HIGH):
+            affine(1)
+            scores(3, 0, places)
+        round_queries("scalar", 0, 1, P, HALF)
+        round_queries("vector", 0, 1, 0, P)
+        quantize(w_mx[2][0])
+        quantize(q_mx[0][1])
+        scores(0, 1, LOW)
+        scores(0, 1, HIGH)
+        for places in (LOW, HIGH):
+            affine(1)
+            scores(1, 1, places)
+        values(0, 0, 0, 0)
+        values(0, HALF, 2, 0)
+        round_queries("scalar", 1, 1, P, HALF)
+        weigh(1, 0)
+        round_queries("vector", 1, 1, 0, P)
+        quantize(w_mx[1][0])
+        values(1, 0, 1, 0)
+        quantize(q_mx[1][1])
+        weigh(3, 0)
+
+        for places in (LOW, HIGH):
+            affine(0)
+            scores(2, 1, places)
+        weigh(0, 1)
+        quantize(w_mx[3][0])
         affine(1)
-        matmuls(scores(3, 0, (0, 1), 0, 256))
+        scores(3, 1, ALL, 0, P)
+        values(1, HALF, 3, 0)
         affine(1)
-        matmuls(scores(3, 0, (2, 3), 0, 256))
-        matmuls(scores(0, 1, (0, 1), 0, 256))
-        matmuls(scores(0, 1, (2, 3), 0, 256))
-        quantize(w_mx[2][0], 0, 256)
-        weigh(1, 0, 0, 256)
-        interleave("scalar", v_mx, v_raw, 0, 128)
-        affine(1)
-        matmuls(scores(1, 1, (0, 1), 0, 256))
-        cast_q("scalar", 1, 384, 512)
-        affine(1)
-        matmuls(scores(1, 1, (2, 3), 0, 256))
-        cast_q("vector", 1, 256, 384)
-        quantize(w_mx[1][0], 0, 256)
-        quantize(v_mx, 0, 128)
-        quantize(q_mx[1][1], 0, 256)
-        values(0, 0, 0, 0, 0, 256)
-        values(0, 256, 2, 0, 0, 256)
-        values(1, 0, 1, 0, 0, 256)
-        weigh(3, 0, 0, 256)
+        scores(3, 1, ALL, P, HALF)
+        finish(0, 0, (0, 2))
+        weigh(1, 1)
+        quantize(w_mx[0][1])
+        values(2, 0, 0, 1)
         affine(0)
         affine(0)
-        matmuls(scores(2, 1, (0, 1), 0, 256))
-        matmuls(scores(2, 1, (2, 3), 0, 256))
-        weigh(0, 1, 0, 256)
-        quantize(w_mx[3][0], 0, 256)
-        affine(1)
-        matmuls(scores(3, 1, (0, 1, 2, 3), 0, 128))
-        values(1, 256, 3, 0, 0, 256)
-        affine(1)
-        matmuls(scores(3, 1, (0, 1, 2, 3), 128, 256))
-        finish(0, 0, [(0, 0, 0, 256), (2, 0, 0, 256)])
-        weigh(1, 1, 0, 256)
-        quantize(w_mx[0][1], 0, 256)
-        values(2, 0, 0, 1, 0, 256)
-        affine(0)
-        affine(0)
-        finish(1, 0, [(1, 0, 0, 256), (3, 0, 0, 256)])
-        weigh(2, 1, 0, 256)
-        quantize(w_mx[1][1], 0, 256)
-        values(0, 0, 1, 1, 0, 256)
+        finish(1, 0, (1, 3))
+        weigh(2, 1)
+        quantize(w_mx[1][1])
+        values(0, 0, 1, 1)
         affine(1)
         affine(1)
-        finish(2, 0, [(0, 1, 0, 256)])
-        finish(0, 0, [(1, 1, 0, 256)])
-        weigh(3, 1, 0, 128)
-        quantize(w_mx[2][1], 0, 256)
-        values(1, 0, 2, 1, 0, 256)
-        weigh(3, 1, 128, 256)
-        finish(1, 0, [(2, 1, 0, 256)])
-        quantize(w_mx[3][1], 0, 128)
-        values(2, 0, 3, 1, 0, 128)
-        quantize(w_mx[3][1], 128, 256)
-        values(0, 0, 3, 1, 128, 256)
-        finish(2, 0, [(3, 1, 0, 128)])
-        finish(0, 0, [(3, 1, 128, 256)])
+        finish(2, 1, (0,))
+        finish(0, 1, (1,))
+        weigh(3, 1, 0, P)
+        quantize(w_mx[2][1])
+        values(1, 0, 2, 1)
+        weigh(3, 1, P, HALF)
+        finish(1, 1, (2,))
+        last_blocks = ((2, 0), (0, P))
+        for bank, c0 in last_blocks:
+            quantize(w_mx[3][1], c0, c0 + P)
+            values(bank, 0, 3, 1, c0, c0 + P)
+        for bank, c0 in last_blocks:
+            finish(bank, 1, (3,), c0, c0 + P)

@@ -24,6 +24,8 @@ SCORE_BANKS = (3, 2)
 Y_BANKS = 3
 K_VECTOR = 44
 Q_VECTOR = 160
+K_START, K_END = 32, 96
+PAIR_WORDS = 2 * P + 2 * P // PACK
 LOW, HIGH, ALL = (0, 1), (2, 3), (0, 1, 2, 3)
 
 
@@ -54,7 +56,7 @@ def tile_rows_a_lin_kb_mask_kernel(tc, qT, kT, t, v, kb, mask, out):
         mask_rows = mask.rearrange("(p r) n -> p r n", r=PACK)
         row_tiles = [slice(g * ROWS, (g + 1) * ROWS) for g in range(2)]
 
-        k_raw = [tile("k_raw%d" % i, [ROWS, PACK, N // 2], F32) for i in range(2)]
+        k_raw = [tile("k_raw%d" % i, [K_END, PACK, N // 2], F32) for i in range(2)]
         q_raw = [[tile("q_raw%d_%d" % (pair, half), [P, PACK, HALF], F32) for half in range(2)] for pair in range(2)]
         mask_sb = [tile("mask%d" % half, [P, PACK, HALF], F32) for half in range(2)]
         v_raw = tile("v_raw", [P, PACK, E], F32)
@@ -62,10 +64,16 @@ def tile_rows_a_lin_kb_mask_kernel(tc, qT, kT, t, v, kb, mask, out):
         kb_sb = tile("kb_sb", [P, PACK], F32)
         kbt = tile("kbt", [P, PACK], F32)
         warm = tile("warm", [P, 2], F32)
-        k_words = tile("k_words", [P, N + N // PACK], I32)
-        k_codes = k_words[:, 0:N]
-        k_scales = k_words[:, N : N + N // PACK].bitcast(U8)
-        k_bf16 = tile("k_bf16", [ROWS, N, PACK], BF16)
+        k_made = tile("k_made", [K_END, 2, PAIR_WORDS], I32)
+        k_words = tile("k_words", [P, 2, PAIR_WORDS], I32)
+        k_bf16 = tile("k_bf16", [K_END, N, PACK], BF16)
+
+        def place_codes(words, r):
+            return words[:, r // 2, r % 2 * P : (r % 2 + 1) * P].bitcast(FP8X4)
+
+        def place_scales(words, r):
+            return words[:, r // 2, 2 * P : PAIR_WORDS].bitcast(U8)[:, r % 2 * P : (r % 2 + 1) * P]
+
         q_mx = [[mx_tiles("q%d_%d" % (pair, half), HALF) for half in range(2)] for pair in range(2)]
         v_mx = mx_tiles("v", E)
         scaled = [[tile("scaled%d_%d" % (h, half), [P, PACK, HALF], F32) for half in range(2)] for h in range(H)]
@@ -114,8 +122,8 @@ def tile_rows_a_lin_kb_mask_kernel(tc, qT, kT, t, v, kb, mask, out):
                     b0 = slot * (c1 - c0) + q0 - c0
                     nc.tensor.matmul_mx(
                         out=bank[:, b0 : b0 + P],
-                        lhsT=k_codes[rows, r * P : (r + 1) * P].bitcast(FP8X4),
-                        lhsT_scale=k_scales[rows, r * P : (r + 1) * P],
+                        lhsT=place_codes(k_words[rows], r),
+                        lhsT_scale=place_scales(k_words[rows], r),
                         rhs=q_mx[pair][half][1][rows, q0 : q0 + P].bitcast(FP8X4),
                         rhs_scale=q_mx[pair][half][2][rows, q0 : q0 + P],
                         start=True,
@@ -171,46 +179,51 @@ def tile_rows_a_lin_kb_mask_kernel(tc, qT, kT, t, v, kb, mask, out):
                     in_=y_sb[:, n * blocks : (n + 1) * blocks],
                 )
 
-        load_half(k_raw[0], k_rows, 0)
+        for raw in k_raw:
+            nc.vector.memset(raw[0:K_START].bitcast(U32), 0)
+        load_half(k_raw[0][K_START:K_END], k_rows, 0)
         nc.scalar.dma_start(out=t_sb[:], in_=t.rearrange("(p r) o -> p (r o)", r=PACK))
         nc.scalar.dma_start(out=kb_sb[:], in_=kb.rearrange("(p r) o -> p (r o)", r=PACK))
-        nc.vector.memset(k_words[0:ROWS, N : N + N // PACK], 0)
         nc.gpsimd.memset(warm[:, 0:1], 0.0)
+        nc.vector.memset(k_made[:, :, 2 * P : PAIR_WORDS], 0)
         nc.scalar.activation(out=warm[:, 1:2], in_=warm[:, 0:1], func=IDENT)
-        load_half(k_raw[1], k_rows, 1)
+        load_half(k_raw[1][K_START:K_END], k_rows, 1)
         load_half(q_raw[0][0], q_rows[0], 0)
         load_half(q_raw[1][0], q_rows[1], 0)
-        load_half(mask_sb[0], mask_rows, 0)
 
         round_keys("vector", 0, 0, ROWS)
         round_keys("vector", 1, 0, K_VECTOR)
         round_keys("scalar", 1, K_VECTOR, ROWS)
-        nc.vector.quantize_mx(
-            out=k_codes[0:ROWS].bitcast(FP8X4), scales=k_scales[0:ROWS], in_=k_bf16[:].rearrange("p c j -> p (c j)")
-        )
-        nc.sync.dma_start(out=k_words[ROWS:P], in_=k_words[0:ROWS])
+        for r in ALL:
+            nc.vector.quantize_mx(
+                out=place_codes(k_made[:], r),
+                scales=place_scales(k_made[:], r),
+                in_=k_bf16[:, r * P : (r + 1) * P, :].rearrange("p c j -> p (c j)"),
+            )
+            if r in (LOW[1], HIGH[1]):
+                nc.sync.dma_start(out=k_words[row_tiles[0], r // 2], in_=k_made[K_START:K_END, r // 2])
+        load_half(mask_sb[0], mask_rows, 0)
+        nc.sync.dma_start(out=k_words[row_tiles[1]], in_=k_made[K_START:K_END])
         nc.sync.dma_start(out=v_raw[:], in_=v[0].rearrange("(p r) e -> p r e", r=PACK))
         load_half(q_raw[0][1], q_rows[0], 1)
         load_half(q_raw[1][1], q_rows[1], 1)
         load_half(mask_sb[1], mask_rows, 1)
 
-        round_queries("vector", 0, 0, 0, P)
-        round_queries("scalar", 0, 0, P, HALF)
-        nc.vector.tensor_tensor(out=kbt[:], in0=kb_sb[:], in1=t_sb[:], op=MULT)
-        quantize(q_mx[0][0], 0, P)
+        for pair in range(2):
+            round_queries("vector", pair, 0, 0, Q_VECTOR)
+            round_queries("scalar", pair, 0, Q_VECTOR, HALF)
+            if pair == 0:
+                nc.vector.tensor_tensor(out=kbt[:], in0=kb_sb[:], in1=t_sb[:], op=MULT)
+            quantize(q_mx[pair][0])
         scores(0, 0, LOW, 0, P)
         scores(0, 0, HIGH, 0, P)
-        quantize(q_mx[0][0], P, HALF)
         scores(0, 0, ALL, P, HALF)
-        round_queries("vector", 1, 0, 0, Q_VECTOR)
-        round_queries("scalar", 1, 0, Q_VECTOR, HALF)
-        for fill in range(SCORE_BANKS[0]):
+        for places in (LOW, HIGH):
             affine(0)
-        quantize(q_mx[1][0], 0, P)
-        quantize(q_mx[1][0], P, HALF)
-        for h in (2, 1):
-            scores(h, 0, LOW)
-            scores(h, 0, HIGH)
+            scores(2, 0, places)
+        affine(0)
+        scores(1, 0, LOW)
+        scores(1, 0, HIGH)
         weigh(0, 0, 0, P)
         weigh(0, 0, P, HALF)
         round_rows("vector", v_mx, v_raw, 0, E)
@@ -234,9 +247,9 @@ def tile_rows_a_lin_kb_mask_kernel(tc, qT, kT, t, v, kb, mask, out):
             scores(1, 1, places)
         values(0, 0, 0, 0)
         values(0, HALF, 2, 0)
-        round_queries("scalar", 1, 1, P, HALF)
+        round_queries("scalar", 1, 1, Q_VECTOR, HALF)
         weigh(1, 0)
-        round_queries("vector", 1, 1, 0, P)
+        round_queries("vector", 1, 1, 0, Q_VECTOR)
         quantize(w_mx[1][0])
         values(1, 0, 1, 0)
         quantize(q_mx[1][1])

@@ -22,7 +22,7 @@ HALF = NQ // 2
 RUN = 4
 SCORE_BANKS = (3, 2)
 Y_BANKS = 3
-K_VECTOR = 44
+K_VECTOR = 84
 Q_VECTOR = 160
 K_START, K_END = 32, 96
 PAIR_WORDS = 2 * P + 2 * P // PACK
@@ -56,7 +56,7 @@ def tile_rows_a_lin_kb_mask_kernel(tc, qT, kT, t, v, kb, mask, out):
         mask_rows = mask.rearrange("(p r) n -> p r n", r=PACK)
         row_tiles = [slice(g * ROWS, (g + 1) * ROWS) for g in range(2)]
 
-        k_raw = [tile("k_raw%d" % i, [K_END, PACK, N // 2], F32) for i in range(2)]
+        k_raw = tile("k_raw", [K_END, PACK, N], F32)
         q_raw = [[tile("q_raw%d_%d" % (pair, half), [P, PACK, HALF], F32) for half in range(2)] for pair in range(2)]
         mask_sb = [tile("mask%d" % half, [P, PACK, HALF], F32) for half in range(2)]
         v_raw = tile("v_raw", [P, PACK, E], F32)
@@ -64,15 +64,20 @@ def tile_rows_a_lin_kb_mask_kernel(tc, qT, kT, t, v, kb, mask, out):
         kb_sb = tile("kb_sb", [P, PACK], F32)
         kbt = tile("kbt", [P, PACK], F32)
         warm = tile("warm", [P, 2], F32)
-        k_made = tile("k_made", [K_END, 2, PAIR_WORDS], I32)
-        k_words = tile("k_words", [P, 2, PAIR_WORDS], I32)
+        k_made = tile("k_made", [K_END, 2 * PAIR_WORDS], I32)
+        k_words = tile("k_words", [P, 2 * PAIR_WORDS], I32)
         k_bf16 = tile("k_bf16", [K_END, N, PACK], BF16)
 
+        def pair_run(words, a):
+            return words[:, a * PAIR_WORDS : (a + 1) * PAIR_WORDS]
+
         def place_codes(words, r):
-            return words[:, r // 2, r % 2 * P : (r % 2 + 1) * P].bitcast(FP8X4)
+            a, b = divmod(r, 2)
+            return pair_run(words, a)[:, b * P : (b + 1) * P].bitcast(FP8X4)
 
         def place_scales(words, r):
-            return words[:, r // 2, 2 * P : PAIR_WORDS].bitcast(U8)[:, r % 2 * P : (r % 2 + 1) * P]
+            a, b = divmod(r, 2)
+            return pair_run(words, a)[:, 2 * P : PAIR_WORDS].bitcast(U8)[:, b * P : (b + 1) * P]
 
         q_mx = [[mx_tiles("q%d_%d" % (pair, half), HALF) for half in range(2)] for pair in range(2)]
         v_mx = mx_tiles("v", E)
@@ -88,10 +93,9 @@ def tile_rows_a_lin_kb_mask_kernel(tc, qT, kT, t, v, kb, mask, out):
             else:
                 nc.scalar.copy(out=dst, in_=src)
 
-        def round_keys(engine, half, s0, s1):
-            base = half * N // 2 // PACK
-            dst = k_bf16[:].rearrange("p (a b s) j -> p a s j b", a=2, b=2)[:, :, base + s0 : base + s1]
-            src = k_raw[half][:].rearrange("p j (s a b) -> p a s j b", a=2, b=2)[:, :, s0:s1]
+        def round_keys(engine, a, s0, s1):
+            dst = k_bf16[:].rearrange("p (a b s) j -> p a s j b", a=2, b=2)[:, a, s0:s1]
+            src = k_raw[:].rearrange("p j (s a b) -> p a s j b", a=2, b=2)[:, a, s0:s1]
             round_copy(engine, dst, src)
 
         def round_rows(engine, mx, raw, c0, c1):
@@ -179,42 +183,45 @@ def tile_rows_a_lin_kb_mask_kernel(tc, qT, kT, t, v, kb, mask, out):
                     in_=y_sb[:, n * blocks : (n + 1) * blocks],
                 )
 
-        for raw in k_raw:
-            nc.vector.memset(raw[0:K_START].bitcast(U32), 0)
-        load_half(k_raw[0][K_START:K_END], k_rows, 0)
+        nc.vector.memset(warm[:, 0:1], 0.0)
+        nc.vector.memset(k_raw[0:K_START].bitcast(U32), 0)
+        nc.sync.dma_start(out=k_raw[K_START:K_END], in_=k_rows)
         nc.scalar.dma_start(out=t_sb[:], in_=t.rearrange("(p r) o -> p (r o)", r=PACK))
         nc.scalar.dma_start(out=kb_sb[:], in_=kb.rearrange("(p r) o -> p (r o)", r=PACK))
-        nc.gpsimd.memset(warm[:, 0:1], 0.0)
-        nc.vector.memset(k_made[:, :, 2 * P : PAIR_WORDS], 0)
+        for a in range(2):
+            nc.vector.memset(pair_run(k_made, a)[:, 2 * P : PAIR_WORDS], 0)
         nc.scalar.activation(out=warm[:, 1:2], in_=warm[:, 0:1], func=IDENT)
-        load_half(k_raw[1][K_START:K_END], k_rows, 1)
         load_half(q_raw[0][0], q_rows[0], 0)
         load_half(q_raw[1][0], q_rows[1], 0)
+        nc.sync.dma_start(out=v_raw[:], in_=v[0].rearrange("(p r) e -> p r e", r=PACK))
 
-        round_keys("vector", 0, 0, ROWS)
-        round_keys("vector", 1, 0, K_VECTOR)
-        round_keys("scalar", 1, K_VECTOR, ROWS)
-        for r in ALL:
-            nc.vector.quantize_mx(
-                out=place_codes(k_made[:], r),
-                scales=place_scales(k_made[:], r),
-                in_=k_bf16[:, r * P : (r + 1) * P, :].rearrange("p c j -> p (c j)"),
-            )
-            if r in (LOW[1], HIGH[1]):
-                nc.sync.dma_start(out=k_words[row_tiles[0], r // 2], in_=k_made[K_START:K_END, r // 2])
+        for a in range(2):
+            round_keys("vector", a, 0, K_VECTOR)
+            round_keys("scalar", a, K_VECTOR, P)
+        for a, places in enumerate((LOW, HIGH)):
+            for r in places:
+                nc.vector.quantize_mx(
+                    out=place_codes(k_made, r),
+                    scales=place_scales(k_made, r),
+                    in_=k_bf16[:, r * P : (r + 1) * P, :].rearrange("p c j -> p (c j)"),
+                )
+            nc.sync.dma_start(out=pair_run(k_words[row_tiles[0]], a), in_=pair_run(k_made[K_START:K_END], a))
         load_half(mask_sb[0], mask_rows, 0)
         nc.sync.dma_start(out=k_words[row_tiles[1]], in_=k_made[K_START:K_END])
-        nc.sync.dma_start(out=v_raw[:], in_=v[0].rearrange("(p r) e -> p r e", r=PACK))
         load_half(q_raw[0][1], q_rows[0], 1)
         load_half(q_raw[1][1], q_rows[1], 1)
         load_half(mask_sb[1], mask_rows, 1)
 
-        for pair in range(2):
-            round_queries("vector", pair, 0, 0, Q_VECTOR)
-            round_queries("scalar", pair, 0, Q_VECTOR, HALF)
-            if pair == 0:
-                nc.vector.tensor_tensor(out=kbt[:], in0=kb_sb[:], in1=t_sb[:], op=MULT)
-            quantize(q_mx[pair][0])
+        round_queries("vector", 0, 0, 0, Q_VECTOR)
+        round_queries("scalar", 0, 0, Q_VECTOR, HALF)
+        nc.vector.tensor_tensor(out=kbt[:], in0=kb_sb[:], in1=t_sb[:], op=MULT)
+        quantize(q_mx[0][0])
+        round_queries("vector", 1, 0, 0, Q_VECTOR)
+        round_queries("scalar", 1, 0, Q_VECTOR, HALF)
+        round_rows("vector", v_mx, v_raw, 0, E)
+        quantize(q_mx[1][0])
+        quantize(v_mx, 0, E)
+
         scores(0, 0, LOW, 0, P)
         scores(0, 0, HIGH, 0, P)
         scores(0, 0, ALL, P, HALF)
@@ -226,9 +233,7 @@ def tile_rows_a_lin_kb_mask_kernel(tc, qT, kT, t, v, kb, mask, out):
         scores(1, 0, HIGH)
         weigh(0, 0, 0, P)
         weigh(0, 0, P, HALF)
-        round_rows("vector", v_mx, v_raw, 0, E)
         quantize(w_mx[0][0])
-        quantize(v_mx, 0, E)
 
         affine(0)
         affine(0)
@@ -236,8 +241,8 @@ def tile_rows_a_lin_kb_mask_kernel(tc, qT, kT, t, v, kb, mask, out):
         for places in (LOW, HIGH):
             affine(1)
             scores(3, 0, places)
-        round_queries("scalar", 0, 1, P, HALF)
-        round_queries("vector", 0, 1, 0, P)
+        round_queries("scalar", 0, 1, Q_VECTOR, HALF)
+        round_queries("vector", 0, 1, 0, Q_VECTOR)
         quantize(w_mx[2][0])
         quantize(q_mx[0][1])
         scores(0, 1, LOW)

@@ -116,23 +116,36 @@ def tile_rows_a_lin_kb_mask_kernel(tc, qT, kT, t, v, kb, mask, out):
         fills = [[], []]
         emptied = [0, 0]
 
-        def scores(h, half, places, c0=0, c1=HALF):
+        def score_calls(h, half, places, c0, c1):
             pair, g = divmod(h, 2)
             bank = score_banks[g][len(fills[g]) % SCORE_BANKS[g]]
             fills[g].append((h, half, places, c0, c1))
             rows = row_tiles[g]
+            calls = []
             for q0 in range(c0, c1, P):
                 for slot, r in enumerate(places):
                     b0 = slot * (c1 - c0) + q0 - c0
-                    nc.tensor.matmul_mx(
-                        out=bank[:, b0 : b0 + P],
-                        lhsT=place_codes(k_words[rows], r),
-                        lhsT_scale=place_scales(k_words[rows], r),
-                        rhs=q_mx[pair][half][1][rows, q0 : q0 + P].bitcast(FP8X4),
-                        rhs_scale=q_mx[pair][half][2][rows, q0 : q0 + P],
-                        start=True,
-                        stop=True,
+                    calls.append(
+                        dict(
+                            out=bank[:, b0 : b0 + P],
+                            lhsT=place_codes(k_words[rows], r),
+                            lhsT_scale=place_scales(k_words[rows], r),
+                            rhs=q_mx[pair][half][1][rows, q0 : q0 + P].bitcast(FP8X4),
+                            rhs_scale=q_mx[pair][half][2][rows, q0 : q0 + P],
+                            start=True,
+                            stop=True,
+                        )
                     )
+            return calls
+
+        def scores(h, half, places, c0=0, c1=HALF):
+            for call in score_calls(h, half, places, c0, c1):
+                nc.tensor.matmul_mx(**call)
+
+        def scores_both(lower, upper):
+            for calls in zip(score_calls(*lower), score_calls(*upper)):
+                for call in calls:
+                    nc.tensor.matmul_mx(**call)
 
         def affine(g):
             n = emptied[g]
@@ -245,11 +258,9 @@ def tile_rows_a_lin_kb_mask_kernel(tc, qT, kT, t, v, kb, mask, out):
         round_queries("vector", 0, 1, 0, Q_VECTOR)
         quantize(w_mx[2][0])
         quantize(q_mx[0][1])
-        scores(0, 1, LOW)
-        scores(0, 1, HIGH)
         for places in (LOW, HIGH):
             affine(1)
-            scores(1, 1, places)
+            scores_both((0, 1, places, 0, HALF), (1, 1, places, 0, HALF))
         values(0, 0, 0, 0)
         values(0, HALF, 2, 0)
         round_queries("scalar", 1, 1, Q_VECTOR, HALF)
@@ -260,16 +271,15 @@ def tile_rows_a_lin_kb_mask_kernel(tc, qT, kT, t, v, kb, mask, out):
         quantize(q_mx[1][1])
         weigh(3, 0)
 
-        for places in (LOW, HIGH):
-            affine(0)
-            scores(2, 1, places)
+        affine(0)
+        affine(0)
         weigh(0, 1)
         quantize(w_mx[3][0])
         affine(1)
-        scores(3, 1, ALL, 0, P)
-        values(1, HALF, 3, 0)
+        scores_both((2, 1, LOW, 0, HALF), (3, 1, ALL, 0, P))
         affine(1)
-        scores(3, 1, ALL, P, HALF)
+        scores_both((2, 1, HIGH, 0, HALF), (3, 1, ALL, P, HALF))
+        values(1, HALF, 3, 0)
         finish(0, 0, (0, 2))
         weigh(1, 1)
         quantize(w_mx[0][1])

@@ -13,6 +13,7 @@ I32 = mybir.dt.int32
 FP8X4 = mybir.dt.float8_e4m3fn_x4
 IDENT = mybir.ActivationFunctionType.Identity
 MULT = mybir.AluOpType.mult
+ADD = mybir.AluOpType.add
 
 P = 128
 PACK = 4
@@ -24,6 +25,7 @@ SCORE_BANKS = (3, 2)
 Y_BANKS = 3
 K_VECTOR = 84
 Q_VECTOR = 160
+Q_VECTOR_LATE = (64, 64)
 K_START, K_END = 32, 96
 PAIR_WORDS = 2 * P + 2 * P // PACK
 LOW, HIGH, ALL = (0, 1), (2, 3), (0, 1, 2, 3)
@@ -147,24 +149,32 @@ def tile_rows_a_lin_kb_mask_kernel(tc, qT, kT, t, v, kb, mask, out):
                 for call in calls:
                     nc.tensor.matmul_mx(**call)
 
-        def affine(g):
+        def affine(g, engine="scalar"):
             n = emptied[g]
             emptied[g] = n + 1
             h, half, places, c0, c1 = fills[g][n]
             for slot, r in enumerate(places):
-                nc.scalar.activation(
-                    out=scaled[h][half][:, r, c0:c1],
-                    in_=score_banks[g][n % SCORE_BANKS[g]][:, slot * (c1 - c0) : (slot + 1) * (c1 - c0)],
-                    func=IDENT,
-                    scale=t_sb[:, r : r + 1],
-                    bias=kbt[:, r : r + 1],
-                )
+                dst = scaled[h][half][:, r, c0:c1]
+                src = score_banks[g][n % SCORE_BANKS[g]][:, slot * (c1 - c0) : (slot + 1) * (c1 - c0)]
+                scale, bias = t_sb[:, r : r + 1], kbt[:, r : r + 1]
+                if engine == "vector":
+                    nc.vector.tensor_scalar(out=dst, in0=src, scalar1=scale, scalar2=bias, op0=MULT, op1=ADD)
+                else:
+                    nc.scalar.activation(out=dst, in_=src, func=IDENT, scale=scale, bias=bias)
 
         def weigh(h, half, c0=0, c1=HALF):
             nc.vector.tensor_tensor(
                 out=w_mx[h][half][0][:, c0:c1].rearrange("p (c i) r -> p c r i", i=RUN),
                 in0=scaled[h][half][:, :, c0:c1].rearrange("p r (c i) -> p c r i", i=RUN),
                 in1=mask_sb[half][:, :, c0:c1].rearrange("p r (c i) -> p c r i", i=RUN),
+                op=MULT,
+            )
+
+        def weigh_dealt(h, half):
+            nc.vector.tensor_tensor(
+                out=w_mx[h][half][0][:].rearrange("p (b m) r -> p m r b", b=2),
+                in0=scaled[h][half][:].rearrange("p r (m b) -> p m r b", b=2),
+                in1=mask_sb[half][:].rearrange("p r (m b) -> p m r b", b=2),
                 op=MULT,
             )
 
@@ -180,7 +190,7 @@ def tile_rows_a_lin_kb_mask_kernel(tc, qT, kT, t, v, kb, mask, out):
                     stop=True,
                 )
 
-        def finish(bank, half, heads, c0=0, c1=HALF):
+        def finish(bank, half, heads, c0=0, c1=HALF, dealt=()):
             blocks = (c1 - c0) // P
             y_sb = tile("y_sb%d_%d_%d" % (heads[0], half, c0), [P, len(heads) * blocks, E], F32)
             nc.scalar.activation(
@@ -192,7 +202,7 @@ def tile_rows_a_lin_kb_mask_kernel(tc, qT, kT, t, v, kb, mask, out):
             q0 = half * HALF + c0
             for n, h in enumerate(heads):
                 nc.sync.dma_start(
-                    out=out[h, q0 : q0 + c1 - c0, :].rearrange("(b m) e -> m b e", m=P),
+                    out=out[h, q0 : q0 + c1 - c0, :].rearrange("(m b) e -> m b e" if h in dealt else "(b m) e -> m b e", m=P),
                     in_=y_sb[:, n * blocks : (n + 1) * blocks],
                 )
 
@@ -206,7 +216,7 @@ def tile_rows_a_lin_kb_mask_kernel(tc, qT, kT, t, v, kb, mask, out):
         nc.scalar.activation(out=warm[:, 1:2], in_=warm[:, 0:1], func=IDENT)
         load_half(q_raw[0][0], q_rows[0], 0)
         load_half(q_raw[1][0], q_rows[1], 0)
-        nc.sync.dma_start(out=v_raw[:], in_=v[0].rearrange("(p r) e -> p r e", r=PACK))
+        nc.sync.dma_start(out=mask_sb[0][:, 0:1], in_=mask_rows[:, 0:1, 0:HALF])
 
         for a in range(2):
             round_keys("vector", a, 0, K_VECTOR)
@@ -219,8 +229,10 @@ def tile_rows_a_lin_kb_mask_kernel(tc, qT, kT, t, v, kb, mask, out):
                     in_=k_bf16[:, r * P : (r + 1) * P, :].rearrange("p c j -> p (c j)"),
                 )
             nc.sync.dma_start(out=pair_run(k_words[row_tiles[0]], a), in_=pair_run(k_made[K_START:K_END], a))
-        load_half(mask_sb[0], mask_rows, 0)
-        nc.sync.dma_start(out=k_words[row_tiles[1]], in_=k_made[K_START:K_END])
+        nc.sync.dma_start(out=pair_run(k_words[row_tiles[1]], 0), in_=pair_run(k_made[K_START:K_END], 0))
+        nc.sync.dma_start(out=mask_sb[0][:, 1:4], in_=mask_rows[:, 1:4, 0:HALF])
+        nc.sync.dma_start(out=pair_run(k_words[row_tiles[1]], 1), in_=pair_run(k_made[K_START:K_END], 1))
+        nc.sync.dma_start(out=v_raw[:], in_=v[0].rearrange("(p r) e -> p r e", r=PACK))
         load_half(q_raw[0][1], q_rows[0], 1)
         load_half(q_raw[1][1], q_rows[1], 1)
         load_half(mask_sb[1], mask_rows, 1)
@@ -231,75 +243,72 @@ def tile_rows_a_lin_kb_mask_kernel(tc, qT, kT, t, v, kb, mask, out):
         quantize(q_mx[0][0])
         round_queries("vector", 1, 0, 0, Q_VECTOR)
         round_queries("scalar", 1, 0, Q_VECTOR, HALF)
-        round_rows("vector", v_mx, v_raw, 0, E)
         quantize(q_mx[1][0])
-        quantize(v_mx, 0, E)
 
-        scores(0, 0, LOW, 0, P)
-        scores(0, 0, HIGH, 0, P)
-        scores(0, 0, ALL, P, HALF)
-        for places in (LOW, HIGH):
-            affine(0)
-            scores(2, 0, places)
+        scores(0, 0, LOW)
+        scores(0, 0, HIGH)
+        scores_both((2, 0, LOW, 0, HALF), (1, 0, LOW, 0, HALF))
         affine(0)
-        scores(1, 0, LOW)
+        scores(2, 0, HIGH)
         scores(1, 0, HIGH)
-        weigh(0, 0, 0, P)
-        weigh(0, 0, P, HALF)
-        quantize(w_mx[0][0])
-
+        affine(0, "vector")
         affine(0)
         affine(0)
-        weigh(2, 0)
-        for places in (LOW, HIGH):
-            affine(1)
-            scores(3, 0, places)
-        round_queries("scalar", 0, 1, Q_VECTOR, HALF)
-        round_queries("vector", 0, 1, 0, Q_VECTOR)
-        quantize(w_mx[2][0])
+        affine(1)
+        scores(3, 0, LOW)
+        affine(1)
+        scores(3, 0, HIGH)
+        weigh_dealt(0, 0)
+        round_rows("vector", v_mx, v_raw, 0, E)
+        weigh_dealt(2, 0)
+        round_queries("scalar", 0, 1, Q_VECTOR_LATE[0], HALF)
+        affine(1)
+        round_queries("vector", 0, 1, 0, Q_VECTOR_LATE[0])
+        affine(1)
+        weigh_dealt(1, 0)
         quantize(q_mx[0][1])
         for places in (LOW, HIGH):
-            affine(1)
             scores_both((0, 1, places, 0, HALF), (1, 1, places, 0, HALF))
+        round_queries("scalar", 1, 1, Q_VECTOR_LATE[1], HALF)
+        quantize(v_mx, 0, E)
+        quantize(w_mx[0][0])
+        quantize(w_mx[2][0])
         values(0, 0, 0, 0)
         values(0, HALF, 2, 0)
-        round_queries("scalar", 1, 1, Q_VECTOR, HALF)
-        weigh(1, 0)
-        round_queries("vector", 1, 1, 0, Q_VECTOR)
+        round_queries("vector", 1, 1, 0, Q_VECTOR_LATE[1])
         quantize(w_mx[1][0])
-        values(1, 0, 1, 0)
+        weigh_dealt(3, 0)
         quantize(q_mx[1][1])
-        weigh(3, 0)
-
         affine(0)
+        scores(2, 1, LOW)
         affine(0)
-        weigh(0, 1)
         quantize(w_mx[3][0])
+        weigh_dealt(0, 1)
         affine(1)
-        scores_both((2, 1, LOW, 0, HALF), (3, 1, ALL, 0, P))
+        scores_both((2, 1, HIGH, 0, HALF), (3, 1, ALL, 0, P))
         affine(1)
-        scores_both((2, 1, HIGH, 0, HALF), (3, 1, ALL, P, HALF))
+        scores(3, 1, ALL, P, HALF)
+        values(1, 0, 1, 0)
         values(1, HALF, 3, 0)
-        finish(0, 0, (0, 2))
-        weigh(1, 1)
+        weigh_dealt(1, 1)
         quantize(w_mx[0][1])
         values(2, 0, 0, 1)
         affine(0)
         affine(0)
-        finish(1, 0, (1, 3))
-        weigh(2, 1)
+        finish(0, 0, (0, 2), dealt=(0, 2))
+        weigh_dealt(2, 1)
         quantize(w_mx[1][1])
-        values(0, 0, 1, 1)
+        values(2, HALF, 1, 1)
         affine(1)
         affine(1)
-        finish(2, 1, (0,))
-        finish(0, 1, (1,))
+        finish(1, 0, (1, 3), dealt=(1, 3))
+        finish(2, 1, (0, 1), dealt=(0, 1))
         weigh(3, 1, 0, P)
         quantize(w_mx[2][1])
-        values(1, 0, 2, 1)
+        values(0, 0, 2, 1)
         weigh(3, 1, P, HALF)
-        finish(1, 1, (2,))
-        last_blocks = ((2, 0), (0, P))
+        finish(0, 1, (2,), dealt=(2,))
+        last_blocks = ((1, 0), (2, P))
         for bank, c0 in last_blocks:
             quantize(w_mx[3][1], c0, c0 + P)
             values(bank, 0, 3, 1, c0, c0 + P)

@@ -24,10 +24,12 @@ RUN = 4
 SCORE_BANKS = (3, 2)
 Y_BANKS = 3
 K_VECTOR = 84
-Q_VECTOR = 160
-Q_VECTOR_LATE = (64, 64)
+Q_VECTOR = 128
+Q_SECOND = 176
+Q_VECTOR_LATE = (0, 32)
 K_START, K_END = 32, 96
-PAIR_WORDS = 2 * P + 2 * P // PACK
+PLACE_WORDS = P + P // PACK
+K_FILL = 64
 LOW, HIGH, ALL = (0, 1), (2, 3), (0, 1, 2, 3)
 
 
@@ -66,20 +68,26 @@ def tile_rows_a_lin_kb_mask_kernel(tc, qT, kT, t, v, kb, mask, out):
         kb_sb = tile("kb_sb", [P, PACK], F32)
         kbt = tile("kbt", [P, PACK], F32)
         warm = tile("warm", [P, 2], F32)
-        k_made = tile("k_made", [K_END, 2 * PAIR_WORDS], I32)
-        k_words = tile("k_words", [P, 2 * PAIR_WORDS], I32)
+        k_made = tile("k_made", [K_END, PACK * PLACE_WORDS], I32)
+        k_words = tile("k_words", [P, PACK * PLACE_WORDS], I32)
         k_bf16 = tile("k_bf16", [K_END, N, PACK], BF16)
 
-        def pair_run(words, a):
-            return words[:, a * PAIR_WORDS : (a + 1) * PAIR_WORDS]
-
         def place_codes(words, r):
-            a, b = divmod(r, 2)
-            return pair_run(words, a)[:, b * P : (b + 1) * P].bitcast(FP8X4)
+            return words[:, r * PLACE_WORDS : r * PLACE_WORDS + P].bitcast(FP8X4)
 
         def place_scales(words, r):
-            a, b = divmod(r, 2)
-            return pair_run(words, a)[:, 2 * P : PAIR_WORDS].bitcast(U8)[:, b * P : (b + 1) * P]
+            return words[:, r * PLACE_WORDS + P : (r + 1) * PLACE_WORDS].bitcast(U8)
+
+        def copy_keys(g, places):
+            run = slice(places[0] * PLACE_WORDS, (places[-1] + 1) * PLACE_WORDS)
+            nc.sync.dma_start(out=k_words[row_tiles[g], run], in_=k_made[K_START:K_END, run])
+
+        def quantize_keys(r):
+            nc.vector.quantize_mx(
+                out=place_codes(k_made, r),
+                scales=place_scales(k_made, r),
+                in_=k_bf16[:, r * P : (r + 1) * P, :].rearrange("p c j -> p (c j)"),
+            )
 
         q_mx = [[mx_tiles("q%d_%d" % (pair, half), HALF) for half in range(2)] for pair in range(2)]
         v_mx = mx_tiles("v", E)
@@ -124,8 +132,8 @@ def tile_rows_a_lin_kb_mask_kernel(tc, qT, kT, t, v, kb, mask, out):
             fills[g].append((h, half, places, c0, c1))
             rows = row_tiles[g]
             calls = []
-            for q0 in range(c0, c1, P):
-                for slot, r in enumerate(places):
+            for slot, r in enumerate(places):
+                for q0 in range(c0, c1, P):
                     b0 = slot * (c1 - c0) + q0 - c0
                     calls.append(
                         dict(
@@ -211,59 +219,57 @@ def tile_rows_a_lin_kb_mask_kernel(tc, qT, kT, t, v, kb, mask, out):
         nc.sync.dma_start(out=k_raw[K_START:K_END], in_=k_rows)
         nc.scalar.dma_start(out=t_sb[:], in_=t.rearrange("(p r) o -> p (r o)", r=PACK))
         nc.scalar.dma_start(out=kb_sb[:], in_=kb.rearrange("(p r) o -> p (r o)", r=PACK))
-        for a in range(2):
-            nc.vector.memset(pair_run(k_made, a)[:, 2 * P : PAIR_WORDS], 0)
+        nc.vector.memset(k_made[:].rearrange("p (r w) -> p r w", r=PACK)[:, :, P:], 0)
         nc.scalar.activation(out=warm[:, 1:2], in_=warm[:, 0:1], func=IDENT)
         load_half(q_raw[0][0], q_rows[0], 0)
         load_half(q_raw[1][0], q_rows[1], 0)
-        nc.sync.dma_start(out=mask_sb[0][:, 0:1], in_=mask_rows[:, 0:1, 0:HALF])
 
-        for a in range(2):
-            round_keys("vector", a, 0, K_VECTOR)
-            round_keys("scalar", a, K_VECTOR, P)
-        for a, places in enumerate((LOW, HIGH)):
-            for r in places:
-                nc.vector.quantize_mx(
-                    out=place_codes(k_made, r),
-                    scales=place_scales(k_made, r),
-                    in_=k_bf16[:, r * P : (r + 1) * P, :].rearrange("p c j -> p (c j)"),
-                )
-            nc.sync.dma_start(out=pair_run(k_words[row_tiles[0]], a), in_=pair_run(k_made[K_START:K_END], a))
-        nc.sync.dma_start(out=pair_run(k_words[row_tiles[1]], 0), in_=pair_run(k_made[K_START:K_END], 0))
-        nc.sync.dma_start(out=mask_sb[0][:, 1:4], in_=mask_rows[:, 1:4, 0:HALF])
-        nc.sync.dma_start(out=pair_run(k_words[row_tiles[1]], 1), in_=pair_run(k_made[K_START:K_END], 1))
+        round_keys("vector", 0, 0, K_VECTOR)
+        round_keys("scalar", 0, K_VECTOR, P)
+        round_keys("vector", 1, 0, K_FILL)
+        round_keys("scalar", 1, K_FILL, P)
+        for r in LOW:
+            quantize_keys(r)
+            copy_keys(0, (r,))
+        copy_keys(1, LOW)
+        nc.vector.tensor_tensor(out=kbt[:], in0=kb_sb[:], in1=t_sb[:], op=MULT)
+        for r in HIGH:
+            quantize_keys(r)
+        round_queries("vector", 0, 0, 0, Q_VECTOR)
+        copy_keys(0, HIGH)
+        load_half(mask_sb[0], mask_rows, 0)
+        copy_keys(1, HIGH)
         nc.sync.dma_start(out=v_raw[:], in_=v[0].rearrange("(p r) e -> p r e", r=PACK))
         load_half(q_raw[0][1], q_rows[0], 1)
         load_half(q_raw[1][1], q_rows[1], 1)
         load_half(mask_sb[1], mask_rows, 1)
 
-        round_queries("vector", 0, 0, 0, Q_VECTOR)
         round_queries("scalar", 0, 0, Q_VECTOR, HALF)
-        nc.vector.tensor_tensor(out=kbt[:], in0=kb_sb[:], in1=t_sb[:], op=MULT)
         quantize(q_mx[0][0])
-        round_queries("vector", 1, 0, 0, Q_VECTOR)
-        round_queries("scalar", 1, 0, Q_VECTOR, HALF)
+        round_queries("vector", 1, 0, 0, Q_SECOND)
+        round_queries("scalar", 1, 0, Q_SECOND, HALF)
         quantize(q_mx[1][0])
 
         scores(0, 0, LOW)
-        scores(0, 0, HIGH)
-        scores_both((2, 0, LOW, 0, HALF), (1, 0, LOW, 0, HALF))
+        scores(1, 0, LOW)
+        for r in HIGH:
+            scores(0, 0, (r,))
         affine(0)
+        scores_both((2, 0, LOW, 0, HALF), (3, 0, LOW, 0, HALF))
+        affine(1)
+        affine(0, "vector")
         scores(2, 0, HIGH)
         scores(1, 0, HIGH)
         affine(0, "vector")
         affine(0)
         affine(0)
         affine(1)
-        scores(3, 0, LOW)
-        affine(1)
         scores(3, 0, HIGH)
+        affine(1)
         weigh_dealt(0, 0)
         round_rows("vector", v_mx, v_raw, 0, E)
         weigh_dealt(2, 0)
         round_queries("scalar", 0, 1, Q_VECTOR_LATE[0], HALF)
-        affine(1)
-        round_queries("vector", 0, 1, 0, Q_VECTOR_LATE[0])
         affine(1)
         weigh_dealt(1, 0)
         quantize(q_mx[0][1])

@@ -21,15 +21,17 @@ ROWS = D // PACK
 BANK = 512
 HALF = NQ // 2
 RUN = 4
-SCORE_BANKS = (3, 2)
-Y_BANKS = 3
+SCORE_BANKS = (4, 2)
+Y_BANKS = 2
 K_VECTOR = 84
 Q_VECTOR = 128
 Q_SECOND = 176
-Q_VECTOR_LATE = (0, 32)
 K_START, K_END = 32, 96
 PLACE_WORDS = P + P // PACK
 K_FILL = 64
+G_SHARE = 120
+G_FIRST = 152
+V_LAST = 160
 LOW, HIGH, ALL = (0, 1), (2, 3), (0, 1, 2, 3)
 
 
@@ -62,7 +64,10 @@ def tile_rows_a_lin_kb_mask_kernel(tc, qT, kT, t, v, kb, mask, out):
 
         k_raw = tile("k_raw", [K_END, PACK, N], F32)
         q_raw = [[tile("q_raw%d_%d" % (pair, half), [P, PACK, HALF], F32) for half in range(2)] for pair in range(2)]
-        mask_sb = [tile("mask%d" % half, [P, PACK, HALF], F32) for half in range(2)]
+        mask_last = tile("mask1", [P, PACK, HALF], F32)
+        mask_half = [tile("mask0", [P, PACK, HALF], F32), mask_last]
+        mask_sb = [[mask_half[half][:, 2 * a : 2 * a + 2] for a in range(2)] for half in range(2)]
+        mask_t = [[tile("maskt%d_%d" % (half, r), [P, HALF], F32) for r in range(PACK)] for half in range(2)]
         v_raw = tile("v_raw", [P, PACK, E], F32)
         t_sb = tile("t_sb", [P, PACK], F32)
         kb_sb = tile("kb_sb", [P, PACK], F32)
@@ -89,10 +94,25 @@ def tile_rows_a_lin_kb_mask_kernel(tc, qT, kT, t, v, kb, mask, out):
                 in_=k_bf16[:, r * P : (r + 1) * P, :].rearrange("p c j -> p (c j)"),
             )
 
-        q_mx = [[mx_tiles("q%d_%d" % (pair, half), HALF) for half in range(2)] for pair in range(2)]
+        def window(mx, c0, columns):
+            return tuple(part[:, c0 : c0 + columns] for part in mx)
+
+        widths = (2 * HALF, HALF, 2 * HALF, HALF, HALF)
+        chain = tile("chain", [P, sum(widths) - 4 * G_SHARE, PACK], BF16)
+        calls = []
+        for n, width in enumerate(widths):
+            c0 = sum(widths[:n]) - n * G_SHARE
+            calls.append(
+                (chain[:, c0 : c0 + width], tile("codes%d" % n, [P, width], U32), tile("scales%d" % n, [P, width], U8))
+            )
+        first_two, third, fourth = calls[0:3]
+        q_mx = [[mx_tiles("q0_0", HALF), mx_tiles("q0_1", HALF)], [mx_tiles("q1_0", HALF), window(fourth, HALF, HALF)]]
         v_mx = mx_tiles("v", E)
-        scaled = [[tile("scaled%d_%d" % (h, half), [P, PACK, HALF], F32) for half in range(2)] for h in range(H)]
-        w_mx = [[mx_tiles("w%d_%d" % (h, half), HALF) for half in range(2)] for h in range(H)]
+        scaled = [tile("scaled%d" % half, [P, PACK, HALF], F32) for half in range(2)]
+        rows_bf = [[tile("rows%d_%d" % (h, half), [P, PACK, HALF], BF16) for half in range(2)] for h in range(H)]
+        w_first = [window(first_two, 0, HALF), third, window(first_two, HALF, HALF), window(fourth, 0, HALF)]
+        w_second = [calls[3], calls[4], mx_tiles("w2_1", HALF), mx_tiles("w3_1", HALF)]
+        w_mx = [[w_first[h], w_second[h]] for h in range(H)]
 
         def load_half(dst, rows, half):
             nc.sync.dma_start(out=dst[:], in_=rows[:, :, half * HALF : (half + 1) * HALF])
@@ -153,8 +173,9 @@ def tile_rows_a_lin_kb_mask_kernel(tc, qT, kT, t, v, kb, mask, out):
                 nc.tensor.matmul_mx(**call)
 
         def scores_both(lower, upper):
-            for calls in zip(score_calls(*lower), score_calls(*upper)):
-                for call in calls:
+            first, second = score_calls(*lower), score_calls(*upper)
+            for n in range(max(len(first), len(second))):
+                for call in first[n : n + 1] + second[n : n + 1]:
                     nc.tensor.matmul_mx(**call)
 
         def affine(g, engine="scalar"):
@@ -162,7 +183,7 @@ def tile_rows_a_lin_kb_mask_kernel(tc, qT, kT, t, v, kb, mask, out):
             emptied[g] = n + 1
             h, half, places, c0, c1 = fills[g][n]
             for slot, r in enumerate(places):
-                dst = scaled[h][half][:, r, c0:c1]
+                dst = scaled[half][:, r, c0:c1]
                 src = score_banks[g][n % SCORE_BANKS[g]][:, slot * (c1 - c0) : (slot + 1) * (c1 - c0)]
                 scale, bias = t_sb[:, r : r + 1], kbt[:, r : r + 1]
                 if engine == "vector":
@@ -170,21 +191,59 @@ def tile_rows_a_lin_kb_mask_kernel(tc, qT, kT, t, v, kb, mask, out):
                 else:
                     nc.scalar.activation(out=dst, in_=src, func=IDENT, scale=scale, bias=bias)
 
-        def weigh(h, half, c0=0, c1=HALF):
+        def weigh(h, half, c0, c1):
             nc.vector.tensor_tensor(
                 out=w_mx[h][half][0][:, c0:c1].rearrange("p (c i) r -> p c r i", i=RUN),
-                in0=scaled[h][half][:, :, c0:c1].rearrange("p r (c i) -> p c r i", i=RUN),
-                in1=mask_sb[half][:, :, c0:c1].rearrange("p r (c i) -> p c r i", i=RUN),
+                in0=scaled[half][:, :, c0:c1].rearrange("p r (c i) -> p c r i", i=RUN),
+                in1=mask_half[half][:, :, c0:c1].rearrange("p r (c i) -> p c r i", i=RUN),
                 op=MULT,
             )
 
         def weigh_dealt(h, half):
             nc.vector.tensor_tensor(
                 out=w_mx[h][half][0][:].rearrange("p (b m) r -> p m r b", b=2),
-                in0=scaled[h][half][:].rearrange("p r (m b) -> p m r b", b=2),
-                in1=mask_sb[half][:].rearrange("p r (m b) -> p m r b", b=2),
+                in0=scaled[half][:].rearrange("p r (m b) -> p m r b", b=2),
+                in1=mask_half[half][:].rearrange("p r (m b) -> p m r b", b=2),
                 op=MULT,
             )
+
+        def weigh_bank(g):
+            n = emptied[g]
+            emptied[g] = n + 1
+            h, half, places, c0, c1 = fills[g][n]
+            for slot, r in enumerate(places):
+                nc.vector.scalar_tensor_tensor(
+                    out=rows_bf[h][half][:, r, :].rearrange("p (b m) -> p m b", b=2),
+                    in0=score_banks[g][n % SCORE_BANKS[g]][:, slot * HALF : (slot + 1) * HALF].rearrange(
+                        "p (m b) -> p m b", b=2
+                    ),
+                    scalar=kb_sb[:, r : r + 1],
+                    in1=mask_t[half][r][:].rearrange("p (m b) -> p m b", b=2),
+                    op0=ADD,
+                    op1=MULT,
+                )
+
+        def scale_mask(engine, half, r):
+            src = mask_sb[half][r // 2][:, r % 2, :]
+            if engine == "vector":
+                nc.vector.tensor_scalar(
+                    out=mask_t[half][r][:], in0=src, scalar1=t_sb[:, r : r + 1], scalar2=None, op0=MULT
+                )
+            else:
+                nc.scalar.activation(out=mask_t[half][r][:], in_=src, func=IDENT, scale=t_sb[:, r : r + 1])
+
+        def pack(engine, h, half, c0, c1):
+            if engine == "gpsimd":
+                nc.gpsimd.tensor_scalar(
+                    out=w_mx[h][half][0][:, c0:c1, :],
+                    in0=rows_bf[h][half][:, :, c0:c1].rearrange("p r c -> p c r"),
+                    scalar1=1.0,
+                    scalar2=0.0,
+                    op0=MULT,
+                    op1=ADD,
+                )
+            else:
+                round_rows(engine, w_mx[h][half], rows_bf[h][half], c0, c1)
 
         def values(bank, b0, h, half, c0=0, c1=HALF):
             for q0 in range(c0, c1, P):
@@ -231,18 +290,18 @@ def tile_rows_a_lin_kb_mask_kernel(tc, qT, kT, t, v, kb, mask, out):
         for r in LOW:
             quantize_keys(r)
             copy_keys(0, (r,))
-        copy_keys(1, LOW)
+        load_half(mask_sb[0][0], mask_rows[:, 0:2], 0)
         nc.vector.tensor_tensor(out=kbt[:], in0=kb_sb[:], in1=t_sb[:], op=MULT)
         for r in HIGH:
             quantize_keys(r)
         round_queries("vector", 0, 0, 0, Q_VECTOR)
         copy_keys(0, HIGH)
-        load_half(mask_sb[0], mask_rows, 0)
-        copy_keys(1, HIGH)
-        nc.sync.dma_start(out=v_raw[:], in_=v[0].rearrange("(p r) e -> p r e", r=PACK))
+        load_half(mask_sb[0][1], mask_rows[:, 2:4], 0)
+        copy_keys(1, ALL)
         load_half(q_raw[0][1], q_rows[0], 1)
+        nc.sync.dma_start(out=v_raw[:], in_=v[0].rearrange("(p r) e -> p r e", r=PACK))
+        load_half(mask_last, mask_rows, 1)
         load_half(q_raw[1][1], q_rows[1], 1)
-        load_half(mask_sb[1], mask_rows, 1)
 
         round_queries("scalar", 0, 0, Q_VECTOR, HALF)
         quantize(q_mx[0][0])
@@ -251,72 +310,82 @@ def tile_rows_a_lin_kb_mask_kernel(tc, qT, kT, t, v, kb, mask, out):
         quantize(q_mx[1][0])
 
         scores(0, 0, LOW)
-        scores(1, 0, LOW)
-        for r in HIGH:
-            scores(0, 0, (r,))
-        affine(0)
-        scores_both((2, 0, LOW, 0, HALF), (3, 0, LOW, 0, HALF))
-        affine(1)
-        affine(0, "vector")
+        scores(2, 0, LOW)
         scores(2, 0, HIGH)
+        scores(0, 0, HIGH)
+        for r in LOW:
+            scale_mask("vector", 0, r)
+        weigh_bank(0)
+        scores(1, 0, LOW)
         scores(1, 0, HIGH)
-        affine(0, "vector")
         affine(0)
         affine(0)
-        affine(1)
-        scores(3, 0, HIGH)
-        affine(1)
-        weigh_dealt(0, 0)
-        round_rows("vector", v_mx, v_raw, 0, E)
+        for r in HIGH:
+            scale_mask("vector", 0, r)
+        weigh_bank(0)
         weigh_dealt(2, 0)
-        round_queries("scalar", 0, 1, Q_VECTOR_LATE[0], HALF)
-        affine(1)
-        weigh_dealt(1, 0)
-        quantize(q_mx[0][1])
+        pack("gpsimd", 0, 0, 0, G_FIRST)
+        pack("scalar", 0, 0, G_FIRST, HALF)
+        round_queries("scalar", 0, 1, 0, HALF)
         for places in (LOW, HIGH):
-            scores_both((0, 1, places, 0, HALF), (1, 1, places, 0, HALF))
-        round_queries("scalar", 1, 1, Q_VECTOR_LATE[1], HALF)
+            weigh_bank(1)
+            scores(3, 0, places)
+        quantize(first_two, 0, 2 * HALF)
+        quantize(q_mx[0][1])
+        scores(0, 1, LOW)
+        scores(0, 1, HIGH)
+        round_rows("scalar", v_mx, v_raw, 0, E)
+        pack("gpsimd", 1, 0, 0, G_SHARE)
+        pack("scalar", 1, 0, G_SHARE, HALF)
+        for places in (LOW, HIGH):
+            weigh_bank(1)
+            scores(1, 1, places)
         quantize(v_mx, 0, E)
-        quantize(w_mx[0][0])
-        quantize(w_mx[2][0])
+        for r in range(1):
+            scale_mask("vector", 1, r)
+        for r in range(1, PACK):
+            scale_mask("scalar", 1, r)
+        quantize(w_mx[1][0])
         values(0, 0, 0, 0)
         values(0, HALF, 2, 0)
-        round_queries("vector", 1, 1, 0, Q_VECTOR_LATE[1])
-        quantize(w_mx[1][0])
-        weigh_dealt(3, 0)
-        quantize(q_mx[1][1])
-        affine(0)
-        scores(2, 1, LOW)
-        affine(0)
-        quantize(w_mx[3][0])
-        weigh_dealt(0, 1)
-        affine(1)
-        scores_both((2, 1, HIGH, 0, HALF), (3, 1, ALL, 0, P))
-        affine(1)
-        scores(3, 1, ALL, P, HALF)
         values(1, 0, 1, 0)
-        values(1, HALF, 3, 0)
-        weigh_dealt(1, 1)
-        quantize(w_mx[0][1])
-        values(2, 0, 0, 1)
-        affine(0)
-        affine(0)
+        round_queries("scalar", 1, 1, 0, HALF)
+        pack("gpsimd", 3, 0, 0, G_SHARE)
+        pack("scalar", 3, 0, G_SHARE, HALF)
         finish(0, 0, (0, 2), dealt=(0, 2))
-        weigh_dealt(2, 1)
+        weigh_bank(0)
+        weigh_bank(0)
+        quantize(fourth, 0, 2 * HALF)
+        pack("gpsimd", 0, 1, 0, G_SHARE)
+        pack("scalar", 0, 1, G_SHARE, HALF)
+        scores(2, 1, ALL, 0, P)
+        weigh_bank(1)
+        scores_both((2, 1, ALL, P, HALF), (3, 1, LOW, 0, HALF))
+        values(1, HALF, 3, 0)
+        weigh_bank(1)
+        scores(3, 1, HIGH)
+        quantize(w_mx[0][1])
+        values(0, 0, 0, 1)
+        affine(0)
+        pack("gpsimd", 1, 1, 0, G_SHARE)
+        pack("scalar", 1, 1, G_SHARE, HALF)
+        affine(0)
+        weigh_bank(1)
+        weigh_bank(1)
         quantize(w_mx[1][1])
-        values(2, HALF, 1, 1)
-        affine(1)
-        affine(1)
+        values(0, HALF, 1, 1)
+        pack("vector", 3, 1, 0, V_LAST)
+        pack("scalar", 3, 1, V_LAST, HALF)
         finish(1, 0, (1, 3), dealt=(1, 3))
-        finish(2, 1, (0, 1), dealt=(0, 1))
-        weigh(3, 1, 0, P)
-        quantize(w_mx[2][1])
-        values(0, 0, 2, 1)
-        weigh(3, 1, P, HALF)
-        finish(0, 1, (2,), dealt=(2,))
-        last_blocks = ((1, 0), (2, P))
+        finish(0, 1, (0, 1), dealt=(0, 1))
+        weigh(2, 1, 0, P)
+        quantize(w_mx[3][1])
+        values(1, 0, 3, 1)
+        weigh(2, 1, P, HALF)
+        finish(1, 1, (3,), dealt=(3,))
+        last_blocks = ((0, 0), (1, P))
         for bank, c0 in last_blocks:
-            quantize(w_mx[3][1], c0, c0 + P)
-            values(bank, 0, 3, 1, c0, c0 + P)
+            quantize(w_mx[2][1], c0, c0 + P)
+            values(bank, 0, 2, 1, c0, c0 + P)
         for bank, c0 in last_blocks:
-            finish(bank, 1, (3,), c0, c0 + P)
+            finish(bank, 1, (2,), c0, c0 + P)

@@ -21,7 +21,7 @@ ROWS = D // PACK
 BANK = 512
 HALF = NQ // 2
 RUN = 4
-SCORE_BANKS = (4, 2)
+SCORE_BANKS = (3, 3)
 Y_BANKS = 2
 K_VECTOR = 84
 Q_VECTOR = 128
@@ -29,9 +29,11 @@ Q_SECOND = 176
 K_START, K_END = 32, 96
 PLACE_WORDS = P + P // PACK
 K_FILL = 64
-G_SHARE = 120
-G_FIRST = 152
-V_LAST = 160
+G_SHARE = 112
+G_WEIGHS = 256
+G_THIRD = 56
+Q_LAST = 160
+V_LAST = 144
 LOW, HIGH, ALL = (0, 1), (2, 3), (0, 1, 2, 3)
 
 
@@ -98,10 +100,10 @@ def tile_rows_a_lin_kb_mask_kernel(tc, qT, kT, t, v, kb, mask, out):
             return tuple(part[:, c0 : c0 + columns] for part in mx)
 
         widths = (2 * HALF, HALF, 2 * HALF, HALF, HALF)
-        chain = tile("chain", [P, sum(widths) - 4 * G_SHARE, PACK], BF16)
+        chain = tile("chain", [P, sum(widths) - 3 * G_SHARE, PACK], BF16)
         calls = []
         for n, width in enumerate(widths):
-            c0 = sum(widths[:n]) - n * G_SHARE
+            c0 = sum(widths[:n]) - max(n - 1, 0) * G_SHARE
             calls.append(
                 (chain[:, c0 : c0 + width], tile("codes%d" % n, [P, width], U32), tile("scales%d" % n, [P, width], U8))
             )
@@ -191,19 +193,11 @@ def tile_rows_a_lin_kb_mask_kernel(tc, qT, kT, t, v, kb, mask, out):
                 else:
                     nc.scalar.activation(out=dst, in_=src, func=IDENT, scale=scale, bias=bias)
 
-        def weigh(h, half, c0, c1):
-            nc.vector.tensor_tensor(
+        def weigh(h, half, c0, c1, engine=nc.vector):
+            engine.tensor_tensor(
                 out=w_mx[h][half][0][:, c0:c1].rearrange("p (c i) r -> p c r i", i=RUN),
                 in0=scaled[half][:, :, c0:c1].rearrange("p r (c i) -> p c r i", i=RUN),
                 in1=mask_half[half][:, :, c0:c1].rearrange("p r (c i) -> p c r i", i=RUN),
-                op=MULT,
-            )
-
-        def weigh_dealt(h, half):
-            nc.vector.tensor_tensor(
-                out=w_mx[h][half][0][:].rearrange("p (b m) r -> p m r b", b=2),
-                in0=scaled[half][:].rearrange("p r (m b) -> p m r b", b=2),
-                in1=mask_half[half][:].rearrange("p r (m b) -> p m r b", b=2),
                 op=MULT,
             )
 
@@ -298,10 +292,10 @@ def tile_rows_a_lin_kb_mask_kernel(tc, qT, kT, t, v, kb, mask, out):
         copy_keys(0, HIGH)
         load_half(mask_sb[0][1], mask_rows[:, 2:4], 0)
         copy_keys(1, ALL)
-        load_half(q_raw[0][1], q_rows[0], 1)
         nc.sync.dma_start(out=v_raw[:], in_=v[0].rearrange("(p r) e -> p r e", r=PACK))
-        load_half(mask_last, mask_rows, 1)
+        load_half(q_raw[0][1], q_rows[0], 1)
         load_half(q_raw[1][1], q_rows[1], 1)
+        load_half(mask_last, mask_rows, 1)
 
         round_queries("scalar", 0, 0, Q_VECTOR, HALF)
         quantize(q_mx[0][0])
@@ -312,34 +306,35 @@ def tile_rows_a_lin_kb_mask_kernel(tc, qT, kT, t, v, kb, mask, out):
         scores(0, 0, LOW)
         scores(2, 0, LOW)
         scores(2, 0, HIGH)
-        scores(0, 0, HIGH)
         for r in LOW:
             scale_mask("vector", 0, r)
         weigh_bank(0)
+        scores(0, 0, HIGH)
         scores(1, 0, LOW)
         scores(1, 0, HIGH)
+        scores(3, 0, LOW)
         affine(0)
         affine(0)
         for r in HIGH:
             scale_mask("vector", 0, r)
         weigh_bank(0)
-        weigh_dealt(2, 0)
-        pack("gpsimd", 0, 0, 0, G_FIRST)
-        pack("scalar", 0, 0, G_FIRST, HALF)
+        weigh(2, 0, 0, G_WEIGHS, nc.gpsimd)
+        round_rows("scalar", v_mx, v_raw, 0, E)
+        pack("scalar", 0, 0, 0, HALF)
         round_queries("scalar", 0, 1, 0, HALF)
-        for places in (LOW, HIGH):
-            weigh_bank(1)
-            scores(3, 0, places)
+        weigh_bank(1)
+        scores(3, 0, HIGH)
+        weigh_bank(1)
+        pack("gpsimd", 1, 0, 0, G_THIRD)
+        pack("scalar", 1, 0, G_THIRD, HALF)
+        weigh_bank(1)
+        weigh_bank(1)
         quantize(first_two, 0, 2 * HALF)
         quantize(q_mx[0][1])
-        scores(0, 1, LOW)
-        scores(0, 1, HIGH)
-        round_rows("scalar", v_mx, v_raw, 0, E)
-        pack("gpsimd", 1, 0, 0, G_SHARE)
-        pack("scalar", 1, 0, G_SHARE, HALF)
         for places in (LOW, HIGH):
-            weigh_bank(1)
-            scores(1, 1, places)
+            scores_both((0, 1, places, 0, HALF), (1, 1, places, 0, HALF))
+        round_queries("vector", 1, 1, 0, Q_LAST)
+        round_queries("scalar", 1, 1, Q_LAST, HALF)
         quantize(v_mx, 0, E)
         for r in range(1):
             scale_mask("vector", 1, r)
@@ -349,21 +344,20 @@ def tile_rows_a_lin_kb_mask_kernel(tc, qT, kT, t, v, kb, mask, out):
         values(0, 0, 0, 0)
         values(0, HALF, 2, 0)
         values(1, 0, 1, 0)
-        round_queries("scalar", 1, 1, 0, HALF)
         pack("gpsimd", 3, 0, 0, G_SHARE)
         pack("scalar", 3, 0, G_SHARE, HALF)
-        finish(0, 0, (0, 2), dealt=(0, 2))
+        finish(0, 0, (0, 2), dealt=(0,))
         weigh_bank(0)
         weigh_bank(0)
         quantize(fourth, 0, 2 * HALF)
         pack("gpsimd", 0, 1, 0, G_SHARE)
         pack("scalar", 0, 1, G_SHARE, HALF)
-        scores(2, 1, ALL, 0, P)
-        weigh_bank(1)
-        scores_both((2, 1, ALL, P, HALF), (3, 1, LOW, 0, HALF))
+        scores_both((2, 1, ALL, 0, P), (3, 1, LOW, 0, HALF))
         values(1, HALF, 3, 0)
+        scores(2, 1, ALL, P, HALF)
         weigh_bank(1)
         scores(3, 1, HIGH)
+        weigh_bank(1)
         quantize(w_mx[0][1])
         values(0, 0, 0, 1)
         affine(0)

@@ -29,10 +29,9 @@ Q_SECOND = 176
 K_START, K_END = 32, 96
 PLACE_WORDS = P + P // PACK
 K_FILL = 64
-G_SHARE = 112
+G_SHARE = 104
 G_WEIGHS = 256
-G_THIRD = 56
-Q_LAST = 160
+Q_LAST = 256
 V_LAST = 144
 LOW, HIGH, ALL = (0, 1), (2, 3), (0, 1, 2, 3)
 
@@ -69,11 +68,11 @@ def tile_rows_a_lin_kb_mask_kernel(tc, qT, kT, t, v, kb, mask, out):
         mask_last = tile("mask1", [P, PACK, HALF], F32)
         mask_half = [tile("mask0", [P, PACK, HALF], F32), mask_last]
         mask_sb = [[mask_half[half][:, 2 * a : 2 * a + 2] for a in range(2)] for half in range(2)]
-        mask_t = [[tile("maskt%d_%d" % (half, r), [P, HALF], F32) for r in range(PACK)] for half in range(2)]
+        mask_t_half = [tile("mask_t%d" % half, [P, PACK, HALF], F32) for half in range(2)]
+        mask_t = [[mask_t_half[half][:, r] for r in range(PACK)] for half in range(2)]
         v_raw = tile("v_raw", [P, PACK, E], F32)
         t_sb = tile("t_sb", [P, PACK], F32)
         kb_sb = tile("kb_sb", [P, PACK], F32)
-        kbt = tile("kbt", [P, PACK], F32)
         warm = tile("warm", [P, 2], F32)
         k_made = tile("k_made", [K_END, PACK * PLACE_WORDS], I32)
         k_words = tile("k_words", [P, PACK * PLACE_WORDS], I32)
@@ -99,7 +98,7 @@ def tile_rows_a_lin_kb_mask_kernel(tc, qT, kT, t, v, kb, mask, out):
         def window(mx, c0, columns):
             return tuple(part[:, c0 : c0 + columns] for part in mx)
 
-        widths = (2 * HALF, HALF, 2 * HALF, HALF, HALF)
+        widths = (2 * HALF, HALF, HALF, HALF, HALF)
         chain = tile("chain", [P, sum(widths) - 3 * G_SHARE, PACK], BF16)
         calls = []
         for n, width in enumerate(widths):
@@ -108,11 +107,13 @@ def tile_rows_a_lin_kb_mask_kernel(tc, qT, kT, t, v, kb, mask, out):
                 (chain[:, c0 : c0 + width], tile("codes%d" % n, [P, width], U32), tile("scales%d" % n, [P, width], U8))
             )
         first_two, third, fourth = calls[0:3]
-        q_mx = [[mx_tiles("q0_0", HALF), mx_tiles("q0_1", HALF)], [mx_tiles("q1_0", HALF), window(fourth, HALF, HALF)]]
+        q_mx = [[mx_tiles("q0_0", HALF), mx_tiles("q0_1", HALF)], [mx_tiles("q1_0", HALF), mx_tiles("q1_1", HALF)]]
         v_mx = mx_tiles("v", E)
         scaled = [tile("scaled%d" % half, [P, PACK, HALF], F32) for half in range(2)]
-        rows_bf = [[tile("rows%d_%d" % (h, half), [P, PACK, HALF], BF16) for half in range(2)] for h in range(H)]
-        w_first = [window(first_two, 0, HALF), third, window(first_two, HALF, HALF), window(fourth, 0, HALF)]
+        rows_upper = tile("rows_upper", [P, PACK, NQ], BF16)
+        rows_first = [None, rows_upper[:, :, 0:HALF], tile("rows2_0", [P, PACK, HALF], BF16), rows_upper[:, :, HALF:]]
+        rows_bf = [[rows_first[h], tile("rows%d_1" % h, [P, PACK, HALF], BF16)] for h in range(H)]
+        w_first = [window(first_two, 0, HALF), third, window(first_two, HALF, HALF), fourth]
         w_second = [calls[3], calls[4], mx_tiles("w2_1", HALF), mx_tiles("w3_1", HALF)]
         w_mx = [[w_first[h], w_second[h]] for h in range(H)]
 
@@ -180,24 +181,20 @@ def tile_rows_a_lin_kb_mask_kernel(tc, qT, kT, t, v, kb, mask, out):
                 for call in first[n : n + 1] + second[n : n + 1]:
                     nc.tensor.matmul_mx(**call)
 
-        def affine(g, engine="scalar"):
+        def affine(g):
             n = emptied[g]
             emptied[g] = n + 1
             h, half, places, c0, c1 = fills[g][n]
             for slot, r in enumerate(places):
                 dst = scaled[half][:, r, c0:c1]
                 src = score_banks[g][n % SCORE_BANKS[g]][:, slot * (c1 - c0) : (slot + 1) * (c1 - c0)]
-                scale, bias = t_sb[:, r : r + 1], kbt[:, r : r + 1]
-                if engine == "vector":
-                    nc.vector.tensor_scalar(out=dst, in0=src, scalar1=scale, scalar2=bias, op0=MULT, op1=ADD)
-                else:
-                    nc.scalar.activation(out=dst, in_=src, func=IDENT, scale=scale, bias=bias)
+                nc.scalar.activation(out=dst, in_=src, func=IDENT, bias=kb_sb[:, r : r + 1])
 
         def weigh(h, half, c0, c1, engine=nc.vector):
             engine.tensor_tensor(
                 out=w_mx[h][half][0][:, c0:c1].rearrange("p (c i) r -> p c r i", i=RUN),
                 in0=scaled[half][:, :, c0:c1].rearrange("p r (c i) -> p c r i", i=RUN),
-                in1=mask_half[half][:, :, c0:c1].rearrange("p r (c i) -> p c r i", i=RUN),
+                in1=mask_t_half[half][:, :, c0:c1].rearrange("p r (c i) -> p c r i", i=RUN),
                 op=MULT,
             )
 
@@ -216,6 +213,48 @@ def tile_rows_a_lin_kb_mask_kernel(tc, qT, kT, t, v, kb, mask, out):
                     op0=ADD,
                     op1=MULT,
                 )
+
+        def scores_upper(r):
+            bank = score_banks[1][len(fills[1]) % SCORE_BANKS[1]]
+            fills[1].append(r)
+            rows = row_tiles[1]
+            for pair in range(2):
+                for q0 in range(0, HALF, P):
+                    nc.tensor.matmul_mx(
+                        out=bank[:, pair * HALF + q0 : pair * HALF + q0 + P],
+                        lhsT=place_codes(k_words[rows], r),
+                        lhsT_scale=place_scales(k_words[rows], r),
+                        rhs=q_mx[pair][0][1][rows, q0 : q0 + P].bitcast(FP8X4),
+                        rhs_scale=q_mx[pair][0][2][rows, q0 : q0 + P],
+                        start=True,
+                        stop=True,
+                    )
+
+        def weigh_upper():
+            n = emptied[1]
+            emptied[1] = n + 1
+            r = fills[1][n]
+            nc.vector.scalar_tensor_tensor(
+                out=rows_upper[:, r, :].rearrange("p (b a m) -> p a m b", b=2, a=2),
+                in0=score_banks[1][n % SCORE_BANKS[1]][:].rearrange("p (a m b) -> p a m b", b=2, a=2),
+                scalar=kb_sb[:, r : r + 1],
+                in1=mask_t[0][r][:].rearrange("p (m b) -> p m b", b=2).unsqueeze(1).to_broadcast([P, 2, P, 2]),
+                op0=ADD,
+                op1=MULT,
+            )
+
+        def values_upper(bank):
+            for a in range(2):
+                for b, mx in enumerate((w_mx[1][0], w_mx[3][0])):
+                    nc.tensor.matmul_mx(
+                        out=y_banks[bank][:, (2 * a + b) * P : (2 * a + b + 1) * P],
+                        lhsT=mx[1][:, a * P : (a + 1) * P].bitcast(FP8X4),
+                        lhsT_scale=mx[2][:, a * P : (a + 1) * P],
+                        rhs=v_mx[1][:].bitcast(FP8X4),
+                        rhs_scale=v_mx[2][:],
+                        start=True,
+                        stop=True,
+                    )
 
         def scale_mask(engine, half, r):
             src = mask_sb[half][r // 2][:, r % 2, :]
@@ -285,7 +324,6 @@ def tile_rows_a_lin_kb_mask_kernel(tc, qT, kT, t, v, kb, mask, out):
             quantize_keys(r)
             copy_keys(0, (r,))
         load_half(mask_sb[0][0], mask_rows[:, 0:2], 0)
-        nc.vector.tensor_tensor(out=kbt[:], in0=kb_sb[:], in1=t_sb[:], op=MULT)
         for r in HIGH:
             quantize_keys(r)
         round_queries("vector", 0, 0, 0, Q_VECTOR)
@@ -305,62 +343,58 @@ def tile_rows_a_lin_kb_mask_kernel(tc, qT, kT, t, v, kb, mask, out):
 
         scores(0, 0, LOW)
         scores(2, 0, LOW)
+        scores(0, 0, HIGH)
+        affine(0)
         scores(2, 0, HIGH)
+        for r in (0, 1, 2):
+            scores_upper(r)
         for r in LOW:
             scale_mask("vector", 0, r)
         weigh_bank(0)
-        scores(0, 0, HIGH)
-        scores(1, 0, LOW)
-        scores(1, 0, HIGH)
-        scores(3, 0, LOW)
-        affine(0)
         affine(0)
         for r in HIGH:
             scale_mask("vector", 0, r)
+        weigh(0, 0, 0, G_WEIGHS, nc.gpsimd)
         weigh_bank(0)
-        weigh(2, 0, 0, G_WEIGHS, nc.gpsimd)
         round_rows("scalar", v_mx, v_raw, 0, E)
-        pack("scalar", 0, 0, 0, HALF)
+        pack("scalar", 2, 0, 0, HALF)
         round_queries("scalar", 0, 1, 0, HALF)
-        weigh_bank(1)
-        scores(3, 0, HIGH)
-        weigh_bank(1)
-        pack("gpsimd", 1, 0, 0, G_THIRD)
-        pack("scalar", 1, 0, G_THIRD, HALF)
-        weigh_bank(1)
-        weigh_bank(1)
+        weigh_upper()
+        scores_upper(3)
+        for r in (1, 2, 3):
+            weigh_upper()
         quantize(first_two, 0, 2 * HALF)
+        quantize(v_mx, 0, E)
         quantize(q_mx[0][1])
         for places in (LOW, HIGH):
             scores_both((0, 1, places, 0, HALF), (1, 1, places, 0, HALF))
+        pack("scalar", 1, 0, 0, HALF)
         round_queries("vector", 1, 1, 0, Q_LAST)
-        round_queries("scalar", 1, 1, Q_LAST, HALF)
-        quantize(v_mx, 0, E)
         for r in range(1):
             scale_mask("vector", 1, r)
         for r in range(1, PACK):
             scale_mask("scalar", 1, r)
-        quantize(w_mx[1][0])
         values(0, 0, 0, 0)
         values(0, HALF, 2, 0)
-        values(1, 0, 1, 0)
+        quantize(q_mx[1][1])
+        quantize(w_mx[1][0])
+        scores_both((2, 1, ALL, 0, P), (3, 1, LOW, 0, HALF))
         pack("gpsimd", 3, 0, 0, G_SHARE)
         pack("scalar", 3, 0, G_SHARE, HALF)
-        finish(0, 0, (0, 2), dealt=(0,))
+        finish(0, 0, (0, 2), dealt=(2,))
         weigh_bank(0)
+        scores(2, 1, ALL, P, HALF)
         weigh_bank(0)
-        quantize(fourth, 0, 2 * HALF)
+        quantize(w_mx[3][0])
+        values_upper(1)
         pack("gpsimd", 0, 1, 0, G_SHARE)
         pack("scalar", 0, 1, G_SHARE, HALF)
-        scores_both((2, 1, ALL, 0, P), (3, 1, LOW, 0, HALF))
-        values(1, HALF, 3, 0)
-        scores(2, 1, ALL, P, HALF)
+        affine(0)
         weigh_bank(1)
         scores(3, 1, HIGH)
         weigh_bank(1)
         quantize(w_mx[0][1])
         values(0, 0, 0, 1)
-        affine(0)
         pack("gpsimd", 1, 1, 0, G_SHARE)
         pack("scalar", 1, 1, G_SHARE, HALF)
         affine(0)

@@ -110,9 +110,9 @@ def tile_rows_a_lin_kb_mask_kernel(tc, qT, kT, t, v, kb, mask, out):
         q_mx = [[mx_tiles("q0_0", HALF), mx_tiles("q0_1", HALF)], [mx_tiles("q1_0", HALF), mx_tiles("q1_1", HALF)]]
         v_mx = mx_tiles("v", E)
         scaled = [tile("scaled%d" % half, [P, PACK, HALF], F32) for half in range(2)]
-        rows_upper = tile("rows_upper", [P, PACK, NQ], BF16)
-        rows_first = [None, rows_upper[:, :, 0:HALF], tile("rows2_0", [P, PACK, HALF], BF16), rows_upper[:, :, HALF:]]
-        rows_bf = [[rows_first[h], tile("rows%d_1" % h, [P, PACK, HALF], BF16)] for h in range(H)]
+        rows_upper = tile("rows_upper", [P, PACK, NQ], F32)
+        rows_first = [None, rows_upper[:, :, 0:HALF], tile("rows2_0", [P, PACK, HALF], F32), rows_upper[:, :, HALF:]]
+        w_rows = [[rows_first[h], tile("rows%d_1" % h, [P, PACK, HALF], F32)] for h in range(H)]
         w_first = [window(first_two, 0, HALF), third, window(first_two, HALF, HALF), fourth]
         w_second = [calls[3], calls[4], mx_tiles("w2_1", HALF), mx_tiles("w3_1", HALF)]
         w_mx = [[w_first[h], w_second[h]] for h in range(H)]
@@ -204,7 +204,7 @@ def tile_rows_a_lin_kb_mask_kernel(tc, qT, kT, t, v, kb, mask, out):
             h, half, places, c0, c1 = fills[g][n]
             for slot, r in enumerate(places):
                 nc.vector.scalar_tensor_tensor(
-                    out=rows_bf[h][half][:, r, :].rearrange("p (b m) -> p m b", b=2),
+                    out=w_rows[h][half][:, r, :].rearrange("p (b m) -> p m b", b=2),
                     in0=score_banks[g][n % SCORE_BANKS[g]][:, slot * HALF : (slot + 1) * HALF].rearrange(
                         "p (m b) -> p m b", b=2
                     ),
@@ -269,14 +269,14 @@ def tile_rows_a_lin_kb_mask_kernel(tc, qT, kT, t, v, kb, mask, out):
             if engine == "gpsimd":
                 nc.gpsimd.tensor_scalar(
                     out=w_mx[h][half][0][:, c0:c1, :],
-                    in0=rows_bf[h][half][:, :, c0:c1].rearrange("p r c -> p c r"),
+                    in0=w_rows[h][half][:, :, c0:c1].rearrange("p r c -> p c r"),
                     scalar1=1.0,
                     scalar2=0.0,
                     op0=MULT,
                     op1=ADD,
                 )
             else:
-                round_rows(engine, w_mx[h][half], rows_bf[h][half], c0, c1)
+                round_rows(engine, w_mx[h][half], w_rows[h][half], c0, c1)
 
         def values(bank, b0, h, half, c0=0, c1=HALF):
             for q0 in range(c0, c1, P):

@@ -21,19 +21,17 @@ ROWS = D // PACK
 BANK = 512
 HALF = NQ // 2
 RUN = 4
-SCORE_BANKS = (3, 3)
+SCORE_BANKS = 3
 Y_BANKS = 2
 K_VECTOR = 84
+K_FILL = 64
 Q_VECTOR = 128
 Q_SECOND = 176
 K_START, K_END = 32, 96
 PLACE_WORDS = P + P // PACK
-K_FILL = 64
-G_SHARE = 104
-G_WEIGHS = 256
-Q_LAST = 256
-V_LAST = 144
-LOW, HIGH, ALL = (0, 1), (2, 3), (0, 1, 2, 3)
+G_PACK = 96
+V_LAST = 192
+LOW, HIGH = (0, 1), (2, 3)
 
 
 def tile_rows_a_lin_kb_mask_kernel(tc, qT, kT, t, v, kb, mask, out):
@@ -54,7 +52,7 @@ def tile_rows_a_lin_kb_mask_kernel(tc, qT, kT, t, v, kb, mask, out):
             )
 
         score_banks = [
-            [ps.tile([P, BANK], F32, name="score%d_%d" % (g, i)) for i in range(SCORE_BANKS[g])] for g in range(2)
+            [ps.tile([P, BANK], F32, name="score%d_%d" % (g, i)) for i in range(SCORE_BANKS)] for g in range(2)
         ]
         y_banks = [ps.tile([P, BANK], F32, name="y%d" % i) for i in range(Y_BANKS)]
 
@@ -73,6 +71,7 @@ def tile_rows_a_lin_kb_mask_kernel(tc, qT, kT, t, v, kb, mask, out):
         v_raw = tile("v_raw", [P, PACK, E], F32)
         t_sb = tile("t_sb", [P, PACK], F32)
         kb_sb = tile("kb_sb", [P, PACK], F32)
+        kbt = tile("kbt", [P, PACK], F32)
         warm = tile("warm", [P, 2], F32)
         k_made = tile("k_made", [K_END, PACK * PLACE_WORDS], I32)
         k_words = tile("k_words", [P, PACK * PLACE_WORDS], I32)
@@ -98,24 +97,19 @@ def tile_rows_a_lin_kb_mask_kernel(tc, qT, kT, t, v, kb, mask, out):
         def window(mx, c0, columns):
             return tuple(part[:, c0 : c0 + columns] for part in mx)
 
-        widths = (2 * HALF, HALF, HALF, HALF, HALF)
-        chain = tile("chain", [P, sum(widths) - 3 * G_SHARE, PACK], BF16)
-        calls = []
-        for n, width in enumerate(widths):
-            c0 = sum(widths[:n]) - max(n - 1, 0) * G_SHARE
-            calls.append(
-                (chain[:, c0 : c0 + width], tile("codes%d" % n, [P, width], U32), tile("scales%d" % n, [P, width], U8))
-            )
-        first_two, third, fourth = calls[0:3]
-        q_mx = [[mx_tiles("q0_0", HALF), mx_tiles("q0_1", HALF)], [mx_tiles("q1_0", HALF), mx_tiles("q1_1", HALF)]]
+        lower = mx_tiles("lower", NQ)
+        q_mx = [[mx_tiles("q%d_%d" % (pair, half), HALF) for half in range(2)] for pair in range(2)]
         v_mx = mx_tiles("v", E)
         scaled = [tile("scaled%d" % half, [P, PACK, HALF], F32) for half in range(2)]
-        rows_upper = tile("rows_upper", [P, PACK, NQ], F32)
-        rows_first = [None, rows_upper[:, :, 0:HALF], tile("rows2_0", [P, PACK, HALF], F32), rows_upper[:, :, HALF:]]
-        w_rows = [[rows_first[h], tile("rows%d_1" % h, [P, PACK, HALF], F32)] for h in range(H)]
-        w_first = [window(first_two, 0, HALF), third, window(first_two, HALF, HALF), fourth]
-        w_second = [calls[3], calls[4], mx_tiles("w2_1", HALF), mx_tiles("w3_1", HALF)]
-        w_mx = [[w_first[h], w_second[h]] for h in range(H)]
+        w_rows = [[tile("rows%d_%d" % (h, half), [P, PACK, HALF], F32) if h else None for half in range(2)] for h in range(H)]
+        w1 = mx_tiles("w1_0", HALF)
+        reused = (w1[0], tile("codes0_1", [P, HALF], U32), tile("scales0_1", [P, HALF], U8))
+        w_mx = [
+            [window(lower, 0, HALF), reused],
+            [w1, mx_tiles("w1_1", HALF)],
+            [window(lower, HALF, HALF), mx_tiles("w2_1", HALF)],
+            [mx_tiles("w3_0", HALF), mx_tiles("w3_1", HALF)],
+        ]
 
         def load_half(dst, rows, half):
             nc.sync.dma_start(out=dst[:], in_=rows[:, :, half * HALF : (half + 1) * HALF])
@@ -151,7 +145,7 @@ def tile_rows_a_lin_kb_mask_kernel(tc, qT, kT, t, v, kb, mask, out):
 
         def score_calls(h, half, places, c0, c1):
             pair, g = divmod(h, 2)
-            bank = score_banks[g][len(fills[g]) % SCORE_BANKS[g]]
+            bank = score_banks[g][len(fills[g]) % SCORE_BANKS]
             fills[g].append((h, half, places, c0, c1))
             rows = row_tiles[g]
             calls = []
@@ -187,14 +181,17 @@ def tile_rows_a_lin_kb_mask_kernel(tc, qT, kT, t, v, kb, mask, out):
             h, half, places, c0, c1 = fills[g][n]
             for slot, r in enumerate(places):
                 dst = scaled[half][:, r, c0:c1]
-                src = score_banks[g][n % SCORE_BANKS[g]][:, slot * (c1 - c0) : (slot + 1) * (c1 - c0)]
-                nc.scalar.activation(out=dst, in_=src, func=IDENT, bias=kb_sb[:, r : r + 1])
+                src = score_banks[g][n % SCORE_BANKS][:, slot * (c1 - c0) : (slot + 1) * (c1 - c0)]
+                if half == 0:
+                    nc.scalar.activation(out=dst, in_=src, func=IDENT, bias=kb_sb[:, r : r + 1])
+                else:
+                    nc.scalar.activation(out=dst, in_=src, func=IDENT, scale=t_sb[:, r : r + 1], bias=kbt[:, r : r + 1])
 
-        def weigh(h, half, c0, c1, engine=nc.vector):
+        def weigh(h, half, c0, c1, engine):
             engine.tensor_tensor(
                 out=w_mx[h][half][0][:, c0:c1].rearrange("p (c i) r -> p c r i", i=RUN),
                 in0=scaled[half][:, :, c0:c1].rearrange("p r (c i) -> p c r i", i=RUN),
-                in1=mask_t_half[half][:, :, c0:c1].rearrange("p r (c i) -> p c r i", i=RUN),
+                in1=(mask_t_half[0], mask_last)[half][:, :, c0:c1].rearrange("p r (c i) -> p c r i", i=RUN),
                 op=MULT,
             )
 
@@ -205,7 +202,7 @@ def tile_rows_a_lin_kb_mask_kernel(tc, qT, kT, t, v, kb, mask, out):
             for slot, r in enumerate(places):
                 nc.vector.scalar_tensor_tensor(
                     out=w_rows[h][half][:, r, :].rearrange("p (b m) -> p m b", b=2),
-                    in0=score_banks[g][n % SCORE_BANKS[g]][:, slot * HALF : (slot + 1) * HALF].rearrange(
+                    in0=score_banks[g][n % SCORE_BANKS][:, slot * HALF : (slot + 1) * HALF].rearrange(
                         "p (m b) -> p m b", b=2
                     ),
                     scalar=kb_sb[:, r : r + 1],
@@ -213,48 +210,6 @@ def tile_rows_a_lin_kb_mask_kernel(tc, qT, kT, t, v, kb, mask, out):
                     op0=ADD,
                     op1=MULT,
                 )
-
-        def scores_upper(r):
-            bank = score_banks[1][len(fills[1]) % SCORE_BANKS[1]]
-            fills[1].append(r)
-            rows = row_tiles[1]
-            for pair in range(2):
-                for q0 in range(0, HALF, P):
-                    nc.tensor.matmul_mx(
-                        out=bank[:, pair * HALF + q0 : pair * HALF + q0 + P],
-                        lhsT=place_codes(k_words[rows], r),
-                        lhsT_scale=place_scales(k_words[rows], r),
-                        rhs=q_mx[pair][0][1][rows, q0 : q0 + P].bitcast(FP8X4),
-                        rhs_scale=q_mx[pair][0][2][rows, q0 : q0 + P],
-                        start=True,
-                        stop=True,
-                    )
-
-        def weigh_upper():
-            n = emptied[1]
-            emptied[1] = n + 1
-            r = fills[1][n]
-            nc.vector.scalar_tensor_tensor(
-                out=rows_upper[:, r, :].rearrange("p (b a m) -> p a m b", b=2, a=2),
-                in0=score_banks[1][n % SCORE_BANKS[1]][:].rearrange("p (a m b) -> p a m b", b=2, a=2),
-                scalar=kb_sb[:, r : r + 1],
-                in1=mask_t[0][r][:].rearrange("p (m b) -> p m b", b=2).unsqueeze(1).to_broadcast([P, 2, P, 2]),
-                op0=ADD,
-                op1=MULT,
-            )
-
-        def values_upper(bank):
-            for a in range(2):
-                for b, mx in enumerate((w_mx[1][0], w_mx[3][0])):
-                    nc.tensor.matmul_mx(
-                        out=y_banks[bank][:, (2 * a + b) * P : (2 * a + b + 1) * P],
-                        lhsT=mx[1][:, a * P : (a + 1) * P].bitcast(FP8X4),
-                        lhsT_scale=mx[2][:, a * P : (a + 1) * P],
-                        rhs=v_mx[1][:].bitcast(FP8X4),
-                        rhs_scale=v_mx[2][:],
-                        start=True,
-                        stop=True,
-                    )
 
         def scale_mask(engine, half, r):
             src = mask_sb[half][r // 2][:, r % 2, :]
@@ -290,19 +245,18 @@ def tile_rows_a_lin_kb_mask_kernel(tc, qT, kT, t, v, kb, mask, out):
                     stop=True,
                 )
 
-        def finish(bank, half, heads, c0=0, c1=HALF, dealt=()):
+        def finish(bank, b0, units, engine="scalar", c0=0, c1=HALF):
             blocks = (c1 - c0) // P
-            y_sb = tile("y_sb%d_%d_%d" % (heads[0], half, c0), [P, len(heads) * blocks, E], F32)
-            nc.scalar.activation(
-                out=y_sb[:].rearrange("p b e -> p (b e)"),
-                in_=y_banks[bank][:, 0 : len(heads) * blocks * E],
-                func=IDENT,
-                scale=1.0 / 16.0,
-            )
-            q0 = half * HALF + c0
-            for n, h in enumerate(heads):
+            y_sb = tile("y_sb%d_%d_%d" % (units[0] + (c0,)), [P, len(units) * blocks, E], F32)
+            dst, src = y_sb[:].rearrange("p b e -> p (b e)"), y_banks[bank][:, b0 : b0 + len(units) * blocks * E]
+            if engine == "vector":
+                nc.vector.tensor_scalar(out=dst, in0=src, scalar1=1.0 / 16.0, scalar2=None, op0=MULT)
+            else:
+                nc.scalar.activation(out=dst, in_=src, func=IDENT, scale=1.0 / 16.0)
+            for n, (h, half) in enumerate(units):
+                q0 = half * HALF + c0
                 nc.sync.dma_start(
-                    out=out[h, q0 : q0 + c1 - c0, :].rearrange("(m b) e -> m b e" if h in dealt else "(b m) e -> m b e", m=P),
+                    out=out[h, q0 : q0 + c1 - c0, :].rearrange("(m b) e -> m b e" if h else "(b m) e -> m b e", m=P),
                     in_=y_sb[:, n * blocks : (n + 1) * blocks],
                 )
 
@@ -324,12 +278,14 @@ def tile_rows_a_lin_kb_mask_kernel(tc, qT, kT, t, v, kb, mask, out):
             quantize_keys(r)
             copy_keys(0, (r,))
         load_half(mask_sb[0][0], mask_rows[:, 0:2], 0)
+        nc.vector.tensor_tensor(out=kbt[:], in0=kb_sb[:], in1=t_sb[:], op=MULT)
         for r in HIGH:
             quantize_keys(r)
         round_queries("vector", 0, 0, 0, Q_VECTOR)
         copy_keys(0, HIGH)
         load_half(mask_sb[0][1], mask_rows[:, 2:4], 0)
-        copy_keys(1, ALL)
+        copy_keys(1, LOW)
+        copy_keys(1, HIGH)
         nc.sync.dma_start(out=v_raw[:], in_=v[0].rearrange("(p r) e -> p r e", r=PACK))
         load_half(q_raw[0][1], q_rows[0], 1)
         load_half(q_raw[1][1], q_rows[1], 1)
@@ -346,74 +302,71 @@ def tile_rows_a_lin_kb_mask_kernel(tc, qT, kT, t, v, kb, mask, out):
         scores(0, 0, HIGH)
         affine(0)
         scores(2, 0, HIGH)
-        for r in (0, 1, 2):
-            scores_upper(r)
+        scores(1, 0, LOW)
+        scores(1, 0, HIGH)
+        scores(3, 0, LOW)
         for r in LOW:
             scale_mask("vector", 0, r)
         weigh_bank(0)
         affine(0)
         for r in HIGH:
             scale_mask("vector", 0, r)
-        weigh(0, 0, 0, G_WEIGHS, nc.gpsimd)
+        weigh(0, 0, 0, HALF, nc.gpsimd)
         weigh_bank(0)
         round_rows("scalar", v_mx, v_raw, 0, E)
-        pack("scalar", 2, 0, 0, HALF)
         round_queries("scalar", 0, 1, 0, HALF)
-        weigh_upper()
-        scores_upper(3)
-        for r in (1, 2, 3):
-            weigh_upper()
-        quantize(first_two, 0, 2 * HALF)
-        quantize(v_mx, 0, E)
+        pack("scalar", 2, 0, 0, HALF)
+        weigh_bank(1)
+        scores(3, 0, HIGH)
+        weigh_bank(1)
+        pack("scalar", 1, 0, 0, HALF)
+        weigh_bank(1)
+        weigh_bank(1)
         quantize(q_mx[0][1])
+        round_queries("vector", 1, 1, 0, HALF)
         for places in (LOW, HIGH):
             scores_both((0, 1, places, 0, HALF), (1, 1, places, 0, HALF))
-        pack("scalar", 1, 0, 0, HALF)
-        round_queries("vector", 1, 1, 0, Q_LAST)
-        for r in range(1):
-            scale_mask("vector", 1, r)
-        for r in range(1, PACK):
-            scale_mask("scalar", 1, r)
+        quantize(lower, 0, NQ)
+        quantize(q_mx[1][1])
+        quantize(v_mx, 0, E)
+        scores_both((2, 1, LOW, 0, HALF), (3, 1, LOW, 0, HALF))
         values(0, 0, 0, 0)
         values(0, HALF, 2, 0)
-        quantize(q_mx[1][1])
-        quantize(w_mx[1][0])
-        scores_both((2, 1, ALL, 0, P), (3, 1, LOW, 0, HALF))
-        pack("gpsimd", 3, 0, 0, G_SHARE)
-        pack("scalar", 3, 0, G_SHARE, HALF)
-        finish(0, 0, (0, 2), dealt=(2,))
-        weigh_bank(0)
-        scores(2, 1, ALL, P, HALF)
-        weigh_bank(0)
-        quantize(w_mx[3][0])
-        values_upper(1)
-        pack("gpsimd", 0, 1, 0, G_SHARE)
-        pack("scalar", 0, 1, G_SHARE, HALF)
         affine(0)
+        affine(0)
+        for r in LOW:
+            scale_mask("vector", 1, r)
+        quantize(w_mx[1][0])
+        weigh(0, 1, 0, HALF, nc.gpsimd)
+        for r in HIGH:
+            scale_mask("scalar", 1, r)
+        values(1, 0, 1, 0)
+        scores(2, 1, HIGH)
         weigh_bank(1)
         scores(3, 1, HIGH)
         weigh_bank(1)
+        pack("scalar", 3, 0, 0, HALF)
+        finish(0, 0, [(0, 0), (2, 0)])
+        weigh_bank(0)
+        weigh_bank(0)
+        pack("scalar", 1, 1, 0, HALF)
+        finish(1, 0, [(1, 0)])
+        weigh_bank(1)
+        weigh_bank(1)
+        pack("gpsimd", 2, 1, 0, G_PACK)
+        pack("scalar", 2, 1, G_PACK, HALF)
+        quantize(w_mx[3][0])
         quantize(w_mx[0][1])
-        values(0, 0, 0, 1)
-        pack("gpsimd", 1, 1, 0, G_SHARE)
-        pack("scalar", 1, 1, G_SHARE, HALF)
-        affine(0)
-        weigh_bank(1)
-        weigh_bank(1)
+        values(0, 0, 3, 0)
+        values(0, HALF, 0, 1)
         quantize(w_mx[1][1])
-        values(0, HALF, 1, 1)
+        values(1, 0, 1, 1)
         pack("vector", 3, 1, 0, V_LAST)
         pack("scalar", 3, 1, V_LAST, HALF)
-        finish(1, 0, (1, 3), dealt=(1, 3))
-        finish(0, 1, (0, 1), dealt=(0, 1))
-        weigh(2, 1, 0, P)
+        quantize(w_mx[2][1])
+        values(1, HALF, 2, 1)
+        finish(0, 0, [(3, 0), (0, 1)])
         quantize(w_mx[3][1])
-        values(1, 0, 3, 1)
-        weigh(2, 1, P, HALF)
-        finish(1, 1, (3,), dealt=(3,))
-        last_blocks = ((0, 0), (1, P))
-        for bank, c0 in last_blocks:
-            quantize(w_mx[2][1], c0, c0 + P)
-            values(bank, 0, 2, 1, c0, c0 + P)
-        for bank, c0 in last_blocks:
-            finish(bank, 1, (2,), c0, c0 + P)
+        values(0, 0, 3, 1)
+        finish(1, 0, [(1, 1), (2, 1)], "vector")
+        finish(0, 0, [(3, 1)])

@@ -30,7 +30,7 @@ Q_SECOND = 176
 K_START, K_END = 32, 96
 PLACE_WORDS = P + P // PACK
 G_PACK = 96
-V_LAST = 192
+V_LAST = 160
 LOW, HIGH = (0, 1), (2, 3)
 
 
@@ -277,17 +277,17 @@ def tile_rows_a_lin_kb_mask_kernel(tc, qT, kT, t, v, kb, mask, out):
         for r in LOW:
             quantize_keys(r)
             copy_keys(0, (r,))
-        load_half(mask_sb[0][0], mask_rows[:, 0:2], 0)
+        copy_keys(1, LOW)
         nc.vector.tensor_tensor(out=kbt[:], in0=kb_sb[:], in1=t_sb[:], op=MULT)
         for r in HIGH:
             quantize_keys(r)
         round_queries("vector", 0, 0, 0, Q_VECTOR)
         copy_keys(0, HIGH)
+        load_half(mask_sb[0][0], mask_rows[:, 0:2], 0)
         load_half(mask_sb[0][1], mask_rows[:, 2:4], 0)
-        copy_keys(1, LOW)
         copy_keys(1, HIGH)
-        nc.sync.dma_start(out=v_raw[:], in_=v[0].rearrange("(p r) e -> p r e", r=PACK))
         load_half(q_raw[0][1], q_rows[0], 1)
+        nc.sync.dma_start(out=v_raw[:], in_=v[0].rearrange("(p r) e -> p r e", r=PACK))
         load_half(q_raw[1][1], q_rows[1], 1)
         load_half(mask_last, mask_rows, 1)
 
@@ -297,32 +297,29 @@ def tile_rows_a_lin_kb_mask_kernel(tc, qT, kT, t, v, kb, mask, out):
         round_queries("scalar", 1, 0, Q_SECOND, HALF)
         quantize(q_mx[1][0])
 
-        scores(0, 0, LOW)
+        scores_both((0, 0, LOW, 0, HALF), (1, 0, LOW, 0, HALF))
+        scores_both((0, 0, HIGH, 0, HALF), (3, 0, LOW, 0, HALF))
         scores(2, 0, LOW)
-        scores(0, 0, HIGH)
         affine(0)
-        scores(2, 0, HIGH)
-        scores(1, 0, LOW)
-        scores(1, 0, HIGH)
-        scores(3, 0, LOW)
         for r in LOW:
             scale_mask("vector", 0, r)
-        weigh_bank(0)
+        weigh_bank(1)
         affine(0)
+        scores_both((2, 0, HIGH, 0, HALF), (1, 0, HIGH, 0, HALF))
         for r in HIGH:
             scale_mask("vector", 0, r)
         weigh(0, 0, 0, HALF, nc.gpsimd)
+        weigh_bank(1)
+        scores(3, 0, HIGH)
         weigh_bank(0)
-        round_rows("scalar", v_mx, v_raw, 0, E)
+        weigh_bank(0)
         round_queries("scalar", 0, 1, 0, HALF)
         pack("scalar", 2, 0, 0, HALF)
         weigh_bank(1)
-        scores(3, 0, HIGH)
-        weigh_bank(1)
         pack("scalar", 1, 0, 0, HALF)
         weigh_bank(1)
-        weigh_bank(1)
         quantize(q_mx[0][1])
+        round_rows("vector", v_mx, v_raw, 0, E)
         round_queries("vector", 1, 1, 0, HALF)
         for places in (LOW, HIGH):
             scores_both((0, 1, places, 0, HALF), (1, 1, places, 0, HALF))

@@ -20,18 +20,20 @@ PACK = 4
 ROWS = D // PACK
 BANK = 512
 HALF = NQ // 2
+BLOCKS = HALF // P
 RUN = 4
 SCORE_BANKS = 3
 Y_BANKS = 2
+K_START, K_END = 32, 96
+PLACE_WORDS = P + P // PACK
+LOWER, UPPER = 0, 1
+LOW, HIGH = (0, 1), (2, 3)
 K_VECTOR = 84
 K_FILL = 64
 Q_VECTOR = 128
 Q_SECOND = 176
-K_START, K_END = 32, 96
-PLACE_WORDS = P + P // PACK
 G_PACK = 96
-V_LAST = 160
-LOW, HIGH = (0, 1), (2, 3)
+V_LAST = 144
 
 
 def tile_rows_a_lin_kb_mask_kernel(tc, qT, kT, t, v, kb, mask, out):
@@ -51,23 +53,27 @@ def tile_rows_a_lin_kb_mask_kernel(tc, qT, kT, t, v, kb, mask, out):
                 tile(name + "_scales", [P, columns], U8),
             )
 
+        def window(mx, c0, columns):
+            return tuple(part[:, c0 : c0 + columns] for part in mx)
+
         score_banks = [
-            [ps.tile([P, BANK], F32, name="score%d_%d" % (g, i)) for i in range(SCORE_BANKS)] for g in range(2)
+            [ps.tile([P, BANK], F32, name="score%d_%d" % (g, i)) for i in range(SCORE_BANKS)] for g in (LOWER, UPPER)
         ]
         y_banks = [ps.tile([P, BANK], F32, name="y%d" % i) for i in range(Y_BANKS)]
 
         k_rows = kT[0].rearrange("(p j) n -> p j n", j=PACK)
         q_rows = qT.rearrange("(a g) (p j) n -> a (g p) j n", g=2, j=PACK)
         mask_rows = mask.rearrange("(p r) n -> p r n", r=PACK)
-        row_tiles = [slice(g * ROWS, (g + 1) * ROWS) for g in range(2)]
+        row_tiles = [slice(g * ROWS, (g + 1) * ROWS) for g in (LOWER, UPPER)]
 
         k_raw = tile("k_raw", [K_END, PACK, N], F32)
         q_raw = [[tile("q_raw%d_%d" % (pair, half), [P, PACK, HALF], F32) for half in range(2)] for pair in range(2)]
         mask_last = tile("mask1", [P, PACK, HALF], F32)
-        mask_half = [tile("mask0", [P, PACK, HALF], F32), mask_last]
-        mask_sb = [[mask_half[half][:, 2 * a : 2 * a + 2] for a in range(2)] for half in range(2)]
-        mask_t_half = [tile("mask_t%d" % half, [P, PACK, HALF], F32) for half in range(2)]
-        mask_t = [[mask_t_half[half][:, r] for r in range(PACK)] for half in range(2)]
+        mask_t_last = tile("mask_t1", [P, PACK, HALF], F32)
+        head0_factor = tile("head0_factor", [P, PACK, HALF], F32)
+        other_rows = tile("other_rows", [P, PACK, HALF], F32)
+        raw_mask = [[other_rows, other_rows, head0_factor, head0_factor], [mask_last] * PACK]
+        mask_t = [[head0_factor, head0_factor, other_rows, other_rows], [mask_t_last] * PACK]
         v_raw = tile("v_raw", [P, PACK, E], F32)
         t_sb = tile("t_sb", [P, PACK], F32)
         kb_sb = tile("kb_sb", [P, PACK], F32)
@@ -76,6 +82,16 @@ def tile_rows_a_lin_kb_mask_kernel(tc, qT, kT, t, v, kb, mask, out):
         k_made = tile("k_made", [K_END, PACK * PLACE_WORDS], I32)
         k_words = tile("k_words", [P, PACK * PLACE_WORDS], I32)
         k_bf16 = tile("k_bf16", [K_END, N, PACK], BF16)
+
+        w_lower = mx_tiles("lower", NQ)
+        q_mx = [[mx_tiles("q%d_%d" % (pair, half), HALF) for half in range(2)] for pair in range(2)]
+        v_mx = mx_tiles("v", E)
+        scaled = [tile("scaled%d" % half, [P, PACK, HALF], F32) for half in range(2)]
+        w_rows = {(h, half): tile("rows%d_%d" % (h, half), [P, PACK, HALF], F32) for h in (1, 2, 3) for half in range(2)}
+        w_mx = {(0, 0): window(w_lower, 0, HALF), (2, 0): window(w_lower, HALF, HALF), (1, 0): mx_tiles("w1_0", HALF)}
+        w_mx[0, 1] = (w_mx[1, 0][0], tile("codes0_1", [P, HALF], U32), tile("scales0_1", [P, HALF], U8))
+        for unit in ((1, 1), (2, 1), (3, 0), (3, 1)):
+            w_mx[unit] = mx_tiles("w%d_%d" % unit, HALF)
 
         def place_codes(words, r):
             return words[:, r * PLACE_WORDS : r * PLACE_WORDS + P].bitcast(FP8X4)
@@ -94,25 +110,12 @@ def tile_rows_a_lin_kb_mask_kernel(tc, qT, kT, t, v, kb, mask, out):
                 in_=k_bf16[:, r * P : (r + 1) * P, :].rearrange("p c j -> p (c j)"),
             )
 
-        def window(mx, c0, columns):
-            return tuple(part[:, c0 : c0 + columns] for part in mx)
+        def load_queries(pair, half):
+            nc.sync.dma_start(out=q_raw[pair][half][:], in_=q_rows[pair][:, :, half * HALF : (half + 1) * HALF])
 
-        lower = mx_tiles("lower", NQ)
-        q_mx = [[mx_tiles("q%d_%d" % (pair, half), HALF) for half in range(2)] for pair in range(2)]
-        v_mx = mx_tiles("v", E)
-        scaled = [tile("scaled%d" % half, [P, PACK, HALF], F32) for half in range(2)]
-        w_rows = [[tile("rows%d_%d" % (h, half), [P, PACK, HALF], F32) if h else None for half in range(2)] for h in range(H)]
-        w1 = mx_tiles("w1_0", HALF)
-        reused = (w1[0], tile("codes0_1", [P, HALF], U32), tile("scales0_1", [P, HALF], U8))
-        w_mx = [
-            [window(lower, 0, HALF), reused],
-            [w1, mx_tiles("w1_1", HALF)],
-            [window(lower, HALF, HALF), mx_tiles("w2_1", HALF)],
-            [mx_tiles("w3_0", HALF), mx_tiles("w3_1", HALF)],
-        ]
-
-        def load_half(dst, rows, half):
-            nc.sync.dma_start(out=dst[:], in_=rows[:, :, half * HALF : (half + 1) * HALF])
+        def load_mask(half, places):
+            run = slice(places[0], places[-1] + 1)
+            nc.sync.dma_start(out=raw_mask[half][places[0]][:, run], in_=mask_rows[:, run, half * HALF : (half + 1) * HALF])
 
         def round_copy(engine, dst, src):
             if engine == "vector":
@@ -130,31 +133,28 @@ def tile_rows_a_lin_kb_mask_kernel(tc, qT, kT, t, v, kb, mask, out):
             src = raw[:, :, c0:c1].rearrange("p j (c i) -> p c j i", i=RUN)
             round_copy(engine, dst, src)
 
-        def round_queries(engine, pair, half, c0, c1):
+        def round_queries(engine, pair, half, c0=0, c1=HALF):
             round_rows(engine, q_mx[pair][half], q_raw[pair][half], c0, c1)
 
-        def quantize(mx, c0=0, c1=HALF):
+        def quantize(mx):
             nc.vector.quantize_mx(
-                out=mx[1][:, c0:c1].bitcast(FP8X4),
-                scales=mx[2][:, c0:c1],
-                in_=mx[0][:, c0:c1, :].rearrange("p c j -> p (c j)"),
+                out=mx[1][:].bitcast(FP8X4), scales=mx[2][:], in_=mx[0][:].rearrange("p c j -> p (c j)")
             )
 
         fills = [[], []]
         emptied = [0, 0]
 
-        def score_calls(h, half, places, c0, c1):
+        def fill_calls(h, half, places):
             pair, g = divmod(h, 2)
             bank = score_banks[g][len(fills[g]) % SCORE_BANKS]
-            fills[g].append((h, half, places, c0, c1))
+            fills[g].append((h, half, places))
             rows = row_tiles[g]
             calls = []
             for slot, r in enumerate(places):
-                for q0 in range(c0, c1, P):
-                    b0 = slot * (c1 - c0) + q0 - c0
+                for q0 in range(0, HALF, P):
                     calls.append(
                         dict(
-                            out=bank[:, b0 : b0 + P],
+                            out=bank[:, slot * HALF + q0 : slot * HALF + q0 + P],
                             lhsT=place_codes(k_words[rows], r),
                             lhsT_scale=place_scales(k_words[rows], r),
                             rhs=q_mx[pair][half][1][rows, q0 : q0 + P].bitcast(FP8X4),
@@ -165,99 +165,90 @@ def tile_rows_a_lin_kb_mask_kernel(tc, qT, kT, t, v, kb, mask, out):
                     )
             return calls
 
-        def scores(h, half, places, c0=0, c1=HALF):
-            for call in score_calls(h, half, places, c0, c1):
-                nc.tensor.matmul_mx(**call)
-
-        def scores_both(lower, upper):
-            first, second = score_calls(*lower), score_calls(*upper)
-            for n in range(max(len(first), len(second))):
-                for call in first[n : n + 1] + second[n : n + 1]:
+        def scores(*fill_by_tile):
+            for calls in zip(*[fill_calls(*fill) for fill in fill_by_tile]):
+                for call in calls:
                     nc.tensor.matmul_mx(**call)
 
-        def affine(g):
+        def oldest_fill(g):
             n = emptied[g]
             emptied[g] = n + 1
-            h, half, places, c0, c1 = fills[g][n]
+            return score_banks[g][n % SCORE_BANKS], fills[g][n]
+
+        def affine():
+            bank, (h, half, places) = oldest_fill(LOWER)
             for slot, r in enumerate(places):
-                dst = scaled[half][:, r, c0:c1]
-                src = score_banks[g][n % SCORE_BANKS][:, slot * (c1 - c0) : (slot + 1) * (c1 - c0)]
-                if half == 0:
+                dst, src = scaled[half][:, r, :], bank[:, slot * HALF : (slot + 1) * HALF]
+                if half == 0 and places == LOW:
                     nc.scalar.activation(out=dst, in_=src, func=IDENT, bias=kb_sb[:, r : r + 1])
                 else:
                     nc.scalar.activation(out=dst, in_=src, func=IDENT, scale=t_sb[:, r : r + 1], bias=kbt[:, r : r + 1])
 
-        def weigh(h, half, c0, c1, engine):
-            engine.tensor_tensor(
-                out=w_mx[h][half][0][:, c0:c1].rearrange("p (c i) r -> p c r i", i=RUN),
-                in0=scaled[half][:, :, c0:c1].rearrange("p r (c i) -> p c r i", i=RUN),
-                in1=(mask_t_half[0], mask_last)[half][:, :, c0:c1].rearrange("p r (c i) -> p c r i", i=RUN),
+        def weigh_head0(half):
+            nc.gpsimd.tensor_tensor(
+                out=w_mx[0, half][0][:].rearrange("p (c i) r -> p c r i", i=RUN),
+                in0=scaled[half][:].rearrange("p r (c i) -> p c r i", i=RUN),
+                in1=(head0_factor, mask_last)[half][:].rearrange("p r (c i) -> p c r i", i=RUN),
                 op=MULT,
             )
 
-        def weigh_bank(g):
-            n = emptied[g]
-            emptied[g] = n + 1
-            h, half, places, c0, c1 = fills[g][n]
+        def weigh_places(g):
+            bank, (h, half, places) = oldest_fill(g)
             for slot, r in enumerate(places):
                 nc.vector.scalar_tensor_tensor(
-                    out=w_rows[h][half][:, r, :].rearrange("p (b m) -> p m b", b=2),
-                    in0=score_banks[g][n % SCORE_BANKS][:, slot * HALF : (slot + 1) * HALF].rearrange(
-                        "p (m b) -> p m b", b=2
-                    ),
+                    out=w_rows[h, half][:, r, :].rearrange("p (b m) -> p m b", b=BLOCKS),
+                    in0=bank[:, slot * HALF : (slot + 1) * HALF].rearrange("p (m b) -> p m b", b=BLOCKS),
                     scalar=kb_sb[:, r : r + 1],
-                    in1=mask_t[half][r][:].rearrange("p (m b) -> p m b", b=2),
+                    in1=mask_t[half][r][:, r, :].rearrange("p (m b) -> p m b", b=BLOCKS),
                     op0=ADD,
                     op1=MULT,
                 )
 
-        def scale_mask(engine, half, r):
-            src = mask_sb[half][r // 2][:, r % 2, :]
-            if engine == "vector":
-                nc.vector.tensor_scalar(
-                    out=mask_t[half][r][:], in0=src, scalar1=t_sb[:, r : r + 1], scalar2=None, op0=MULT
-                )
-            else:
-                nc.scalar.activation(out=mask_t[half][r][:], in_=src, func=IDENT, scale=t_sb[:, r : r + 1])
+        def scale_mask(engine, half, places):
+            for r in places:
+                dst, src, factor = mask_t[half][r][:, r, :], raw_mask[half][r][:, r, :], t_sb[:, r : r + 1]
+                if engine == "vector":
+                    nc.vector.tensor_scalar(out=dst, in0=src, scalar1=factor, scalar2=None, op0=MULT)
+                else:
+                    nc.scalar.activation(out=dst, in_=src, func=IDENT, scale=factor)
 
-        def pack(engine, h, half, c0, c1):
+        def pack(engine, unit, c0=0, c1=HALF):
             if engine == "gpsimd":
                 nc.gpsimd.tensor_scalar(
-                    out=w_mx[h][half][0][:, c0:c1, :],
-                    in0=w_rows[h][half][:, :, c0:c1].rearrange("p r c -> p c r"),
+                    out=w_mx[unit][0][:, c0:c1, :],
+                    in0=w_rows[unit][:, :, c0:c1].rearrange("p r c -> p c r"),
                     scalar1=1.0,
                     scalar2=0.0,
                     op0=MULT,
                     op1=ADD,
                 )
             else:
-                round_rows(engine, w_mx[h][half], w_rows[h][half], c0, c1)
+                round_rows(engine, w_mx[unit], w_rows[unit], c0, c1)
 
-        def values(bank, b0, h, half, c0=0, c1=HALF):
-            for q0 in range(c0, c1, P):
+        def values(bank, slot, unit):
+            for q0 in range(0, HALF, P):
                 nc.tensor.matmul_mx(
-                    out=y_banks[bank][:, b0 + q0 - c0 : b0 + q0 - c0 + P],
-                    lhsT=w_mx[h][half][1][:, q0 : q0 + P].bitcast(FP8X4),
-                    lhsT_scale=w_mx[h][half][2][:, q0 : q0 + P],
+                    out=y_banks[bank][:, slot * HALF + q0 : slot * HALF + q0 + P],
+                    lhsT=w_mx[unit][1][:, q0 : q0 + P].bitcast(FP8X4),
+                    lhsT_scale=w_mx[unit][2][:, q0 : q0 + P],
                     rhs=v_mx[1][:].bitcast(FP8X4),
                     rhs_scale=v_mx[2][:],
                     start=True,
                     stop=True,
                 )
 
-        def finish(bank, b0, units, engine="scalar", c0=0, c1=HALF):
-            blocks = (c1 - c0) // P
-            y_sb = tile("y_sb%d_%d_%d" % (units[0] + (c0,)), [P, len(units) * blocks, E], F32)
-            dst, src = y_sb[:].rearrange("p b e -> p (b e)"), y_banks[bank][:, b0 : b0 + len(units) * blocks * E]
+        def finish(engine, bank, units):
+            y_sb = tile("y_sb%d_%d_0" % units[0], [P, len(units) * BLOCKS, E], F32)
+            dst, src = y_sb[:].rearrange("p b e -> p (b e)"), y_banks[bank][:, 0 : len(units) * BLOCKS * E]
             if engine == "vector":
                 nc.vector.tensor_scalar(out=dst, in0=src, scalar1=1.0 / 16.0, scalar2=None, op0=MULT)
             else:
                 nc.scalar.activation(out=dst, in_=src, func=IDENT, scale=1.0 / 16.0)
             for n, (h, half) in enumerate(units):
-                q0 = half * HALF + c0
+                order = "(m b) e -> m b e" if h else "(b m) e -> m b e"
                 nc.sync.dma_start(
-                    out=out[h, q0 : q0 + c1 - c0, :].rearrange("(m b) e -> m b e" if h else "(b m) e -> m b e", m=P),
-                    in_=y_sb[:, n * blocks : (n + 1) * blocks],
+                    out=out[h, half * HALF : (half + 1) * HALF, :].rearrange(order, m=P),
+                    in_=y_sb[:, n * BLOCKS : (n + 1) * BLOCKS],
                 )
 
         nc.vector.memset(warm[:, 0:1], 0.0)
@@ -267,8 +258,8 @@ def tile_rows_a_lin_kb_mask_kernel(tc, qT, kT, t, v, kb, mask, out):
         nc.scalar.dma_start(out=kb_sb[:], in_=kb.rearrange("(p r) o -> p (r o)", r=PACK))
         nc.vector.memset(k_made[:].rearrange("p (r w) -> p r w", r=PACK)[:, :, P:], 0)
         nc.scalar.activation(out=warm[:, 1:2], in_=warm[:, 0:1], func=IDENT)
-        load_half(q_raw[0][0], q_rows[0], 0)
-        load_half(q_raw[1][0], q_rows[1], 0)
+        load_queries(0, 0)
+        load_queries(1, 0)
 
         round_keys("vector", 0, 0, K_VECTOR)
         round_keys("scalar", 0, K_VECTOR, P)
@@ -276,20 +267,20 @@ def tile_rows_a_lin_kb_mask_kernel(tc, qT, kT, t, v, kb, mask, out):
         round_keys("scalar", 1, K_FILL, P)
         for r in LOW:
             quantize_keys(r)
-            copy_keys(0, (r,))
-        copy_keys(1, LOW)
+            copy_keys(LOWER, (r,))
+        copy_keys(UPPER, LOW)
         nc.vector.tensor_tensor(out=kbt[:], in0=kb_sb[:], in1=t_sb[:], op=MULT)
         for r in HIGH:
             quantize_keys(r)
         round_queries("vector", 0, 0, 0, Q_VECTOR)
-        copy_keys(0, HIGH)
-        load_half(mask_sb[0][0], mask_rows[:, 0:2], 0)
-        load_half(mask_sb[0][1], mask_rows[:, 2:4], 0)
-        copy_keys(1, HIGH)
-        load_half(q_raw[0][1], q_rows[0], 1)
+        copy_keys(LOWER, HIGH)
+        load_mask(0, LOW)
+        load_mask(0, HIGH)
+        copy_keys(UPPER, HIGH)
+        load_queries(0, 1)
         nc.sync.dma_start(out=v_raw[:], in_=v[0].rearrange("(p r) e -> p r e", r=PACK))
-        load_half(q_raw[1][1], q_rows[1], 1)
-        load_half(mask_last, mask_rows, 1)
+        load_queries(1, 1)
+        load_mask(1, LOW + HIGH)
 
         round_queries("scalar", 0, 0, Q_VECTOR, HALF)
         quantize(q_mx[0][0])
@@ -297,73 +288,72 @@ def tile_rows_a_lin_kb_mask_kernel(tc, qT, kT, t, v, kb, mask, out):
         round_queries("scalar", 1, 0, Q_SECOND, HALF)
         quantize(q_mx[1][0])
 
-        scores_both((0, 0, LOW, 0, HALF), (1, 0, LOW, 0, HALF))
-        scores_both((0, 0, HIGH, 0, HALF), (3, 0, LOW, 0, HALF))
-        scores(2, 0, LOW)
-        affine(0)
-        for r in LOW:
-            scale_mask("vector", 0, r)
-        weigh_bank(1)
-        affine(0)
-        scores_both((2, 0, HIGH, 0, HALF), (1, 0, HIGH, 0, HALF))
-        for r in HIGH:
-            scale_mask("vector", 0, r)
-        weigh(0, 0, 0, HALF, nc.gpsimd)
-        weigh_bank(1)
-        scores(3, 0, HIGH)
-        weigh_bank(0)
-        weigh_bank(0)
-        round_queries("scalar", 0, 1, 0, HALF)
-        pack("scalar", 2, 0, 0, HALF)
-        weigh_bank(1)
-        pack("scalar", 1, 0, 0, HALF)
-        weigh_bank(1)
+        scores((0, 0, LOW), (1, 0, LOW))
+        scores((0, 0, HIGH), (3, 0, LOW))
+        scores((2, 0, LOW))
+        affine()
+        scale_mask("vector", 0, LOW)
+        weigh_places(UPPER)
+        affine()
+        scores((2, 0, HIGH), (1, 0, HIGH))
+        weigh_head0(0)
+        scale_mask("scalar", 0, HIGH)
+        weigh_places(UPPER)
+        scores((3, 0, HIGH))
+        weigh_places(LOWER)
+        weigh_places(LOWER)
+        round_queries("scalar", 0, 1)
+        pack("scalar", (2, 0))
+        weigh_places(UPPER)
+        pack("scalar", (1, 0))
+        weigh_places(UPPER)
+
         quantize(q_mx[0][1])
         round_rows("vector", v_mx, v_raw, 0, E)
-        round_queries("vector", 1, 1, 0, HALF)
+        round_queries("vector", 1, 1)
         for places in (LOW, HIGH):
-            scores_both((0, 1, places, 0, HALF), (1, 1, places, 0, HALF))
-        quantize(lower, 0, NQ)
+            scores((0, 1, places), (1, 1, places))
+        quantize(w_lower)
         quantize(q_mx[1][1])
-        quantize(v_mx, 0, E)
-        scores_both((2, 1, LOW, 0, HALF), (3, 1, LOW, 0, HALF))
-        values(0, 0, 0, 0)
-        values(0, HALF, 2, 0)
-        affine(0)
-        affine(0)
-        for r in LOW:
-            scale_mask("vector", 1, r)
-        quantize(w_mx[1][0])
-        weigh(0, 1, 0, HALF, nc.gpsimd)
-        for r in HIGH:
-            scale_mask("scalar", 1, r)
-        values(1, 0, 1, 0)
-        scores(2, 1, HIGH)
-        weigh_bank(1)
-        scores(3, 1, HIGH)
-        weigh_bank(1)
-        pack("scalar", 3, 0, 0, HALF)
-        finish(0, 0, [(0, 0), (2, 0)])
-        weigh_bank(0)
-        weigh_bank(0)
-        pack("scalar", 1, 1, 0, HALF)
-        finish(1, 0, [(1, 0)])
-        weigh_bank(1)
-        weigh_bank(1)
-        pack("gpsimd", 2, 1, 0, G_PACK)
-        pack("scalar", 2, 1, G_PACK, HALF)
-        quantize(w_mx[3][0])
-        quantize(w_mx[0][1])
-        values(0, 0, 3, 0)
-        values(0, HALF, 0, 1)
-        quantize(w_mx[1][1])
-        values(1, 0, 1, 1)
-        pack("vector", 3, 1, 0, V_LAST)
-        pack("scalar", 3, 1, V_LAST, HALF)
-        quantize(w_mx[2][1])
-        values(1, HALF, 2, 1)
-        finish(0, 0, [(3, 0), (0, 1)])
-        quantize(w_mx[3][1])
-        values(0, 0, 3, 1)
-        finish(1, 0, [(1, 1), (2, 1)], "vector")
-        finish(0, 0, [(3, 1)])
+        quantize(v_mx)
+        scores((2, 1, LOW), (3, 1, LOW))
+        values(0, 0, (0, 0))
+        values(0, 1, (2, 0))
+        affine()
+        affine()
+        scale_mask("vector", 1, LOW)
+        quantize(w_mx[1, 0])
+
+        weigh_head0(1)
+        scale_mask("scalar", 1, HIGH)
+        values(1, 0, (1, 0))
+        scores((2, 1, HIGH))
+        weigh_places(UPPER)
+        scores((3, 1, HIGH))
+        weigh_places(UPPER)
+        pack("scalar", (3, 0))
+        finish("scalar", 0, [(0, 0), (2, 0)])
+        weigh_places(LOWER)
+        weigh_places(LOWER)
+        pack("scalar", (1, 1))
+        finish("scalar", 1, [(1, 0)])
+        weigh_places(UPPER)
+        weigh_places(UPPER)
+        pack("gpsimd", (2, 1), 0, G_PACK)
+        pack("scalar", (2, 1), G_PACK, HALF)
+
+        quantize(w_mx[3, 0])
+        quantize(w_mx[0, 1])
+        values(0, 0, (3, 0))
+        values(0, 1, (0, 1))
+        quantize(w_mx[1, 1])
+        values(1, 0, (1, 1))
+        pack("vector", (3, 1), 0, V_LAST)
+        pack("scalar", (3, 1), V_LAST, HALF)
+        quantize(w_mx[2, 1])
+        values(1, 1, (2, 1))
+        finish("scalar", 0, [(3, 0), (0, 1)])
+        quantize(w_mx[3, 1])
+        values(0, 0, (3, 1))
+        finish("vector", 1, [(1, 1), (2, 1)])
+        finish("scalar", 0, [(3, 1)])

from contextlib import ExitStack

import concourse.mybir as mybir

H, D, NQ, N, E = 4, 256, 512, 512, 128
FLOPS = 2 * H * N * NQ * (D + E)

F32 = mybir.dt.float32
BF16 = mybir.dt.bfloat16
U32 = mybir.dt.uint32
U8 = mybir.dt.uint8
I32 = mybir.dt.int32
FP8X4 = mybir.dt.float8_e4m3fn_x4
IDENT = mybir.ActivationFunctionType.Identity
MULT = mybir.AluOpType.mult
ADD = mybir.AluOpType.add

P = 128
PACK = 4
ROWS = D // PACK
BANK = 512
HALF = NQ // 2
BLOCKS = HALF // P
RUN = 4
SCORE_BANKS = 3
Y_BANKS = 2
K_START, K_END = 32, 96
PLACE_WORDS = P + P // PACK
LOWER, UPPER = 0, 1
LOW, HIGH = (0, 1), (2, 3)
K_VECTOR = 84
K_FILL = 64
Q_VECTOR = 128
Q_SECOND = 176
G_PACK = 96
V_LAST = 144


def tile_rows_a_lin_kb_mask_kernel(tc, qT, kT, t, v, kb, mask, out):
    nc = tc.nc
    with ExitStack() as ctx:
        sb = ctx.enter_context(tc.tile_pool(name="sb", bufs=1))
        ps = ctx.enter_context(tc.psum_pool(name="ps", bufs=1))
        ctx.enter_context(tc.manual_schedule())

        def tile(name, shape, dtype):
            return sb.tile(shape, dtype, name=name, align_bytes=64)

        def mx_tiles(name, columns):
            return (
                tile(name + "_bf16", [P, columns, PACK], BF16),
                tile(name + "_codes", [P, columns], U32),
                tile(name + "_scales", [P, columns], U8),
            )

        def window(mx, c0, columns):
            return tuple(part[:, c0 : c0 + columns] for part in mx)

        score_banks = [
            [ps.tile([P, BANK], F32, name="score%d_%d" % (g, i)) for i in range(SCORE_BANKS)] for g in (LOWER, UPPER)
        ]
        y_banks = [ps.tile([P, BANK], F32, name="y%d" % i) for i in range(Y_BANKS)]

        k_rows = kT[0].rearrange("(p j) n -> p j n", j=PACK)
        q_rows = qT.rearrange("(a g) (p j) n -> a (g p) j n", g=2, j=PACK)
        mask_rows = mask.rearrange("(p r) n -> p r n", r=PACK)
        row_tiles = [slice(g * ROWS, (g + 1) * ROWS) for g in (LOWER, UPPER)]

        k_raw = tile("k_raw", [K_END, PACK, N], F32)
        q_raw = [[tile("q_raw%d_%d" % (pair, half), [P, PACK, HALF], F32) for half in range(2)] for pair in range(2)]
        mask_last = tile("mask1", [P, PACK, HALF], F32)
        mask_t_last = tile("mask_t1", [P, PACK, HALF], F32)
        head0_factor = tile("head0_factor", [P, PACK, HALF], F32)
        other_rows = tile("other_rows", [P, PACK, HALF], F32)
        raw_mask = [[other_rows, other_rows, head0_factor, head0_factor], [mask_last] * PACK]
        mask_t = [[head0_factor, head0_factor, other_rows, other_rows], [mask_t_last] * PACK]
        v_raw = tile("v_raw", [P, PACK, E], F32)
        t_sb = tile("t_sb", [P, PACK], F32)
        kb_sb = tile("kb_sb", [P, PACK], F32)
        kbt = tile("kbt", [P, PACK], F32)
        warm = tile("warm", [P, 2], F32)
        k_made = tile("k_made", [K_END, PACK * PLACE_WORDS], I32)
        k_words = tile("k_words", [P, PACK * PLACE_WORDS], I32)
        k_bf16 = tile("k_bf16", [K_END, N, PACK], BF16)

        w_lower = mx_tiles("lower", NQ)
        q_mx = [[mx_tiles("q%d_%d" % (pair, half), HALF) for half in range(2)] for pair in range(2)]
        v_mx = mx_tiles("v", E)
        scaled = [tile("scaled%d" % half, [P, PACK, HALF], F32) for half in range(2)]
        w_rows = {(h, half): tile("rows%d_%d" % (h, half), [P, PACK, HALF], F32) for h in (1, 2, 3) for half in range(2)}
        w_mx = {(0, 0): window(w_lower, 0, HALF), (2, 0): window(w_lower, HALF, HALF), (1, 0): mx_tiles("w1_0", HALF)}
        w_mx[0, 1] = (w_mx[1, 0][0], tile("codes0_1", [P, HALF], U32), tile("scales0_1", [P, HALF], U8))
        for unit in ((1, 1), (2, 1), (3, 0), (3, 1)):
            w_mx[unit] = mx_tiles("w%d_%d" % unit, HALF)

        def place_codes(words, r):
            return words[:, r * PLACE_WORDS : r * PLACE_WORDS + P].bitcast(FP8X4)

        def place_scales(words, r):
            return words[:, r * PLACE_WORDS + P : (r + 1) * PLACE_WORDS].bitcast(U8)

        def copy_keys(g, places):
            run = slice(places[0] * PLACE_WORDS, (places[-1] + 1) * PLACE_WORDS)
            nc.sync.dma_start(out=k_words[row_tiles[g], run], in_=k_made[K_START:K_END, run])

        def quantize_keys(r):
            nc.vector.quantize_mx(
                out=place_codes(k_made, r),
                scales=place_scales(k_made, r),
                in_=k_bf16[:, r * P : (r + 1) * P, :].rearrange("p c j -> p (c j)"),
            )

        def load_queries(pair, half):
            nc.sync.dma_start(out=q_raw[pair][half][:], in_=q_rows[pair][:, :, half * HALF : (half + 1) * HALF])

        def load_mask(half, places):
            run = slice(places[0], places[-1] + 1)
            nc.sync.dma_start(out=raw_mask[half][places[0]][:, run], in_=mask_rows[:, run, half * HALF : (half + 1) * HALF])

        def round_copy(engine, dst, src):
            if engine == "vector":
                nc.vector.tensor_copy(out=dst, in_=src)
            else:
                nc.scalar.copy(out=dst, in_=src)

        def round_keys(engine, a, s0, s1):
            dst = k_bf16[:].rearrange("p (a b s) j -> p a s j b", a=2, b=2)[:, a, s0:s1]
            src = k_raw[:].rearrange("p j (s a b) -> p a s j b", a=2, b=2)[:, a, s0:s1]
            round_copy(engine, dst, src)

        def round_rows(engine, mx, raw, c0, c1):
            dst = mx[0][:, c0:c1, :].rearrange("p (c i) j -> p c j i", i=RUN)
            src = raw[:, :, c0:c1].rearrange("p j (c i) -> p c j i", i=RUN)
            round_copy(engine, dst, src)

        def round_queries(engine, pair, half, c0=0, c1=HALF):
            round_rows(engine, q_mx[pair][half], q_raw[pair][half], c0, c1)

        def quantize(mx):
            nc.vector.quantize_mx(
                out=mx[1][:].bitcast(FP8X4), scales=mx[2][:], in_=mx[0][:].rearrange("p c j -> p (c j)")
            )

        fills = [[], []]
        emptied = [0, 0]

        def fill_calls(h, half, places):
            pair, g = divmod(h, 2)
            bank = score_banks[g][len(fills[g]) % SCORE_BANKS]
            fills[g].append((h, half, places))
            rows = row_tiles[g]
            calls = []
            for slot, r in enumerate(places):
                for q0 in range(0, HALF, P):
                    calls.append(
                        dict(
                            out=bank[:, slot * HALF + q0 : slot * HALF + q0 + P],
                            lhsT=place_codes(k_words[rows], r),
                            lhsT_scale=place_scales(k_words[rows], r),
                            rhs=q_mx[pair][half][1][rows, q0 : q0 + P].bitcast(FP8X4),
                            rhs_scale=q_mx[pair][half][2][rows, q0 : q0 + P],
                            start=True,
                            stop=True,
                        )
                    )
            return calls

        def scores(*fill_by_tile):
            for calls in zip(*[fill_calls(*fill) for fill in fill_by_tile]):
                for call in calls:
                    nc.tensor.matmul_mx(**call)

        def oldest_fill(g):
            n = emptied[g]
            emptied[g] = n + 1
            return score_banks[g][n % SCORE_BANKS], fills[g][n]

        def affine():
            bank, (h, half, places) = oldest_fill(LOWER)
            for slot, r in enumerate(places):
                dst, src = scaled[half][:, r, :], bank[:, slot * HALF : (slot + 1) * HALF]
                if half == 0 and places == LOW:
                    nc.scalar.activation(out=dst, in_=src, func=IDENT, bias=kb_sb[:, r : r + 1])
                else:
                    nc.scalar.activation(out=dst, in_=src, func=IDENT, scale=t_sb[:, r : r + 1], bias=kbt[:, r : r + 1])

        def weigh_head0(half):
            nc.gpsimd.tensor_tensor(
                out=w_mx[0, half][0][:].rearrange("p (c i) r -> p c r i", i=RUN),
                in0=scaled[half][:].rearrange("p r (c i) -> p c r i", i=RUN),
                in1=(head0_factor, mask_last)[half][:].rearrange("p r (c i) -> p c r i", i=RUN),
                op=MULT,
            )

        def weigh_places(g):
            bank, (h, half, places) = oldest_fill(g)
            for slot, r in enumerate(places):
                nc.vector.scalar_tensor_tensor(
                    out=w_rows[h, half][:, r, :].rearrange("p (b m) -> p m b", b=BLOCKS),
                    in0=bank[:, slot * HALF : (slot + 1) * HALF].rearrange("p (m b) -> p m b", b=BLOCKS),
                    scalar=kb_sb[:, r : r + 1],
                    in1=mask_t[half][r][:, r, :].rearrange("p (m b) -> p m b", b=BLOCKS),
                    op0=ADD,
                    op1=MULT,
                )

        def scale_mask(engine, half, places):
            for r in places:
                dst, src, factor = mask_t[half][r][:, r, :], raw_mask[half][r][:, r, :], t_sb[:, r : r + 1]
                if engine == "vector":
                    nc.vector.tensor_scalar(out=dst, in0=src, scalar1=factor, scalar2=None, op0=MULT)
                else:
                    nc.scalar.activation(out=dst, in_=src, func=IDENT, scale=factor)

        def pack(engine, unit, c0=0, c1=HALF):
            if engine == "gpsimd":
                nc.gpsimd.tensor_scalar(
                    out=w_mx[unit][0][:, c0:c1, :],
                    in0=w_rows[unit][:, :, c0:c1].rearrange("p r c -> p c r"),
                    scalar1=1.0,
                    scalar2=0.0,
                    op0=MULT,
                    op1=ADD,
                )
            else:
                round_rows(engine, w_mx[unit], w_rows[unit], c0, c1)

        def values(bank, slot, unit):
            for q0 in range(0, HALF, P):
                nc.tensor.matmul_mx(
                    out=y_banks[bank][:, slot * HALF + q0 : slot * HALF + q0 + P],
                    lhsT=w_mx[unit][1][:, q0 : q0 + P].bitcast(FP8X4),
                    lhsT_scale=w_mx[unit][2][:, q0 : q0 + P],
                    rhs=v_mx[1][:].bitcast(FP8X4),
                    rhs_scale=v_mx[2][:],
                    start=True,
                    stop=True,
                )

        def finish(engine, bank, units):
            y_sb = tile("y_sb%d_%d_0" % units[0], [P, len(units) * BLOCKS, E], F32)
            dst, src = y_sb[:].rearrange("p b e -> p (b e)"), y_banks[bank][:, 0 : len(units) * BLOCKS * E]
            if engine == "vector":
                nc.vector.tensor_scalar(out=dst, in0=src, scalar1=1.0 / 16.0, scalar2=None, op0=MULT)
            else:
                nc.scalar.activation(out=dst, in_=src, func=IDENT, scale=1.0 / 16.0)
            for n, (h, half) in enumerate(units):
                order = "(m b) e -> m b e" if h else "(b m) e -> m b e"
                nc.sync.dma_start(
                    out=out[h, half * HALF : (half + 1) * HALF, :].rearrange(order, m=P),
                    in_=y_sb[:, n * BLOCKS : (n + 1) * BLOCKS],
                )

        nc.vector.memset(warm[:, 0:1], 0.0)
        nc.vector.memset(k_raw[0:K_START].bitcast(U32), 0)
        nc.sync.dma_start(out=k_raw[K_START:K_END], in_=k_rows)
        nc.scalar.dma_start(out=t_sb[:], in_=t.rearrange("(p r) o -> p (r o)", r=PACK))
        nc.scalar.dma_start(out=kb_sb[:], in_=kb.rearrange("(p r) o -> p (r o)", r=PACK))
        nc.vector.memset(k_made[:].rearrange("p (r w) -> p r w", r=PACK)[:, :, P:], 0)
        nc.scalar.activation(out=warm[:, 1:2], in_=warm[:, 0:1], func=IDENT)
        load_queries(0, 0)
        load_queries(1, 0)

        round_keys("vector", 0, 0, K_VECTOR)
        round_keys("scalar", 0, K_VECTOR, P)
        round_keys("vector", 1, 0, K_FILL)
        round_keys("scalar", 1, K_FILL, P)
        for r in LOW:
            quantize_keys(r)
            copy_keys(LOWER, (r,))
        copy_keys(UPPER, LOW)
        nc.vector.tensor_tensor(out=kbt[:], in0=kb_sb[:], in1=t_sb[:], op=MULT)
        for r in HIGH:
            quantize_keys(r)
        round_queries("vector", 0, 0, 0, Q_VECTOR)
        copy_keys(LOWER, HIGH)
        load_mask(0, LOW)
        load_mask(0, HIGH)
        copy_keys(UPPER, HIGH)
        load_queries(0, 1)
        nc.sync.dma_start(out=v_raw[:], in_=v[0].rearrange("(p r) e -> p r e", r=PACK))
        load_queries(1, 1)
        load_mask(1, LOW + HIGH)

        round_queries("scalar", 0, 0, Q_VECTOR, HALF)
        quantize(q_mx[0][0])
        round_queries("vector", 1, 0, 0, Q_SECOND)
        round_queries("scalar", 1, 0, Q_SECOND, HALF)
        quantize(q_mx[1][0])

        scores((0, 0, LOW), (1, 0, LOW))
        scores((0, 0, HIGH), (3, 0, LOW))
        scores((2, 0, LOW))
        affine()
        scale_mask("vector", 0, LOW)
        weigh_places(UPPER)
        affine()
        scores((2, 0, HIGH), (1, 0, HIGH))
        weigh_head0(0)
        scale_mask("scalar", 0, HIGH)
        weigh_places(UPPER)
        scores((3, 0, HIGH))
        weigh_places(LOWER)
        weigh_places(LOWER)
        round_queries("scalar", 0, 1)
        pack("scalar", (2, 0))
        weigh_places(UPPER)
        pack("scalar", (1, 0))
        weigh_places(UPPER)

        quantize(q_mx[0][1])
        round_rows("vector", v_mx, v_raw, 0, E)
        round_queries("vector", 1, 1)
        for places in (LOW, HIGH):
            scores((0, 1, places), (1, 1, places))
        quantize(w_lower)
        quantize(q_mx[1][1])
        quantize(v_mx)
        scores((2, 1, LOW), (3, 1, LOW))
        values(0, 0, (0, 0))
        values(0, 1, (2, 0))
        affine()
        affine()
        scale_mask("vector", 1, LOW)
        quantize(w_mx[1, 0])

        weigh_head0(1)
        scale_mask("scalar", 1, HIGH)
        values(1, 0, (1, 0))
        scores((2, 1, HIGH))
        weigh_places(UPPER)
        scores((3, 1, HIGH))
        weigh_places(UPPER)
        pack("scalar", (3, 0))
        finish("scalar", 0, [(0, 0), (2, 0)])
        weigh_places(LOWER)
        weigh_places(LOWER)
        pack("scalar", (1, 1))
        finish("scalar", 1, [(1, 0)])
        weigh_places(UPPER)
        weigh_places(UPPER)
        pack("gpsimd", (2, 1), 0, G_PACK)
        pack("scalar", (2, 1), G_PACK, HALF)

        quantize(w_mx[3, 0])
        quantize(w_mx[0, 1])
        values(0, 0, (3, 0))
        values(0, 1, (0, 1))
        quantize(w_mx[1, 1])
        values(1, 0, (1, 1))
        pack("vector", (3, 1), 0, V_LAST)
        pack("scalar", (3, 1), V_LAST, HALF)
        quantize(w_mx[2, 1])
        values(1, 1, (2, 1))
        finish("scalar", 0, [(3, 0), (0, 1)])
        quantize(w_mx[3, 1])
        values(0, 0, (3, 1))
        finish("vector", 1, [(1, 1), (2, 1)])
        finish("scalar", 0, [(3, 1)])
